import numpy as np
import ml_dtypes


def mxq(x, axis, fmt="e4m3"):
    dtype, down = {"e4m3": (ml_dtypes.float8_e4m3fn, 7), "e5m2": (ml_dtypes.float8_e5m2, 14)}[fmt]
    v = np.moveaxis(np.asarray(x, np.float32).astype(ml_dtypes.bfloat16).astype(np.float64), axis, -1)
    blocks = v.reshape(v.shape[:-1] + (-1, 32))
    amax = np.abs(blocks).max(-1, keepdims=True)
    byte = np.maximum(np.where(amax > 0, np.frexp(amax)[1] - 1 + 127, 0) - down, 1)
    scale = np.exp2(byte - 127.0)
    codes = (blocks / scale).astype(np.float32).astype(dtype).astype(np.float64)
    return np.moveaxis((codes * scale).reshape(v.shape), -1, axis)


WIDE = False


def mx_kscale(k):
    if not WIDE:
        return np.ones(k)
    levels = np.array([10, -10, 5, -5, 0])
    if k % 512:
        return np.exp2(np.random.permutation(np.resize(levels, k // 32))).repeat(32)
    a = np.empty((k // 512, 16))
    for p in range(k // 512):
        a[p, :8] = np.random.permutation(np.resize(levels, 8))
        for g in range(8):
            far = levels[np.abs(levels - a[p, g]) >= 10]
            a[p, g + 8] = far[np.random.randint(len(far))]
    return np.exp2(a.ravel()).repeat(32)


def f64(x):
    return np.asarray(x).astype(np.float64)


def striped(idx):
    return np.tile(idx.reshape(-1, 16).T, (8, 1)).astype(np.uint16)


def unstriped(offs):
    return offs[:16].T.reshape(-1).astype(np.int64)


E2M1 = np.array([0.0, 0.5, 1.0, 1.5, 2.0, 3.0, 4.0, 6.0, -0.0, -0.5, -1.0, -1.5, -2.0, -3.0, -4.0, -6.0])


def pack_weight(w, fmt):
    k, n = w.shape
    w = f64(np.asarray(w, np.float32).astype(ml_dtypes.bfloat16)).reshape(k // 32, 32, n)
    amax = np.abs(w).max(1)
    if fmt == "e4m3":
        byte = np.frexp(amax)[1] - 1 + 127 - 7
    else:
        mant, ex = np.frexp(amax / 6.0)
        byte = np.where(mant > 0.5, ex, ex - 1) + 127
    byte = np.clip(np.where(amax > 0, byte, 1), 1, 254)
    scaled = (w * np.exp2(127.0 - byte)[:, None, :]).reshape(k, n).astype(np.float32)
    by_word = np.ascontiguousarray(scaled.reshape(k // 512, 128, 4, n).transpose(0, 1, 3, 2))
    if fmt == "e4m3":
        words = by_word.astype(ml_dtypes.float8_e4m3fn).view(np.uint8)
    else:
        c = by_word.astype(ml_dtypes.float4_e2m1fn).view(np.uint8) & 0xF
        words = (c[..., 0::2] | (c[..., 1::2] << 4)).reshape(k // 512, 128, 2 * n)
    return np.ascontiguousarray(words), np.ascontiguousarray(byte.astype(np.uint8).reshape(k // 512, 16, n))


def unpack_weight(words, scales, fmt):
    g, _, n = scales.shape
    words = np.ascontiguousarray(words).reshape(g, 128, n, -1)
    if fmt == "e4m3":
        vals = words.view(ml_dtypes.float8_e4m3fn).astype(np.float64)
    else:
        nib = np.empty((g, 128, n, 4), np.uint8)
        nib[..., 0::2] = words & 0xF
        nib[..., 1::2] = words >> 4
        vals = E2M1[nib]
    vals = vals * np.repeat(np.exp2(scales.astype(np.float64) - 127.0), 8, axis=1)[..., None]
    return vals.transpose(0, 1, 3, 2).reshape(g * 512, n)


def gelu(v):
    return 0.5 * v * (1.0 + np.tanh(np.sqrt(2.0 / np.pi) * (v + 0.044715 * v**3)))


K, T, E, C, H, N = 1024, 512, 8, 128, 512, 384


def by_expert(wq, xq):
    return np.concatenate([wq[e].T @ xq[:, e * C:(e + 1) * C] for e in range(E)], axis=1)


def setup_inputs():
    n = np.random.standard_normal
    s = mx_kscale(K)[:, None]
    u = mx_kscale(H)
    first = np.random.permutation(np.repeat(np.arange(E), T // E))
    second = (first + 1 + np.random.permutation(np.repeat(np.arange(E - 1), -(-T // (E - 1)))[:T])) % E
    while np.bincount(second, minlength=E).max() != T // E:
        load = np.bincount(second, minlength=E); hi, lo = int(load.argmax()), int(load.argmin())
        t = np.flatnonzero((second == hi) & (first != lo))[0]; second[t] = lo
    slot_token = np.empty(E * C, np.int64); pos = np.empty((2, T), np.int64); fill = np.zeros(E, np.int64)
    place = np.stack([np.random.permutation(C) for _ in range(E)])
    for r, deal in enumerate((first, second)):
        for t in np.random.permutation(T):
            e = deal[t]; j = e * C + place[e, fill[e]]; fill[e] += 1; slot_token[j] = t; pos[r, t] = j
    g = np.random.uniform(0.2, 0.8, T)
    w1 = [pack_weight(m, "e2m1") for m in n((E, K, H)) / np.sqrt(K) / s[None] * u[None, None, :]]
    w2 = [pack_weight(m, "e2m1") for m in n((E, H, N)) / np.sqrt(H) / u[None, :, None]]
    w_slot = np.empty(E * C); w_slot[pos[0]] = g; w_slot[pos[1]] = 1.0 - g
    return {
        "xT": (n((K, T)) * s).astype(np.float32),
        "w1_words": np.stack([m[0] for m in w1]),
        "w1_scales": np.stack([m[1] for m in w1]),
        "w2_words": np.stack([m[0] for m in w2]),
        "w2_scales": np.stack([m[1] for m in w2]),
        "gate": np.tile(w_slot, (K, 1)).astype(np.float32),
        "offs": striped(slot_token),
        "pos1": striped(pos[0]),
        "pos2": striped(pos[1]),
    }


def reference(xT, w1_words, w1_scales, w2_words, w2_scales, gate, offs, pos1, pos2):
    idx = unstriped(offs)
    w1 = np.stack([unpack_weight(w1_words[e], w1_scales[e], "e2m1") for e in range(E)])
    w2 = np.stack([unpack_weight(w2_words[e], w2_scales[e], "e2m1") for e in range(E)])
    xq = mxq(f64(gate) * f64(xT)[:, idx], 0, "e4m3")
    h = gelu(by_expert(w1, xq))
    y = by_expert(w2, mxq(h, 0, "e4m3"))
    return y[:, unstriped(pos1)] + y[:, unstriped(pos2)]

@@ -1,0 +1,240 @@
+from contextlib import ExitStack
+
+import concourse.mybir as mybir
+from concourse.masks import make_identity
+
+K, T, E, C, H, N = 1024, 512, 8, 128, 512, 384
+SLOTS = E * C
+FLOPS = 2 * SLOTS * (K * H + H * N)
+P = 128
+PACK = 4
+PASSES = K // (P * PACK)
+CHUNKS = N // P
+BYTES = 4 * K * T + E * (K * H + H * N) // 2 + E * (K * H + H * N) // 32 + 4 * P * SLOTS + 2 * P * (SLOTS + 2 * T) // 16 + 4 * N * T
+
+F32 = mybir.dt.float32
+BF16 = mybir.dt.bfloat16
+I32 = mybir.dt.int32
+U32 = mybir.dt.uint32
+U16 = mybir.dt.uint16
+U8 = mybir.dt.uint8
+FP8X4 = mybir.dt.float8_e4m3fn_x4
+FP4X4 = mybir.dt.float4_e2m1fn_x4
+MULT = mybir.AluOpType.mult
+ADD = mybir.AluOpType.add
+GELU = mybir.ActivationFunctionType.Gelu_apprx_tanh
+
+GROUPS = [(0, 2), (2, 4), (4, 6), (6, 7), (7, 8)]
+SECOND_BEFORE = {0: 7, 1: 7, 2: 9, 3: 9}
+REGION = 9216
+G_AT = 3072
+
+
+def tile_moe_pre_mlp_gelu_kernel(
+    tc, xT, w1_words, w1_scales, w2_words, w2_scales, gate, offs, pos1, pos2, out
+):
+    nc = tc.nc
+    with ExitStack() as ctx:
+        keep = ctx.enter_context(tc.tile_pool(name="keep", bufs=1))
+        ring = ctx.enter_context(tc.tile_pool(name="ring", bufs=3))
+        arena = ctx.enter_context(tc.tile_pool(name="arena", bufs=1))
+        psum = ctx.enter_context(tc.psum_pool(name="psum", bufs=1))
+
+        offs_sb = keep.tile([P, SLOTS // 16], U16, name="offs_sb")
+        pos_sb = [keep.tile([P, T // 16], U16, name="pos%d_sb" % r) for r in range(2)]
+        gate_sb = keep.tile([P, SLOTS], F32, name="gate_sb")
+        planes = [[keep.tile([P, T], F32, name="x_%d_%d" % (s, j)) for j in range(PACK)] for s in range(PASSES)]
+        w1c = keep.tile([P, E, PASSES, 2 * H], U8, name="w1c", align_bytes=64)
+        w1s = keep.tile([P, E, PASSES, H], U8, name="w1s", align_bytes=64)
+        w2c = keep.tile([P, E, 2 * N], U8, name="w2c", align_bytes=64)
+        w2s = keep.tile([P, E, N], U8, name="w2s", align_bytes=64)
+        xs = keep.tile([P, PASSES, SLOTS], U8, name="xs", align_bytes=64)
+        hs = keep.tile([P, SLOTS], U8, name="hs", align_bytes=64)
+        y = keep.tile([P, CHUNKS, SLOTS], F32, name="y")
+        ident = keep.tile([P, P], F32, name="ident")
+        warm = keep.tile([P, 8], F32, name="warm")
+
+        nc.vector.memset(w1s[:].rearrange("p e s i -> p (e s i)").bitcast(I32), 0)
+        nc.vector.memset(w2s[:].rearrange("p e n -> p (e n)").bitcast(I32), 0)
+        make_identity(nc, ident[:])
+        nc.scalar.activation(warm[:], ident[:, 0:8], GELU)
+
+        x_rows = xT.rearrange("(s p j) t -> s j p t", s=PASSES, j=PACK)
+        first = GROUPS[0][1] * C
+
+        def load_w1_scales(e0, e1):
+            rows = w1_scales[e0:e1].rearrange("e s q i -> q (e s) i")
+            for r in range(4):
+                nc.sync.dma_start(
+                    w1s[r:P:32, e0:e1].rearrange("p e s i -> p (e s) i").bitcast(I32), rows[r:16:4].bitcast(I32)
+                )
+
+        def load_w2_scales():
+            rows = w2_scales.rearrange("e s q n -> q (e s) n")
+            for r in range(4):
+                nc.sync.dma_start(w2s[r:P:32].bitcast(I32), rows[r:16:4].bitcast(I32))
+
+        def load_w1(e0, e1):
+            nc.sync.dma_start(
+                w1c[:, e0:e1].rearrange("p e s b -> p (e s) b").bitcast(I32),
+                w1_words[e0:e1].rearrange("e s p b -> p (e s) b").bitcast(I32),
+            )
+
+        def load_w2(e0, e1):
+            nc.sync.dma_start(
+                w2c[:, e0:e1].bitcast(I32), w2_words[e0:e1].rearrange("e s p b -> p (e s) b").bitcast(I32)
+            )
+
+        nc.sync.dma_start(offs_sb[:], offs)
+        nc.sync.dma_start(gate_sb[:, 0:first], gate[0:P, 0:first])
+        for s in range(PASSES):
+            for j in range(PACK):
+                nc.sync.dma_start(planes[s][j][:], x_rows[s, j])
+        nc.sync.dma_start(gate_sb[:, first:SLOTS], gate[0:P, first:SLOTS])
+        load_w1_scales(0, 4)
+        load_w1(0, 2)
+        load_w1(2, 4)
+        load_w2_scales()
+        load_w2(0, 4)
+        load_w1_scales(4, 8)
+        load_w1(4, 6)
+        load_w1(6, 8)
+        load_w2(4, 8)
+        nc.sync.dma_start(pos_sb[0][:], pos1)
+        nc.sync.dma_start(pos_sb[1][:], pos2)
+
+        gathered = {}
+        rounded = {}
+        h_in = {}
+        x_codes = {}
+
+        units = [(grp, s) for grp in GROUPS for s in range(PASSES)]
+
+        def rounded_at(u):
+            (e0, e1), s = units[u]
+            return (u + 2) * REGION + G_AT + 64 - 2 * PACK * C * (e1 - e0)
+
+        def codes_at(u):
+            (e0, e1), s = units[u]
+            later = u + 4 - 2 * s
+            if later < len(units) - 1:
+                return rounded_at(later) + 64 - 4 * C * (e1 - e0)
+            return u * REGION + G_AT + 4096
+
+        def gather(unit):
+            (e0, e1), s = unit
+            lo, hi = e0 * C, e1 * C
+            u = units.index(unit)
+            g = arena.tile([P, PACK, hi - lo], F32, name="g%d" % u, offset=u * REGION + G_AT, align_bytes=64)
+            for j in range(PACK):
+                nc.vector.tensor_tensor(
+                    g[:, j, :], planes[s][j][:].indirect(offs_sb[:, lo // 16 : hi // 16]), gate_sb[:, lo:hi], MULT
+                )
+            gathered[unit] = g
+
+        def interleave(unit, copy):
+            g = gathered[unit]
+            u = units.index(unit)
+            at = rounded_at(u)
+            xb = arena.tile([P, g.shape[2], PACK], BF16, name="xb%d" % u, offset=at, align_bytes=64)
+            copy(
+                xb[:].rearrange("p (c i) t -> p c t i", i=4),
+                g[:].rearrange("p t (c i) -> p c t i", i=4),
+            )
+            rounded[unit] = xb
+
+        def quantise_x(unit):
+            (e0, e1), s = unit
+            lo, hi = e0 * C, e1 * C
+            u = units.index(unit)
+            at = codes_at(u)
+            xc = arena.tile([P, hi - lo], U32, name="xc%d" % u, offset=at, align_bytes=64)
+            for e in range(e0, e1):
+                x_codes[e, s] = xc[:, (e - e0) * C : (e - e0 + 1) * C]
+            nc.vector.quantize_mx(
+                out=xc[:].bitcast(FP8X4),
+                scales=xs[:, s, lo:hi],
+                in_=rounded[unit][:].rearrange("p c t -> p (c t)"),
+            )
+
+        def first_layer(e, copy):
+            cols = slice(e * C, (e + 1) * C)
+            a = psum.tile([P, H], F32, name="a", tag="a", bufs=3)
+            for s in range(PASSES):
+                nc.tensor.matmul_mx(
+                    out=a[:],
+                    lhsT=x_codes[e, s].bitcast(FP8X4),
+                    lhsT_scale=xs[:, s, cols],
+                    rhs=w1c[:, e, s, :].bitcast(FP4X4),
+                    rhs_scale=w1s[:, e, s, :],
+                    start=(s == 0),
+                    stop=(s == PASSES - 1),
+                )
+            hb = ring.tile([P, 2, P, 2], BF16, name="hb", tag="hb")
+            nc.scalar.activation(hb[:], a[:].rearrange("c (p u d) -> c u p d", u=2, d=2), GELU)
+            words = hb[:].rearrange("c u p d -> c (u p d)").bitcast(F32)
+            turned = psum.tile([P, 2, C], F32, name="turned", tag="turned", bufs=2)
+            for u in range(2):
+                nc.tensor.transpose(turned[:, u, :], words[:, u * P : (u + 1) * P], ident[:])
+            if e in SECOND_BEFORE:
+                at = SECOND_BEFORE[e] * REGION + G_AT + 128 + (e % 2) * 1024
+            else:
+                at = 12 * REGION + (e - 4) * 1024
+            hq = arena.tile([P, C * PACK], BF16, name="hq%d" % e, offset=at, align_bytes=64)
+            copy(hq[:].bitcast(F32).rearrange("p (c u) -> p c u", u=2), turned[:].rearrange("p u c -> p c u"))
+            h_in[e] = hq
+
+        def second_layer(e, copies):
+            cols = slice(e * C, (e + 1) * C)
+            at = codes_at(e + 3) if e in (4, 5) else 13 * REGION + e * 512
+            hc = arena.tile([P, C], U32, name="hc%d" % e, offset=at, align_bytes=64)
+            nc.vector.quantize_mx(out=hc[:].bitcast(FP8X4), scales=hs[:, cols], in_=h_in[e][:])
+            acc = psum.tile([P, CHUNKS, C], F32, name="acc", tag="acc", bufs=3)
+            for c in range(CHUNKS):
+                nc.tensor.matmul_mx(
+                    out=acc[:, c, :],
+                    lhsT=w2c[:, e, 2 * P * c : 2 * P * (c + 1)].bitcast(FP4X4),
+                    lhsT_scale=w2s[:, e, P * c : P * (c + 1)],
+                    rhs=hc[:].bitcast(FP8X4),
+                    rhs_scale=hs[:, cols],
+                    start=True,
+                    stop=True,
+                )
+            for copy, c0, c1 in copies:
+                copy(y[:, c0:c1, cols], acc[:, c0:c1, :])
+
+        for u, unit in enumerate(units):
+            last = u == len(units) - 1
+            for e in SECOND_BEFORE:
+                if SECOND_BEFORE[e] == u:
+                    second_layer(e, [(nc.scalar.copy, 0, CHUNKS)])
+            gather(unit)
+            if not last:
+                interleave(unit, nc.scalar.copy)
+            if u > 0:
+                quantise_x(units[u - 1])
+                (e0, e1), s = units[u - 1]
+                if s == PASSES - 1:
+                    for e in range(e0, e1):
+                        first_layer(e, nc.scalar.copy)
+        interleave(units[-1], nc.vector.tensor_copy)
+        quantise_x(units[-1])
+        first_layer(E - 1, nc.vector.tensor_copy)
+        second_layer(4, [(nc.scalar.copy, 0, CHUNKS)])
+        second_layer(5, [(nc.scalar.copy, 0, CHUNKS)])
+        second_layer(6, [(nc.vector.tensor_copy, 0, CHUNKS)])
+        second_layer(E - 1, [(nc.vector.tensor_copy, 0, 1), (nc.scalar.copy, 1, CHUNKS)])
+
+        picked = [[keep.tile([P, T], F32, name="pick_%d_%d" % (c, r)) for r in range(2)] for c in range(CHUNKS)]
+        summed = [keep.tile([P, T], F32, name="sum_%d" % c) for c in range(CHUNKS)]
+
+        def combine(c):
+            nc.vector.tensor_tensor(summed[c][:], picked[c][0][:], picked[c][1][:], ADD)
+            nc.sync.dma_start(out[c * P : (c + 1) * P, :], summed[c][:])
+
+        for c in range(CHUNKS):
+            nc.vector.tensor_copy(picked[c][0][:], y[:, c, :].indirect(pos_sb[0][:]))
+            if c > 0:
+                combine(c - 1)
+            nc.vector.tensor_copy(picked[c][1][:], y[:, c, :].indirect(pos_sb[1][:]))
+        combine(CHUNKS - 1)

@@ -24,10 +24,20 @@ MULT = mybir.AluOpType.mult
 ADD = mybir.AluOpType.add
 GELU = mybir.ActivationFunctionType.Gelu_apprx_tanh
 
-GROUPS = [(0, 2), (2, 4), (4, 6), (6, 7), (7, 8)]
-SECOND_BEFORE = {0: 7, 1: 7, 2: 9, 3: 9}
-REGION = 9216
-G_AT = 3072
+GROUPS = [(0, 3), (3, 5), (5, 7), (7, 8)]
+REGION = 6144
+CHAINS = [
+    ["xb0", "g2"],
+    ["xb1", "g3"],
+    ["xb2", "g4"],
+    ["xc1", "xb3", "g5"],
+    ["hb2", "xb4"],
+    ["xc3", "xb5", "g7"],
+    ["hk2", "xb6"],
+    ["hk1", "xc5", "hk3"],
+    ["xc7", "hk4"],
+]
+BESIDE = {"g6": ("xb4", 1984), "hq2": ("xb4", 2112)}
 
 
 def tile_moe_pre_mlp_gelu_kernel(
@@ -36,7 +46,6 @@ def tile_moe_pre_mlp_gelu_kernel(
     nc = tc.nc
     with ExitStack() as ctx:
         keep = ctx.enter_context(tc.tile_pool(name="keep", bufs=1))
-        ring = ctx.enter_context(tc.tile_pool(name="ring", bufs=3))
         arena = ctx.enter_context(tc.tile_pool(name="arena", bufs=1))
         psum = ctx.enter_context(tc.psum_pool(name="psum", bufs=1))
 
@@ -91,73 +100,68 @@ def tile_moe_pre_mlp_gelu_kernel(
             for j in range(PACK):
                 nc.sync.dma_start(planes[s][j][:], x_rows[s, j])
         nc.sync.dma_start(gate_sb[:, first:SLOTS], gate[0:P, first:SLOTS])
-        load_w1_scales(0, 4)
-        load_w1(0, 2)
-        load_w1(2, 4)
+        load_w1_scales(0, 8)
+        load_w1(0, 1)
+        load_w1(1, 3)
+        load_w1(3, 5)
         load_w2_scales()
         load_w2(0, 4)
-        load_w1_scales(4, 8)
-        load_w1(4, 6)
-        load_w1(6, 8)
+        load_w1(5, 7)
+        load_w1(7, 8)
         load_w2(4, 8)
         nc.sync.dma_start(pos_sb[0][:], pos1)
         nc.sync.dma_start(pos_sb[1][:], pos2)
 
+        places = {name: r * REGION for r, chain in enumerate(CHAINS) for name in chain}
+        for name in BESIDE:
+            places[name] = places[BESIDE[name][0]] + BESIDE[name][1]
+
+        def staged(name, shape, dtype):
+            if name in places:
+                return arena.tile(shape, dtype, name=name, offset=places[name], align_bytes=64)
+            return keep.tile(shape, dtype, name=name, align_bytes=64)
+
+        units = [(e0, e1, s) for e0, e1 in GROUPS for s in range(PASSES)]
         gathered = {}
         rounded = {}
-        h_in = {}
         x_codes = {}
+        h_rows = {}
+        h_in = {}
+        sums = {}
 
-        units = [(grp, s) for grp in GROUPS for s in range(PASSES)]
-
-        def rounded_at(u):
-            (e0, e1), s = units[u]
-            return (u + 2) * REGION + G_AT + 64 - 2 * PACK * C * (e1 - e0)
-
-        def codes_at(u):
-            (e0, e1), s = units[u]
-            later = u + 4 - 2 * s
-            if later < len(units) - 1:
-                return rounded_at(later) + 64 - 4 * C * (e1 - e0)
-            return u * REGION + G_AT + 4096
-
-        def gather(unit):
-            (e0, e1), s = unit
+        def gather(u):
+            e0, e1, s = units[u]
             lo, hi = e0 * C, e1 * C
-            u = units.index(unit)
-            g = arena.tile([P, PACK, hi - lo], F32, name="g%d" % u, offset=u * REGION + G_AT, align_bytes=64)
+            g = staged("g%d" % u, [P, PACK, hi - lo], F32)
             for j in range(PACK):
                 nc.vector.tensor_tensor(
                     g[:, j, :], planes[s][j][:].indirect(offs_sb[:, lo // 16 : hi // 16]), gate_sb[:, lo:hi], MULT
                 )
-            gathered[unit] = g
+            gathered[u] = g
 
-        def interleave(unit, copy):
-            g = gathered[unit]
-            u = units.index(unit)
-            at = rounded_at(u)
-            xb = arena.tile([P, g.shape[2], PACK], BF16, name="xb%d" % u, offset=at, align_bytes=64)
+        def interleave(u, copy):
+            g = gathered[u]
+            xb = staged("xb%d" % u, [P, g.shape[2], PACK], BF16)
             copy(
                 xb[:].rearrange("p (c i) t -> p c t i", i=4),
                 g[:].rearrange("p t (c i) -> p c t i", i=4),
             )
-            rounded[unit] = xb
+            rounded[u] = xb
 
-        def quantise_x(unit):
-            (e0, e1), s = unit
-            lo, hi = e0 * C, e1 * C
-            u = units.index(unit)
-            at = codes_at(u)
-            xc = arena.tile([P, hi - lo], U32, name="xc%d" % u, offset=at, align_bytes=64)
+        def quantise_x(u):
+            e0, e1, s = units[u]
+            xc = staged("xc%d" % u, [P, (e1 - e0) * C], U32)
             for e in range(e0, e1):
                 x_codes[e, s] = xc[:, (e - e0) * C : (e - e0 + 1) * C]
-            nc.vector.quantize_mx(
-                out=xc[:].bitcast(FP8X4),
-                scales=xs[:, s, lo:hi],
-                in_=rounded[unit][:].rearrange("p c t -> p (c t)"),
-            )
+            for b0 in range(e0, e1, 2):
+                lo, hi = (b0 - e0) * C, (min(b0 + 2, e1) - e0) * C
+                nc.vector.quantize_mx(
+                    out=xc[:, lo:hi].bitcast(FP8X4),
+                    scales=xs[:, s, e0 * C + lo : e0 * C + hi],
+                    in_=rounded[u][:, lo:hi, :].rearrange("p c t -> p (c t)"),
+                )
 
-        def first_layer(e, copy):
+        def first_product(e):
             cols = slice(e * C, (e + 1) * C)
             a = psum.tile([P, H], F32, name="a", tag="a", bufs=3)
             for s in range(PASSES):
@@ -170,60 +174,92 @@ def tile_moe_pre_mlp_gelu_kernel(
                     start=(s == 0),
                     stop=(s == PASSES - 1),
                 )
-            hb = ring.tile([P, 2, P, 2], BF16, name="hb", tag="hb")
+            hb = staged("hb%d" % e, [P, 2, P, 2], BF16)
             nc.scalar.activation(hb[:], a[:].rearrange("c (p u d) -> c u p d", u=2, d=2), GELU)
-            words = hb[:].rearrange("c u p d -> c (u p d)").bitcast(F32)
+            h_rows[e] = hb
+
+        def turn(e, copy):
+            words = h_rows[e][:].rearrange("c u p d -> c (u p d)").bitcast(F32)
             turned = psum.tile([P, 2, C], F32, name="turned", tag="turned", bufs=2)
             for u in range(2):
                 nc.tensor.transpose(turned[:, u, :], words[:, u * P : (u + 1) * P], ident[:])
-            if e in SECOND_BEFORE:
-                at = SECOND_BEFORE[e] * REGION + G_AT + 128 + (e % 2) * 1024
-            else:
-                at = 12 * REGION + (e - 4) * 1024
-            hq = arena.tile([P, C * PACK], BF16, name="hq%d" % e, offset=at, align_bytes=64)
+            hq = staged("hq%d" % e, [P, C * PACK], BF16)
             copy(hq[:].bitcast(F32).rearrange("p (c u) -> p c u", u=2), turned[:].rearrange("p u c -> p c u"))
             h_in[e] = hq
 
-        def second_layer(e, copies):
+        def second_product(e):
             cols = slice(e * C, (e + 1) * C)
-            at = codes_at(e + 3) if e in (4, 5) else 13 * REGION + e * 512
-            hc = arena.tile([P, C], U32, name="hc%d" % e, offset=at, align_bytes=64)
-            nc.vector.quantize_mx(out=hc[:].bitcast(FP8X4), scales=hs[:, cols], in_=h_in[e][:])
+            hk = staged("hk%d" % e, [P, C], U32)
+            nc.vector.quantize_mx(out=hk[:].bitcast(FP8X4), scales=hs[:, cols], in_=h_in[e][:])
             acc = psum.tile([P, CHUNKS, C], F32, name="acc", tag="acc", bufs=3)
             for c in range(CHUNKS):
                 nc.tensor.matmul_mx(
                     out=acc[:, c, :],
                     lhsT=w2c[:, e, 2 * P * c : 2 * P * (c + 1)].bitcast(FP4X4),
                     lhsT_scale=w2s[:, e, P * c : P * (c + 1)],
-                    rhs=hc[:].bitcast(FP8X4),
+                    rhs=hk[:].bitcast(FP8X4),
                     rhs_scale=hs[:, cols],
                     start=True,
                     stop=True,
                 )
-            for copy, c0, c1 in copies:
-                copy(y[:, c0:c1, cols], acc[:, c0:c1, :])
+            sums[e] = acc
 
-        for u, unit in enumerate(units):
-            last = u == len(units) - 1
-            for e in SECOND_BEFORE:
-                if SECOND_BEFORE[e] == u:
-                    second_layer(e, [(nc.scalar.copy, 0, CHUNKS)])
-            gather(unit)
-            if not last:
-                interleave(unit, nc.scalar.copy)
-            if u > 0:
-                quantise_x(units[u - 1])
-                (e0, e1), s = units[u - 1]
-                if s == PASSES - 1:
-                    for e in range(e0, e1):
-                        first_layer(e, nc.scalar.copy)
-        interleave(units[-1], nc.vector.tensor_copy)
-        quantise_x(units[-1])
-        first_layer(E - 1, nc.vector.tensor_copy)
-        second_layer(4, [(nc.scalar.copy, 0, CHUNKS)])
-        second_layer(5, [(nc.scalar.copy, 0, CHUNKS)])
-        second_layer(6, [(nc.vector.tensor_copy, 0, CHUNKS)])
-        second_layer(E - 1, [(nc.vector.tensor_copy, 0, 1), (nc.scalar.copy, 1, CHUNKS)])
+        def store_slots(e, copy, c0, c1):
+            copy(y[:, c0:c1, e * C : (e + 1) * C], sums[e][:, c0:c1, :])
+
+        on_scalar, on_vector = nc.scalar.copy, nc.vector.tensor_copy
+        gather(0)
+        interleave(0, on_scalar)
+        gather(1)
+        interleave(1, on_scalar)
+        quantise_x(0)
+        gather(2)
+        interleave(2, on_scalar)
+        quantise_x(1)
+        for e in range(0, 3):
+            first_product(e)
+        gather(3)
+        interleave(3, on_scalar)
+        quantise_x(2)
+        for e in range(0, 3):
+            turn(e, on_scalar)
+        gather(4)
+        interleave(4, on_scalar)
+        quantise_x(3)
+        for e in range(3, 5):
+            first_product(e)
+        gather(5)
+        interleave(5, on_scalar)
+        quantise_x(4)
+        for e in range(3, 5):
+            turn(e, on_scalar)
+        for e in range(0, 3):
+            second_product(e)
+            store_slots(e, on_scalar, 0, CHUNKS)
+        gather(6)
+        interleave(6, on_scalar)
+        quantise_x(5)
+        for e in range(5, 7):
+            first_product(e)
+        gather(7)
+        quantise_x(6)
+        interleave(7, on_vector)
+        second_product(3)
+        quantise_x(7)
+        turn(5, on_scalar)
+        turn(6, on_scalar)
+        first_product(7)
+        turn(7, on_vector)
+        store_slots(3, on_scalar, 0, CHUNKS)
+        second_product(4)
+        store_slots(4, on_scalar, 0, CHUNKS)
+        second_product(5)
+        store_slots(5, on_vector, 0, CHUNKS)
+        second_product(6)
+        store_slots(6, on_scalar, 0, CHUNKS)
+        second_product(7)
+        store_slots(7, on_vector, 0, 1)
+        store_slots(7, on_scalar, 1, CHUNKS)
 
         picked = [[keep.tile([P, T], F32, name="pick_%d_%d" % (c, r)) for r in range(2)] for c in range(CHUNKS)]
         summed = [keep.tile([P, T], F32, name="sum_%d" % c) for c in range(CHUNKS)]

@@ -33,8 +33,9 @@ CHAINS = [
     ["xc1", "xb3", "g5"],
     ["hb2", "xb4"],
     ["xc3", "xb5", "g7"],
-    ["hk2", "xb6"],
-    ["hk1", "xc5", "hk3"],
+    ["hk1", "xb6"],
+    ["hk0", "xc5", "hk3"],
+    ["x_1_2", "xc6"],
     ["xc7", "hk4"],
 ]
 BESIDE = {"g6": ("xb4", 1984), "hq2": ("xb4", 2112)}
@@ -49,10 +50,19 @@ def tile_moe_pre_mlp_gelu_kernel(
         arena = ctx.enter_context(tc.tile_pool(name="arena", bufs=1))
         psum = ctx.enter_context(tc.psum_pool(name="psum", bufs=1))
 
+        places = {name: r * REGION for r, chain in enumerate(CHAINS) for name in chain}
+        for name in BESIDE:
+            places[name] = places[BESIDE[name][0]] + BESIDE[name][1]
+
+        def staged(name, shape, dtype):
+            if name in places:
+                return arena.tile(shape, dtype, name=name, offset=places[name], align_bytes=64)
+            return keep.tile(shape, dtype, name=name, align_bytes=64)
+
+        planes = [[staged("x_%d_%d" % (s, j), [P, T], F32) for j in range(PACK)] for s in range(PASSES)]
         offs_sb = keep.tile([P, SLOTS // 16], U16, name="offs_sb")
         pos_sb = [keep.tile([P, T // 16], U16, name="pos%d_sb" % r) for r in range(2)]
         gate_sb = keep.tile([P, SLOTS], F32, name="gate_sb")
-        planes = [[keep.tile([P, T], F32, name="x_%d_%d" % (s, j)) for j in range(PACK)] for s in range(PASSES)]
         w1c = keep.tile([P, E, PASSES, 2 * H], U8, name="w1c", align_bytes=64)
         w1s = keep.tile([P, E, PASSES, H], U8, name="w1s", align_bytes=64)
         w2c = keep.tile([P, E, 2 * N], U8, name="w2c", align_bytes=64)
@@ -63,9 +73,9 @@ def tile_moe_pre_mlp_gelu_kernel(
         ident = keep.tile([P, P], F32, name="ident")
         warm = keep.tile([P, 8], F32, name="warm")
 
-        nc.vector.memset(w1s[:].rearrange("p e s i -> p (e s i)").bitcast(I32), 0)
-        nc.vector.memset(w2s[:].rearrange("p e n -> p (e n)").bitcast(I32), 0)
         make_identity(nc, ident[:])
+        nc.gpsimd.memset(w1s[:].rearrange("p e s i -> p (e s i)").bitcast(I32), 0)
+        nc.gpsimd.memset(w2s[:].rearrange("p e n -> p (e n)").bitcast(I32), 0)
         nc.scalar.activation(warm[:], ident[:, 0:8], GELU)
 
         x_rows = xT.rearrange("(s p j) t -> s j p t", s=PASSES, j=PACK)
@@ -100,10 +110,11 @@ def tile_moe_pre_mlp_gelu_kernel(
             for j in range(PACK):
                 nc.sync.dma_start(planes[s][j][:], x_rows[s, j])
         nc.sync.dma_start(gate_sb[:, first:SLOTS], gate[0:P, first:SLOTS])
-        load_w1_scales(0, 8)
+        load_w1_scales(0, 5)
         load_w1(0, 1)
         load_w1(1, 3)
         load_w1(3, 5)
+        load_w1_scales(5, 8)
         load_w2_scales()
         load_w2(0, 4)
         load_w1(5, 7)
@@ -111,15 +122,6 @@ def tile_moe_pre_mlp_gelu_kernel(
         load_w2(4, 8)
         nc.sync.dma_start(pos_sb[0][:], pos1)
         nc.sync.dma_start(pos_sb[1][:], pos2)
-
-        places = {name: r * REGION for r, chain in enumerate(CHAINS) for name in chain}
-        for name in BESIDE:
-            places[name] = places[BESIDE[name][0]] + BESIDE[name][1]
-
-        def staged(name, shape, dtype):
-            if name in places:
-                return arena.tile(shape, dtype, name=name, offset=places[name], align_bytes=64)
-            return keep.tile(shape, dtype, name=name, align_bytes=64)
 
         units = [(e0, e1, s) for e0, e1 in GROUPS for s in range(PASSES)]
         gathered = {}
@@ -129,11 +131,11 @@ def tile_moe_pre_mlp_gelu_kernel(
         h_in = {}
         sums = {}
 
-        def gather(u):
+        def gather(u, j0=0, j1=PACK):
             e0, e1, s = units[u]
             lo, hi = e0 * C, e1 * C
-            g = staged("g%d" % u, [P, PACK, hi - lo], F32)
-            for j in range(PACK):
+            g = gathered[u] if j0 else staged("g%d" % u, [P, PACK, hi - lo], F32)
+            for j in range(j0, j1):
                 nc.vector.tensor_tensor(
                     g[:, j, :], planes[s][j][:].indirect(offs_sb[:, lo // 16 : hi // 16]), gate_sb[:, lo:hi], MULT
                 )
@@ -161,7 +163,7 @@ def tile_moe_pre_mlp_gelu_kernel(
                     in_=rounded[u][:, lo:hi, :].rearrange("p c t -> p (c t)"),
                 )
 
-        def first_product(e):
+        def first_product(e, halves=1):
             cols = slice(e * C, (e + 1) * C)
             a = psum.tile([P, H], F32, name="a", tag="a", bufs=3)
             for s in range(PASSES):
@@ -175,7 +177,9 @@ def tile_moe_pre_mlp_gelu_kernel(
                     stop=(s == PASSES - 1),
                 )
             hb = staged("hb%d" % e, [P, 2, P, 2], BF16)
-            nc.scalar.activation(hb[:], a[:].rearrange("c (p u d) -> c u p d", u=2, d=2), GELU)
+            pairs = a[:].rearrange("c (p u d) -> c u p d", u=2, d=2)
+            for u in range(0, 2, 2 // halves):
+                nc.scalar.activation(hb[:, u : u + 2 // halves], pairs[:, u : u + 2 // halves], GELU)
             h_rows[e] = hb
 
         def turn(e, copy):
@@ -235,42 +239,66 @@ def tile_moe_pre_mlp_gelu_kernel(
             turn(e, on_scalar)
         for e in range(0, 3):
             second_product(e)
+        for e in range(0, 2):
             store_slots(e, on_scalar, 0, CHUNKS)
         gather(6)
         interleave(6, on_scalar)
+        store_slots(2, on_scalar, 0, CHUNKS)
         quantise_x(5)
         for e in range(5, 7):
             first_product(e)
-        gather(7)
+        gather(7, 0, 3)
         quantise_x(6)
+        gather(7, 3, PACK)
         interleave(7, on_vector)
         second_product(3)
         quantise_x(7)
         turn(5, on_scalar)
         turn(6, on_scalar)
-        first_product(7)
+        first_product(7, 2)
         turn(7, on_vector)
-        store_slots(3, on_scalar, 0, CHUNKS)
-        second_product(4)
-        store_slots(4, on_scalar, 0, CHUNKS)
-        second_product(5)
-        store_slots(5, on_vector, 0, CHUNKS)
-        second_product(6)
-        store_slots(6, on_scalar, 0, CHUNKS)
+        for e in range(3, 7):
+            if e > 3:
+                second_product(e)
+            store_slots(e, on_scalar, 0, CHUNKS)
         second_product(7)
         store_slots(7, on_vector, 0, 1)
         store_slots(7, on_scalar, 1, CHUNKS)
 
         picked = [[keep.tile([P, T], F32, name="pick_%d_%d" % (c, r)) for r in range(2)] for c in range(CHUNKS)]
         summed = [keep.tile([P, T], F32, name="sum_%d" % c) for c in range(CHUNKS)]
+        half = T // 2
 
-        def combine(c):
-            nc.vector.tensor_tensor(summed[c][:], picked[c][0][:], picked[c][1][:], ADD)
-            nc.sync.dma_start(out[c * P : (c + 1) * P, :], summed[c][:])
+        def add_on_tensor(c):
+            for h in range(2):
+                by_token = psum.tile([P, 2, P], F32, name="by_token", tag="a", bufs=3)
+                for b in range(2):
+                    cols = slice(h * half + b * P, h * half + (b + 1) * P)
+                    for r in range(2):
+                        nc.tensor.matmul(
+                            by_token[:, b, :], picked[c][r][:, cols], ident[:], start=(r == 0), stop=(r == 1), is_transpose=True
+                        )
+                rows = keep.tile([P, 2, P], F32, name="rows_%d_%d" % (c, h))
+                nc.scalar.copy(rows[:], by_token[:])
+                back = psum.tile([P, 2, P], F32, name="back", tag="acc", bufs=3)
+                for b in range(2):
+                    nc.tensor.transpose(back[:, b, :], rows[:, b, :], ident[:])
+                cols = slice(h * half, (h + 1) * half)
+                nc.scalar.copy(summed[c][:, cols], back[:].rearrange("p b t -> p (b t)"))
+                nc.sync.dma_start(out[c * P : (c + 1) * P, cols], summed[c][:, cols])
 
-        for c in range(CHUNKS):
-            nc.vector.tensor_copy(picked[c][0][:], y[:, c, :].indirect(pos_sb[0][:]))
-            if c > 0:
-                combine(c - 1)
-            nc.vector.tensor_copy(picked[c][1][:], y[:, c, :].indirect(pos_sb[1][:]))
-        combine(CHUNKS - 1)
+        for c in range(CHUNKS - 1):
+            for r in range(2):
+                nc.vector.tensor_copy(picked[c][r][:], y[:, c, :].indirect(pos_sb[r][:]))
+            add_on_tensor(c)
+        c = CHUNKS - 1
+        nc.vector.tensor_copy(picked[c][0][:], y[:, c, :].indirect(pos_sb[0][:]))
+        for h in range(2):
+            cols = slice(h * half, (h + 1) * half)
+            nc.vector.tensor_copy(
+                picked[c][1][:, cols], y[:, c, :].indirect(pos_sb[1][:, h * half // 16 : (h + 1) * half // 16])
+            )
+        for h in range(2):
+            cols = slice(h * half, (h + 1) * half)
+            nc.vector.tensor_tensor(summed[c][:, cols], picked[c][0][:, cols], picked[c][1][:, cols], ADD)
+            nc.sync.dma_start(out[c * P : (c + 1) * P, cols], summed[c][:, cols])

@@ -25,20 +25,8 @@ ADD = mybir.AluOpType.add
 GELU = mybir.ActivationFunctionType.Gelu_apprx_tanh
 
 GROUPS = [(0, 3), (3, 5), (5, 7), (7, 8)]
-REGION = 6144
-CHAINS = [
-    ["xb0", "g2"],
-    ["xb1", "g3"],
-    ["xb2", "g4"],
-    ["xc1", "xb3", "g5"],
-    ["hb2", "xb4"],
-    ["xc3", "xb5", "g7"],
-    ["hk1", "xb6"],
-    ["hk0", "xc5", "hk3"],
-    ["x_1_2", "xc6"],
-    ["xc7", "hk4"],
-]
-BESIDE = {"g6": ("xb4", 1984), "hq2": ("xb4", 2112)}
+TURNS = [(0, 2), (2, 3), (3, 5), (5, 7), (7, 8)]
+HELD_BEHIND = {3: "xc1", 4: "hb2", 5: "xc3", 6: "hb4"}
 
 
 def tile_moe_pre_mlp_gelu_kernel(
@@ -47,21 +35,13 @@ def tile_moe_pre_mlp_gelu_kernel(
     nc = tc.nc
     with ExitStack() as ctx:
         keep = ctx.enter_context(tc.tile_pool(name="keep", bufs=1))
-        arena = ctx.enter_context(tc.tile_pool(name="arena", bufs=1))
         psum = ctx.enter_context(tc.psum_pool(name="psum", bufs=1))
 
-        places = {name: r * REGION for r, chain in enumerate(CHAINS) for name in chain}
-        for name in BESIDE:
-            places[name] = places[BESIDE[name][0]] + BESIDE[name][1]
-
-        def staged(name, shape, dtype):
-            if name in places:
-                return arena.tile(shape, dtype, name=name, offset=places[name], align_bytes=64)
-            return keep.tile(shape, dtype, name=name, align_bytes=64)
-
-        planes = [[staged("x_%d_%d" % (s, j), [P, T], F32) for j in range(PACK)] for s in range(PASSES)]
         offs_sb = keep.tile([P, SLOTS // 16], U16, name="offs_sb")
         pos_sb = [keep.tile([P, T // 16], U16, name="pos%d_sb" % r) for r in range(2)]
+        planes = [
+            [keep.tile([P, T], F32, name="x_%d_%d" % (s, j), align_bytes=64) for j in range(PACK)] for s in range(PASSES)
+        ]
         gate_sb = keep.tile([P, SLOTS], F32, name="gate_sb")
         w1c = keep.tile([P, E, PASSES, 2 * H], U8, name="w1c", align_bytes=64)
         w1s = keep.tile([P, E, PASSES, H], U8, name="w1s", align_bytes=64)
@@ -69,7 +49,7 @@ def tile_moe_pre_mlp_gelu_kernel(
         w2s = keep.tile([P, E, N], U8, name="w2s", align_bytes=64)
         xs = keep.tile([P, PASSES, SLOTS], U8, name="xs", align_bytes=64)
         hs = keep.tile([P, SLOTS], U8, name="hs", align_bytes=64)
-        y = keep.tile([P, CHUNKS, SLOTS], F32, name="y")
+        y = [keep.tile([P, SLOTS], F32, name="y%d" % c) for c in range(CHUNKS)]
         ident = keep.tile([P, P], F32, name="ident")
         warm = keep.tile([P, 8], F32, name="warm")
 
@@ -110,16 +90,15 @@ def tile_moe_pre_mlp_gelu_kernel(
             for j in range(PACK):
                 nc.sync.dma_start(planes[s][j][:], x_rows[s, j])
         nc.sync.dma_start(gate_sb[:, first:SLOTS], gate[0:P, first:SLOTS])
-        load_w1_scales(0, 5)
+        load_w1_scales(0, 3)
         load_w1(0, 1)
         load_w1(1, 3)
-        load_w1(3, 5)
-        load_w1_scales(5, 8)
+        load_w1_scales(3, 8)
         load_w2_scales()
-        load_w2(0, 4)
+        load_w1(3, 5)
         load_w1(5, 7)
         load_w1(7, 8)
-        load_w2(4, 8)
+        load_w2(0, 8)
         nc.sync.dma_start(pos_sb[0][:], pos1)
         nc.sync.dma_start(pos_sb[1][:], pos2)
 
@@ -129,13 +108,12 @@ def tile_moe_pre_mlp_gelu_kernel(
         x_codes = {}
         h_rows = {}
         h_in = {}
-        sums = {}
 
-        def gather(u, j0=0, j1=PACK):
+        def gather(u):
             e0, e1, s = units[u]
             lo, hi = e0 * C, e1 * C
-            g = gathered[u] if j0 else staged("g%d" % u, [P, PACK, hi - lo], F32)
-            for j in range(j0, j1):
+            g = keep.tile([P, PACK, hi - lo], F32, name="g%d" % u, tag="g%d" % (u % 2))
+            for j in range(PACK):
                 nc.vector.tensor_tensor(
                     g[:, j, :], planes[s][j][:].indirect(offs_sb[:, lo // 16 : hi // 16]), gate_sb[:, lo:hi], MULT
                 )
@@ -143,7 +121,8 @@ def tile_moe_pre_mlp_gelu_kernel(
 
         def interleave(u, copy):
             g = gathered[u]
-            xb = staged("xb%d" % u, [P, g.shape[2], PACK], BF16)
+            tag = HELD_BEHIND.get(u, "xb%d" % u)
+            xb = keep.tile([P, g.shape[2], PACK], BF16, name="xb%d" % u, tag=tag, align_bytes=64)
             copy(
                 xb[:].rearrange("p (c i) t -> p c t i", i=4),
                 g[:].rearrange("p t (c i) -> p c t i", i=4),
@@ -152,7 +131,7 @@ def tile_moe_pre_mlp_gelu_kernel(
 
         def quantise_x(u):
             e0, e1, s = units[u]
-            xc = staged("xc%d" % u, [P, (e1 - e0) * C], U32)
+            xc = keep.tile([P, (e1 - e0) * C], U32, name="xc%d" % u, tag="xc%d" % u, align_bytes=64)
             for e in range(e0, e1):
                 x_codes[e, s] = xc[:, (e - e0) * C : (e - e0 + 1) * C]
             for b0 in range(e0, e1, 2):
@@ -176,40 +155,44 @@ def tile_moe_pre_mlp_gelu_kernel(
                     start=(s == 0),
                     stop=(s == PASSES - 1),
                 )
-            hb = staged("hb%d" % e, [P, 2, P, 2], BF16)
+            hb = keep.tile([P, 2, P, 2], BF16, name="hb%d" % e, align_bytes=64)
             pairs = a[:].rearrange("c (p u d) -> c u p d", u=2, d=2)
             for u in range(0, 2, 2 // halves):
                 nc.scalar.activation(hb[:, u : u + 2 // halves], pairs[:, u : u + 2 // halves], GELU)
             h_rows[e] = hb
 
-        def turn(e, copy):
-            words = h_rows[e][:].rearrange("c u p d -> c (u p d)").bitcast(F32)
-            turned = psum.tile([P, 2, C], F32, name="turned", tag="turned", bufs=2)
-            for u in range(2):
-                nc.tensor.transpose(turned[:, u, :], words[:, u * P : (u + 1) * P], ident[:])
-            hq = staged("hq%d" % e, [P, C * PACK], BF16)
-            copy(hq[:].bitcast(F32).rearrange("p (c u) -> p c u", u=2), turned[:].rearrange("p u c -> p c u"))
-            h_in[e] = hq
+        def turn(i, copy):
+            e0, e1 = TURNS[i]
+            turned = psum.tile([P, e1 - e0, 2, C], F32, name="turned", tag="turned", bufs=2)
+            for e in range(e0, e1):
+                words = h_rows[e][:].rearrange("c u p d -> c (u p d)").bitcast(F32)
+                for u in range(2):
+                    nc.tensor.transpose(turned[:, e - e0, u, :], words[:, u * P : (u + 1) * P], ident[:])
+            hq = keep.tile([P, (e1 - e0) * C * PACK], BF16, name="hq%d" % i, align_bytes=64)
+            copy(
+                hq[:].bitcast(F32).rearrange("p (e c u) -> p e c u", u=2, c=C),
+                turned[:].rearrange("p e u c -> p e c u"),
+            )
+            h_in[i] = hq
 
-        def second_product(e):
-            cols = slice(e * C, (e + 1) * C)
-            hk = staged("hk%d" % e, [P, C], U32)
-            nc.vector.quantize_mx(out=hk[:].bitcast(FP8X4), scales=hs[:, cols], in_=h_in[e][:])
-            acc = psum.tile([P, CHUNKS, C], F32, name="acc", tag="acc", bufs=3)
-            for c in range(CHUNKS):
+        def quantise_h(hk, i):
+            cols = slice(TURNS[i][0] * C, TURNS[i][1] * C)
+            nc.vector.quantize_mx(out=hk[:, cols].bitcast(FP8X4), scales=hs[:, cols], in_=h_in[i][:])
+
+        def second_product(hk, c, e0, e1, tag, copy):
+            acc = psum.tile([P, (e1 - e0) * C], F32, name="acc", tag=tag, bufs=3)
+            for e in range(e0, e1):
+                cols = slice(e * C, (e + 1) * C)
                 nc.tensor.matmul_mx(
-                    out=acc[:, c, :],
+                    out=acc[:, (e - e0) * C : (e - e0 + 1) * C],
                     lhsT=w2c[:, e, 2 * P * c : 2 * P * (c + 1)].bitcast(FP4X4),
                     lhsT_scale=w2s[:, e, P * c : P * (c + 1)],
-                    rhs=hk[:].bitcast(FP8X4),
+                    rhs=hk[:, cols].bitcast(FP8X4),
                     rhs_scale=hs[:, cols],
                     start=True,
                     stop=True,
                 )
-            sums[e] = acc
-
-        def store_slots(e, copy, c0, c1):
-            copy(y[:, c0:c1, e * C : (e + 1) * C], sums[e][:, c0:c1, :])
+            copy(y[c][:, e0 * C : e1 * C], acc[:])
 
         on_scalar, on_vector = nc.scalar.copy, nc.vector.tensor_copy
         gather(0)
@@ -225,8 +208,8 @@ def tile_moe_pre_mlp_gelu_kernel(
         gather(3)
         interleave(3, on_scalar)
         quantise_x(2)
-        for e in range(0, 3):
-            turn(e, on_scalar)
+        turn(0, on_scalar)
+        turn(1, on_scalar)
         gather(4)
         interleave(4, on_scalar)
         quantise_x(3)
@@ -235,70 +218,45 @@ def tile_moe_pre_mlp_gelu_kernel(
         gather(5)
         interleave(5, on_scalar)
         quantise_x(4)
-        for e in range(3, 5):
-            turn(e, on_scalar)
-        for e in range(0, 3):
-            second_product(e)
-        for e in range(0, 2):
-            store_slots(e, on_scalar, 0, CHUNKS)
         gather(6)
+        turn(2, on_scalar)
         interleave(6, on_scalar)
-        store_slots(2, on_scalar, 0, CHUNKS)
         quantise_x(5)
+        quantise_x(6)
         for e in range(5, 7):
             first_product(e)
-        gather(7, 0, 3)
-        quantise_x(6)
-        gather(7, 3, PACK)
+        gather(7)
         interleave(7, on_vector)
-        second_product(3)
         quantise_x(7)
-        turn(5, on_scalar)
-        turn(6, on_scalar)
+        turn(3, on_scalar)
         first_product(7, 2)
-        turn(7, on_vector)
-        for e in range(3, 7):
-            if e > 3:
-                second_product(e)
-            store_slots(e, on_scalar, 0, CHUNKS)
-        second_product(7)
-        store_slots(7, on_vector, 0, 1)
-        store_slots(7, on_scalar, 1, CHUNKS)
+        hk = keep.tile([P, SLOTS], U32, name="hk", tag="x_1_3", align_bytes=64)
+        turn(4, on_vector)
+        quantise_h(hk, 4)
+        for i in range(4):
+            quantise_h(hk, i)
+        second_product(hk, 0, 7, 8, "acc", on_vector)
+        second_product(hk, 0, 0, 3, "acc", on_scalar)
+        second_product(hk, 0, 3, 7, "acc", on_scalar)
+        for c in range(1, CHUNKS):
+            for e0 in range(0, E, 4):
+                second_product(hk, c, e0, e0 + 4, "a" if c == 1 else "acc", on_scalar)
 
-        picked = [[keep.tile([P, T], F32, name="pick_%d_%d" % (c, r)) for r in range(2)] for c in range(CHUNKS)]
-        summed = [keep.tile([P, T], F32, name="sum_%d" % c) for c in range(CHUNKS)]
         half = T // 2
-
-        def add_on_tensor(c):
+        for c in range(CHUNKS):
+            picked = keep.tile([P, T], F32, name="picked%d" % c)
+            summed = keep.tile([P, T], F32, name="summed%d" % c)
             for h in range(2):
-                by_token = psum.tile([P, 2, P], F32, name="by_token", tag="a", bufs=3)
-                for b in range(2):
-                    cols = slice(h * half + b * P, h * half + (b + 1) * P)
-                    for r in range(2):
-                        nc.tensor.matmul(
-                            by_token[:, b, :], picked[c][r][:, cols], ident[:], start=(r == 0), stop=(r == 1), is_transpose=True
-                        )
-                rows = keep.tile([P, 2, P], F32, name="rows_%d_%d" % (c, h))
-                nc.scalar.copy(rows[:], by_token[:])
-                back = psum.tile([P, 2, P], F32, name="back", tag="acc", bufs=3)
-                for b in range(2):
-                    nc.tensor.transpose(back[:, b, :], rows[:, b, :], ident[:])
                 cols = slice(h * half, (h + 1) * half)
-                nc.scalar.copy(summed[c][:, cols], back[:].rearrange("p b t -> p (b t)"))
-                nc.sync.dma_start(out[c * P : (c + 1) * P, cols], summed[c][:, cols])
-
-        for c in range(CHUNKS - 1):
-            for r in range(2):
-                nc.vector.tensor_copy(picked[c][r][:], y[:, c, :].indirect(pos_sb[r][:]))
-            add_on_tensor(c)
-        c = CHUNKS - 1
-        nc.vector.tensor_copy(picked[c][0][:], y[:, c, :].indirect(pos_sb[0][:]))
-        for h in range(2):
-            cols = slice(h * half, (h + 1) * half)
-            nc.vector.tensor_copy(
-                picked[c][1][:, cols], y[:, c, :].indirect(pos_sb[1][:, h * half // 16 : (h + 1) * half // 16])
-            )
-        for h in range(2):
-            cols = slice(h * half, (h + 1) * half)
-            nc.vector.tensor_tensor(summed[c][:, cols], picked[c][0][:, cols], picked[c][1][:, cols], ADD)
-            nc.sync.dma_start(out[c * P : (c + 1) * P, cols], summed[c][:, cols])
+                nc.vector.tensor_copy(
+                    picked[:, cols], y[c][:].indirect(pos_sb[0][:, h * half // 16 : (h + 1) * half // 16])
+                )
+            for h in range(2):
+                cols = slice(h * half, (h + 1) * half)
+                nc.vector.tensor_tensor(
+                    summed[:, cols],
+                    y[c][:].indirect(pos_sb[1][:, h * half // 16 : (h + 1) * half // 16]),
+                    picked[:, cols],
+                    ADD,
+                )
+                nc.sync.dma_start(out[c * P : (c + 1) * P, cols], summed[:, cols])

@@ -25,7 +25,7 @@ ADD = mybir.AluOpType.add
 GELU = mybir.ActivationFunctionType.Gelu_apprx_tanh
 
 GROUPS = [(0, 3), (3, 5), (5, 7), (7, 8)]
-TURNS = [(0, 2), (2, 3), (3, 5), (5, 7), (7, 8)]
+TURNS = [(0, 2), (2, 3), (3, 5), (5, 6), (6, 7), (7, 8)]
 HELD_BEHIND = {3: "xc1", 4: "hb2", 5: "xc3", 6: "hb4"}
 
 
@@ -54,7 +54,7 @@ def tile_moe_pre_mlp_gelu_kernel(
         warm = keep.tile([P, 8], F32, name="warm")
 
         make_identity(nc, ident[:])
-        nc.gpsimd.memset(w1s[:].rearrange("p e s i -> p (e s i)").bitcast(I32), 0)
+        nc.vector.memset(w1s[:].rearrange("p e s i -> p (e s i)").bitcast(I32), 0)
         nc.gpsimd.memset(w2s[:].rearrange("p e n -> p (e n)").bitcast(I32), 0)
         nc.scalar.activation(warm[:], ident[:, 0:8], GELU)
 
@@ -84,11 +84,14 @@ def tile_moe_pre_mlp_gelu_kernel(
                 w2c[:, e0:e1].bitcast(I32), w2_words[e0:e1].rearrange("e s p b -> p (e s) b").bitcast(I32)
             )
 
+        nc.sync.dma_start(planes[0][0][:], x_rows[0, 0])
         nc.sync.dma_start(offs_sb[:], offs)
-        nc.sync.dma_start(gate_sb[:, 0:first], gate[0:P, 0:first])
+        nc.sync.dma_start(gate_sb[:, 0:C], gate[0:P, 0:C])
+        nc.sync.dma_start(gate_sb[:, C:first], gate[0:P, C:first])
         for s in range(PASSES):
             for j in range(PACK):
-                nc.sync.dma_start(planes[s][j][:], x_rows[s, j])
+                if s or j:
+                    nc.sync.dma_start(planes[s][j][:], x_rows[s, j])
         nc.sync.dma_start(gate_sb[:, first:SLOTS], gate[0:P, first:SLOTS])
         load_w1_scales(0, 3)
         load_w1(0, 1)
@@ -106,7 +109,9 @@ def tile_moe_pre_mlp_gelu_kernel(
         gathered = {}
         rounded = {}
         x_codes = {}
+        sums = {}
         h_rows = {}
+        h_turned = {}
         h_in = {}
 
         def gather(u):
@@ -114,9 +119,14 @@ def tile_moe_pre_mlp_gelu_kernel(
             lo, hi = e0 * C, e1 * C
             g = keep.tile([P, PACK, hi - lo], F32, name="g%d" % u, tag="g%d" % (u % 2))
             for j in range(PACK):
-                nc.vector.tensor_tensor(
-                    g[:, j, :], planes[s][j][:].indirect(offs_sb[:, lo // 16 : hi // 16]), gate_sb[:, lo:hi], MULT
-                )
+                cuts = [lo, C, hi] if (u, j) == (0, 0) else [lo, hi]
+                for a, b in zip(cuts, cuts[1:]):
+                    nc.vector.tensor_tensor(
+                        g[:, j, a - lo : b - lo],
+                        planes[s][j][:].indirect(offs_sb[:, a // 16 : b // 16]),
+                        gate_sb[:, a:b],
+                        MULT,
+                    )
             gathered[u] = g
 
         def interleave(u, copy):
@@ -142,32 +152,40 @@ def tile_moe_pre_mlp_gelu_kernel(
                     in_=rounded[u][:, lo:hi, :].rearrange("p c t -> p (c t)"),
                 )
 
-        def first_product(e, halves=1):
-            cols = slice(e * C, (e + 1) * C)
-            a = psum.tile([P, H], F32, name="a", tag="a", bufs=3)
-            for s in range(PASSES):
+        def first_pass(u):
+            e0, e1, s = units[u]
+            for e in range(e0, e1):
+                if s == 0:
+                    sums[e] = psum.tile([P, H], F32, name="a", tag="a%d" % (e % 3))
                 nc.tensor.matmul_mx(
-                    out=a[:],
+                    out=sums[e][:],
                     lhsT=x_codes[e, s].bitcast(FP8X4),
-                    lhsT_scale=xs[:, s, cols],
+                    lhsT_scale=xs[:, s, e * C : (e + 1) * C],
                     rhs=w1c[:, e, s, :].bitcast(FP4X4),
                     rhs_scale=w1s[:, e, s, :],
                     start=(s == 0),
                     stop=(s == PASSES - 1),
                 )
+
+        def activate(e, halves=1):
             hb = keep.tile([P, 2, P, 2], BF16, name="hb%d" % e, align_bytes=64)
-            pairs = a[:].rearrange("c (p u d) -> c u p d", u=2, d=2)
+            pairs = sums[e][:].rearrange("c (p u d) -> c u p d", u=2, d=2)
             for u in range(0, 2, 2 // halves):
                 nc.scalar.activation(hb[:, u : u + 2 // halves], pairs[:, u : u + 2 // halves], GELU)
             h_rows[e] = hb
 
-        def turn(i, copy):
+        def turn(i):
             e0, e1 = TURNS[i]
             turned = psum.tile([P, e1 - e0, 2, C], F32, name="turned", tag="turned", bufs=2)
             for e in range(e0, e1):
                 words = h_rows[e][:].rearrange("c u p d -> c (u p d)").bitcast(F32)
                 for u in range(2):
                     nc.tensor.transpose(turned[:, e - e0, u, :], words[:, u * P : (u + 1) * P], ident[:])
+            h_turned[i] = turned
+
+        def weave(i, copy):
+            e0, e1 = TURNS[i]
+            turned = h_turned[i]
             hq = keep.tile([P, (e1 - e0) * C * PACK], BF16, name="hq%d" % i, align_bytes=64)
             copy(
                 hq[:].bitcast(F32).rearrange("p (e c u) -> p e c u", u=2, c=C),
@@ -180,7 +198,7 @@ def tile_moe_pre_mlp_gelu_kernel(
             nc.vector.quantize_mx(out=hk[:, cols].bitcast(FP8X4), scales=hs[:, cols], in_=h_in[i][:])
 
         def second_product(hk, c, e0, e1, tag, copy):
-            acc = psum.tile([P, (e1 - e0) * C], F32, name="acc", tag=tag, bufs=3)
+            acc = psum.tile([P, (e1 - e0) * C], F32, name="acc", tag=tag)
             for e in range(e0, e1):
                 cols = slice(e * C, (e + 1) * C)
                 nc.tensor.matmul_mx(
@@ -200,47 +218,60 @@ def tile_moe_pre_mlp_gelu_kernel(
         gather(1)
         interleave(1, on_scalar)
         quantise_x(0)
+        first_pass(0)
         gather(2)
         interleave(2, on_scalar)
         quantise_x(1)
+        first_pass(1)
         for e in range(0, 3):
-            first_product(e)
+            activate(e)
         gather(3)
         interleave(3, on_scalar)
         quantise_x(2)
-        turn(0, on_scalar)
-        turn(1, on_scalar)
+        first_pass(2)
+        for i in range(2):
+            turn(i)
+            weave(i, on_scalar)
         gather(4)
         interleave(4, on_scalar)
         quantise_x(3)
+        first_pass(3)
         for e in range(3, 5):
-            first_product(e)
+            activate(e)
         gather(5)
         interleave(5, on_scalar)
         quantise_x(4)
+        first_pass(4)
         gather(6)
-        turn(2, on_scalar)
+        turn(2)
         interleave(6, on_scalar)
+        weave(2, on_scalar)
         quantise_x(5)
+        first_pass(5)
         quantise_x(6)
+        first_pass(6)
         for e in range(5, 7):
-            first_product(e)
+            activate(e)
         gather(7)
         interleave(7, on_vector)
         quantise_x(7)
-        turn(3, on_scalar)
-        first_product(7, 2)
+        first_pass(7)
+        for i in range(3, 5):
+            turn(i)
+            weave(i, on_vector)
+        activate(7, 2)
         hk = keep.tile([P, SLOTS], U32, name="hk", tag="x_1_3", align_bytes=64)
-        turn(4, on_vector)
-        quantise_h(hk, 4)
-        for i in range(4):
+        turn(5)
+        weave(5, on_vector)
+        for i in reversed(range(len(TURNS))):
             quantise_h(hk, i)
-        second_product(hk, 0, 7, 8, "acc", on_vector)
-        second_product(hk, 0, 0, 3, "acc", on_scalar)
-        second_product(hk, 0, 3, 7, "acc", on_scalar)
-        for c in range(1, CHUNKS):
-            for e0 in range(0, E, 4):
-                second_product(hk, c, e0, e0 + 4, "a" if c == 1 else "acc", on_scalar)
+        second_product(hk, 0, 7, 8, "acc0", on_vector)
+        second_product(hk, 0, 0, 3, "acc1", on_scalar)
+        second_product(hk, 0, 3, 7, "acc2", on_scalar)
+        second_product(hk, 1, 0, 4, "a1", on_scalar)
+        second_product(hk, 1, 4, 8, "a2", on_scalar)
+        second_product(hk, 2, 0, 4, "acc2", on_scalar)
+        second_product(hk, 2, 4, 8, "a0", on_scalar)
 
         half = T // 2
         for c in range(CHUNKS):
@@ -251,12 +282,9 @@ def tile_moe_pre_mlp_gelu_kernel(
                 nc.vector.tensor_copy(
                     picked[:, cols], y[c][:].indirect(pos_sb[0][:, h * half // 16 : (h + 1) * half // 16])
                 )
-            for h in range(2):
-                cols = slice(h * half, (h + 1) * half)
+            cuts = [0, half, T - P, T] if c == CHUNKS - 1 else [0, half, T]
+            for a, b in zip(cuts, cuts[1:]):
                 nc.vector.tensor_tensor(
-                    summed[:, cols],
-                    y[c][:].indirect(pos_sb[1][:, h * half // 16 : (h + 1) * half // 16]),
-                    picked[:, cols],
-                    ADD,
+                    summed[:, a:b], y[c][:].indirect(pos_sb[1][:, a // 16 : b // 16]), picked[:, a:b], ADD
                 )
-                nc.sync.dma_start(out[c * P : (c + 1) * P, cols], summed[:, cols])
+                nc.sync.dma_start(out[c * P : (c + 1) * P, a:b], summed[:, a:b])

@@ -24,9 +24,9 @@ MULT = mybir.AluOpType.mult
 ADD = mybir.AluOpType.add
 GELU = mybir.ActivationFunctionType.Gelu_apprx_tanh
 
-GROUPS = [(0, 3), (3, 5), (5, 7), (7, 8)]
+UNITS = [(0, 3, 0), (0, 3, 1), (3, 5, 0), (3, 5, 1), (5, 7, 0), (7, 8, 0), (5, 6, 1), (6, 7, 1), (7, 8, 1)]
 TURNS = [(0, 2), (2, 3), (3, 5), (5, 6), (6, 7), (7, 8)]
-HELD_BEHIND = {3: "xc1", 4: "hb2", 5: "xc3", 6: "hb4"}
+HELD_BEHIND = {3: "xc1", 4: "hb2", 5: "xc3", 7: "hb4"}
 
 
 def tile_moe_pre_mlp_gelu_kernel(
@@ -59,7 +59,7 @@ def tile_moe_pre_mlp_gelu_kernel(
         nc.scalar.activation(warm[:], ident[:, 0:8], GELU)
 
         x_rows = xT.rearrange("(s p j) t -> s j p t", s=PASSES, j=PACK)
-        first = GROUPS[0][1] * C
+        first = UNITS[0][1] * C
 
         def load_w1_scales(e0, e1):
             rows = w1_scales[e0:e1].rearrange("e s q i -> q (e s) i")
@@ -105,7 +105,6 @@ def tile_moe_pre_mlp_gelu_kernel(
         nc.sync.dma_start(pos_sb[0][:], pos1)
         nc.sync.dma_start(pos_sb[1][:], pos2)
 
-        units = [(e0, e1, s) for e0, e1 in GROUPS for s in range(PASSES)]
         gathered = {}
         rounded = {}
         x_codes = {}
@@ -114,10 +113,23 @@ def tile_moe_pre_mlp_gelu_kernel(
         h_turned = {}
         h_in = {}
 
+        def staging(u, tag, count=1):
+            width = (UNITS[u][1] - UNITS[u][0]) * C
+            g = keep.tile([P, count, PACK, width], F32, name="g%d" % u, tag=tag)
+            for k in range(count):
+                gathered[u + k] = g[:, k]
+
+        def rounding(u, count=1):
+            width = (UNITS[u][1] - UNITS[u][0]) * C
+            tag = HELD_BEHIND.get(u, "xb%d" % u)
+            xb = keep.tile([P, count, width, PACK], BF16, name="xb%d" % u, tag=tag, align_bytes=64)
+            for k in range(count):
+                rounded[u + k] = xb[:, k]
+
         def gather(u):
-            e0, e1, s = units[u]
+            e0, e1, s = UNITS[u]
             lo, hi = e0 * C, e1 * C
-            g = keep.tile([P, PACK, hi - lo], F32, name="g%d" % u, tag="g%d" % (u % 2))
+            g = gathered[u]
             for j in range(PACK):
                 cuts = [lo, C, hi] if (u, j) == (0, 0) else [lo, hi]
                 for a, b in zip(cuts, cuts[1:]):
@@ -127,20 +139,15 @@ def tile_moe_pre_mlp_gelu_kernel(
                         gate_sb[:, a:b],
                         MULT,
                     )
-            gathered[u] = g
 
         def interleave(u, copy):
-            g = gathered[u]
-            tag = HELD_BEHIND.get(u, "xb%d" % u)
-            xb = keep.tile([P, g.shape[2], PACK], BF16, name="xb%d" % u, tag=tag, align_bytes=64)
             copy(
-                xb[:].rearrange("p (c i) t -> p c t i", i=4),
-                g[:].rearrange("p t (c i) -> p c t i", i=4),
+                rounded[u].rearrange("p (c i) t -> p c t i", i=4),
+                gathered[u].rearrange("p t (c i) -> p c t i", i=4),
             )
-            rounded[u] = xb
 
         def quantise_x(u):
-            e0, e1, s = units[u]
+            e0, e1, s = UNITS[u]
             xc = keep.tile([P, (e1 - e0) * C], U32, name="xc%d" % u, tag="xc%d" % u, align_bytes=64)
             for e in range(e0, e1):
                 x_codes[e, s] = xc[:, (e - e0) * C : (e - e0 + 1) * C]
@@ -153,7 +160,7 @@ def tile_moe_pre_mlp_gelu_kernel(
                 )
 
         def first_pass(u):
-            e0, e1, s = units[u]
+            e0, e1, s = UNITS[u]
             for e in range(e0, e1):
                 if s == 0:
                     sums[e] = psum.tile([P, H], F32, name="a", tag="a%d" % (e % 3))
@@ -213,49 +220,66 @@ def tile_moe_pre_mlp_gelu_kernel(
             copy(y[c][:, e0 * C : e1 * C], acc[:])
 
         on_scalar, on_vector = nc.scalar.copy, nc.vector.tensor_copy
-        gather(0)
-        interleave(0, on_scalar)
-        gather(1)
-        interleave(1, on_scalar)
+        for u in range(2):
+            staging(u, "g%d" % u)
+            gather(u)
+            rounding(u)
+            interleave(u, on_scalar)
         quantise_x(0)
         first_pass(0)
+        staging(2, "g0")
         gather(2)
+        rounding(2)
         interleave(2, on_scalar)
         quantise_x(1)
         first_pass(1)
         for e in range(0, 3):
             activate(e)
+        staging(3, "g1")
         gather(3)
+        rounding(3)
         interleave(3, on_scalar)
         quantise_x(2)
         first_pass(2)
         for i in range(2):
             turn(i)
             weave(i, on_scalar)
+        staging(4, "g0")
         gather(4)
+        rounding(4)
         interleave(4, on_scalar)
         quantise_x(3)
         first_pass(3)
         for e in range(3, 5):
             activate(e)
+        staging(5, "g1", 2)
         gather(5)
+        gather(6)
+        rounding(5, 2)
         interleave(5, on_scalar)
+        interleave(6, on_scalar)
         quantise_x(4)
         first_pass(4)
-        gather(6)
+        staging(7, "g0")
+        gather(7)
         turn(2)
-        interleave(6, on_scalar)
+        rounding(7)
+        interleave(7, on_scalar)
         weave(2, on_scalar)
-        quantise_x(5)
-        first_pass(5)
         quantise_x(6)
         first_pass(6)
-        for e in range(5, 7):
-            activate(e)
-        gather(7)
-        interleave(7, on_vector)
+        quantise_x(5)
+        first_pass(5)
         quantise_x(7)
         first_pass(7)
+        for e in range(5, 7):
+            activate(e)
+        staging(8, "g1")
+        gather(8)
+        rounding(8)
+        interleave(8, on_vector)
+        quantise_x(8)
+        first_pass(8)
         for i in range(3, 5):
             turn(i)
             weave(i, on_vector)

@@ -24,9 +24,10 @@ MULT = mybir.AluOpType.mult
 ADD = mybir.AluOpType.add
 GELU = mybir.ActivationFunctionType.Gelu_apprx_tanh
 
-UNITS = [(0, 3, 0), (0, 3, 1), (3, 5, 0), (3, 5, 1), (5, 7, 0), (7, 8, 0), (5, 6, 1), (6, 7, 1), (7, 8, 1)]
+UNITS = [(0, 3, 0), (0, 3, 1), (3, 7, 0), (3, 5, 1), (5, 7, 1), (7, 8, 0), (7, 8, 1)]
+SPARE = 16
 TURNS = [(0, 2), (2, 3), (3, 5), (5, 6), (6, 7), (7, 8)]
-HELD_BEHIND = {3: "xc1", 4: "hb2", 5: "xc3", 7: "hb4"}
+HELD_BEHIND = {2: "xc1", 3: "hb2"}
 
 
 def tile_moe_pre_mlp_gelu_kernel(
@@ -40,7 +41,7 @@ def tile_moe_pre_mlp_gelu_kernel(
         offs_sb = keep.tile([P, SLOTS // 16], U16, name="offs_sb")
         pos_sb = [keep.tile([P, T // 16], U16, name="pos%d_sb" % r) for r in range(2)]
         planes = [
-            [keep.tile([P, T], F32, name="x_%d_%d" % (s, j), align_bytes=64) for j in range(PACK)] for s in range(PASSES)
+            [keep.tile([P, T + (0 if s else SPARE)], F32, name="x_%d_%d" % (s, j), align_bytes=64) for j in range(PACK)] for s in range(PASSES)
         ]
         gate_sb = keep.tile([P, SLOTS], F32, name="gate_sb")
         w1c = keep.tile([P, E, PASSES, 2 * H], U8, name="w1c", align_bytes=64)
@@ -53,6 +54,8 @@ def tile_moe_pre_mlp_gelu_kernel(
         ident = keep.tile([P, P], F32, name="ident")
         warm = keep.tile([P, 8], F32, name="warm")
 
+        for j in range(PACK):
+            nc.gpsimd.memset(planes[0][j][:, T:], 0.0)
         make_identity(nc, ident[:])
         nc.vector.memset(w1s[:].rearrange("p e s i -> p (e s i)").bitcast(I32), 0)
         nc.gpsimd.memset(w2s[:].rearrange("p e n -> p (e n)").bitcast(I32), 0)
@@ -84,14 +87,14 @@ def tile_moe_pre_mlp_gelu_kernel(
                 w2c[:, e0:e1].bitcast(I32), w2_words[e0:e1].rearrange("e s p b -> p (e s) b").bitcast(I32)
             )
 
-        nc.sync.dma_start(planes[0][0][:], x_rows[0, 0])
+        nc.sync.dma_start(planes[0][0][:, 0:T], x_rows[0, 0])
         nc.sync.dma_start(offs_sb[:], offs)
         nc.sync.dma_start(gate_sb[:, 0:C], gate[0:P, 0:C])
         nc.sync.dma_start(gate_sb[:, C:first], gate[0:P, C:first])
         for s in range(PASSES):
             for j in range(PACK):
                 if s or j:
-                    nc.sync.dma_start(planes[s][j][:], x_rows[s, j])
+                    nc.sync.dma_start(planes[s][j][:, 0:T], x_rows[s, j])
         nc.sync.dma_start(gate_sb[:, first:SLOTS], gate[0:P, first:SLOTS])
         load_w1_scales(0, 3)
         load_w1(0, 1)
@@ -113,18 +116,20 @@ def tile_moe_pre_mlp_gelu_kernel(
         h_turned = {}
         h_in = {}
 
-        def staging(u, tag, count=1):
-            width = (UNITS[u][1] - UNITS[u][0]) * C
-            g = keep.tile([P, count, PACK, width], F32, name="g%d" % u, tag=tag)
-            for k in range(count):
-                gathered[u + k] = g[:, k]
+        def staging(units, tag):
+            widths = [(UNITS[u][1] - UNITS[u][0]) * C * PACK for u in units]
+            g = keep.tile([P, sum(widths)], F32, name="g%d" % units[0], tag=tag, align_bytes=64)
+            for k, u in enumerate(units):
+                at = sum(widths[:k])
+                gathered[u] = g[:, at : at + widths[k]].rearrange("p (t c) -> p t c", t=PACK)
 
-        def rounding(u, count=1):
-            width = (UNITS[u][1] - UNITS[u][0]) * C
-            tag = HELD_BEHIND.get(u, "xb%d" % u)
-            xb = keep.tile([P, count, width, PACK], BF16, name="xb%d" % u, tag=tag, align_bytes=64)
-            for k in range(count):
-                rounded[u + k] = xb[:, k]
+        def rounding(units):
+            widths = [(UNITS[u][1] - UNITS[u][0]) * C for u in units]
+            tag = HELD_BEHIND.get(units[0], "xb%d" % units[0])
+            xb = keep.tile([P, sum(widths), PACK], BF16, name="xb%d" % units[0], tag=tag, align_bytes=64)
+            for k, u in enumerate(units):
+                at = sum(widths[:k])
+                rounded[u] = xb[:, at : at + widths[k], :]
 
         def gather(u):
             e0, e1, s = UNITS[u]
@@ -151,16 +156,16 @@ def tile_moe_pre_mlp_gelu_kernel(
             xc = keep.tile([P, (e1 - e0) * C], U32, name="xc%d" % u, tag="xc%d" % u, align_bytes=64)
             for e in range(e0, e1):
                 x_codes[e, s] = xc[:, (e - e0) * C : (e - e0 + 1) * C]
-            for b0 in range(e0, e1, 2):
-                lo, hi = (b0 - e0) * C, (min(b0 + 2, e1) - e0) * C
+            step = 2 if e1 - e0 == 3 else e1 - e0
+            for b0 in range(e0, e1, step):
+                lo, hi = (b0 - e0) * C, (min(b0 + step, e1) - e0) * C
                 nc.vector.quantize_mx(
                     out=xc[:, lo:hi].bitcast(FP8X4),
                     scales=xs[:, s, e0 * C + lo : e0 * C + hi],
                     in_=rounded[u][:, lo:hi, :].rearrange("p c t -> p (c t)"),
                 )
 
-        def first_pass(u):
-            e0, e1, s = UNITS[u]
+        def first_pass(e0, e1, s):
             for e in range(e0, e1):
                 if s == 0:
                     sums[e] = psum.tile([P, H], F32, name="a", tag="a%d" % (e % 3))
@@ -183,7 +188,8 @@ def tile_moe_pre_mlp_gelu_kernel(
 
         def turn(i):
             e0, e1 = TURNS[i]
-            turned = psum.tile([P, e1 - e0, 2, C], F32, name="turned", tag="turned", bufs=2)
+            tag, bufs = ("acc0", 1) if e1 == E else ("turned", 2)
+            turned = psum.tile([P, e1 - e0, 2, C], F32, name="turned", tag=tag, bufs=bufs)
             for e in range(e0, e1):
                 words = h_rows[e][:].rearrange("c u p d -> c (u p d)").bitcast(F32)
                 for u in range(2):
@@ -221,65 +227,55 @@ def tile_moe_pre_mlp_gelu_kernel(
 
         on_scalar, on_vector = nc.scalar.copy, nc.vector.tensor_copy
         for u in range(2):
-            staging(u, "g%d" % u)
+            staging([u], "g%d" % u)
             gather(u)
-            rounding(u)
+            rounding([u])
             interleave(u, on_scalar)
-        quantise_x(0)
-        first_pass(0)
-        staging(2, "g0")
+        for u in range(2):
+            quantise_x(u)
+            first_pass(0, 3, u)
+        staging([2], "g0")
         gather(2)
-        rounding(2)
-        interleave(2, on_scalar)
-        quantise_x(1)
-        first_pass(1)
         for e in range(0, 3):
             activate(e)
-        staging(3, "g1")
+        rounding([2])
+        interleave(2, on_scalar)
+        staging([3], "g1")
         gather(3)
-        rounding(3)
-        interleave(3, on_scalar)
-        quantise_x(2)
-        first_pass(2)
-        for i in range(2):
-            turn(i)
-            weave(i, on_scalar)
-        staging(4, "g0")
+        staging([4], "xb1")
         gather(4)
-        rounding(4)
+        turn(0)
+        turn(1)
+        rounding([3, 4])
+        interleave(3, on_scalar)
+        weave(0, on_scalar)
+        weave(1, on_scalar)
         interleave(4, on_scalar)
+        quantise_x(2)
+        first_pass(3, 6, 0)
         quantise_x(3)
-        first_pass(3)
-        for e in range(3, 5):
-            activate(e)
-        staging(5, "g1", 2)
+        first_pass(3, 5, 1)
+        staging([5], "g1")
         gather(5)
-        gather(6)
-        rounding(5, 2)
+        activate(3)
+        first_pass(6, 7, 0)
+        rounding([5])
         interleave(5, on_scalar)
-        interleave(6, on_scalar)
+        activate(4)
         quantise_x(4)
-        first_pass(4)
-        staging(7, "g0")
-        gather(7)
+        first_pass(5, 7, 1)
         turn(2)
-        rounding(7)
-        interleave(7, on_scalar)
         weave(2, on_scalar)
-        quantise_x(6)
-        first_pass(6)
+        activate(5)
+        activate(6)
+        staging([6], "xb1")
+        gather(6)
+        rounding([6])
+        interleave(6, on_vector)
         quantise_x(5)
-        first_pass(5)
-        quantise_x(7)
-        first_pass(7)
-        for e in range(5, 7):
-            activate(e)
-        staging(8, "g1")
-        gather(8)
-        rounding(8)
-        interleave(8, on_vector)
-        quantise_x(8)
-        first_pass(8)
+        first_pass(7, 8, 0)
+        quantise_x(6)
+        first_pass(7, 8, 1)
         for i in range(3, 5):
             turn(i)
             weave(i, on_vector)
@@ -289,9 +285,9 @@ def tile_moe_pre_mlp_gelu_kernel(
         weave(5, on_vector)
         for i in reversed(range(len(TURNS))):
             quantise_h(hk, i)
-        second_product(hk, 0, 7, 8, "acc0", on_vector)
         second_product(hk, 0, 0, 3, "acc1", on_scalar)
         second_product(hk, 0, 3, 7, "acc2", on_scalar)
+        second_product(hk, 0, 7, 8, "acc0", on_vector)
         second_product(hk, 1, 0, 4, "a1", on_scalar)
         second_product(hk, 1, 4, 8, "a2", on_scalar)
         second_product(hk, 2, 0, 4, "acc2", on_scalar)

@@ -5,12 +5,15 @@ from concourse.masks import make_identity
 
 K, T, E, C, H, N = 1024, 512, 8, 128, 512, 384
 SLOTS = E * C
-FLOPS = 2 * SLOTS * (K * H + H * N)
 P = 128
 PACK = 4
 PASSES = K // (P * PACK)
 CHUNKS = N // P
-BYTES = 4 * K * T + E * (K * H + H * N) // 2 + E * (K * H + H * N) // 32 + 4 * P * SLOTS + 2 * P * (SLOTS + 2 * T) // 16 + 4 * N * T
+LIST = 16
+FLOPS = 2 * SLOTS * (K * H + H * N)
+BYTES = (
+    4 * K * T + E * (K * H + H * N) // 2 + E * (K * H + H * N) // 32 + 4 * P * SLOTS + 2 * P * (SLOTS + 2 * T) // LIST + 4 * N * T
+)
 
 F32 = mybir.dt.float32
 BF16 = mybir.dt.bfloat16
@@ -27,7 +30,7 @@ GELU = mybir.ActivationFunctionType.Gelu_apprx_tanh
 UNITS = [(0, 3, 0), (0, 3, 1), (3, 7, 0), (3, 5, 1), (5, 7, 1), (7, 8, 0), (7, 8, 1)]
 SPARE = 16
 TURNS = [(0, 2), (2, 3), (3, 5), (5, 6), (6, 7), (7, 8)]
-HELD_BEHIND = {2: "xc1", 3: "hb2"}
+SUM_BANKS = 3
 
 
 def tile_moe_pre_mlp_gelu_kernel(
@@ -38,73 +41,69 @@ def tile_moe_pre_mlp_gelu_kernel(
         keep = ctx.enter_context(tc.tile_pool(name="keep", bufs=1))
         psum = ctx.enter_context(tc.psum_pool(name="psum", bufs=1))
 
-        offs_sb = keep.tile([P, SLOTS // 16], U16, name="offs_sb")
-        pos_sb = [keep.tile([P, T // 16], U16, name="pos%d_sb" % r) for r in range(2)]
-        planes = [
-            [keep.tile([P, T + (0 if s else SPARE)], F32, name="x_%d_%d" % (s, j), align_bytes=64) for j in range(PACK)] for s in range(PASSES)
+        offs_sb = keep.tile([P, SLOTS // LIST], U16, name="offs_sb")
+        pos_sb = [keep.tile([P, T // LIST], U16, name="pos%d_sb" % r) for r in range(2)]
+        tokens = [
+            [
+                keep.tile([P, T + (0 if s else SPARE)], F32, name="tokens_%d_%d" % (s, d), align_bytes=64)
+                for d in range(PACK)
+            ]
+            for s in range(PASSES)
         ]
         gate_sb = keep.tile([P, SLOTS], F32, name="gate_sb")
-        w1c = keep.tile([P, E, PASSES, 2 * H], U8, name="w1c", align_bytes=64)
-        w1s = keep.tile([P, E, PASSES, H], U8, name="w1s", align_bytes=64)
-        w2c = keep.tile([P, E, 2 * N], U8, name="w2c", align_bytes=64)
-        w2s = keep.tile([P, E, N], U8, name="w2s", align_bytes=64)
-        xs = keep.tile([P, PASSES, SLOTS], U8, name="xs", align_bytes=64)
-        hs = keep.tile([P, SLOTS], U8, name="hs", align_bytes=64)
+        w1_codes = keep.tile([P, E, PASSES, 2 * H], U8, name="w1_codes", align_bytes=64)
+        w1_bytes = keep.tile([P, E, PASSES, H], U8, name="w1_bytes", align_bytes=64)
+        w2_codes = keep.tile([P, E, 2 * N], U8, name="w2_codes", align_bytes=64)
+        w2_bytes = keep.tile([P, E, N], U8, name="w2_bytes", align_bytes=64)
+        x_bytes = keep.tile([P, PASSES, SLOTS], U8, name="x_bytes", align_bytes=64)
+        h_bytes = keep.tile([P, SLOTS], U8, name="h_bytes", align_bytes=64)
         y = [keep.tile([P, SLOTS], F32, name="y%d" % c) for c in range(CHUNKS)]
         ident = keep.tile([P, P], F32, name="ident")
-        warm = keep.tile([P, 8], F32, name="warm")
 
-        for j in range(PACK):
-            nc.gpsimd.memset(planes[0][j][:, T:], 0.0)
+        for d in range(PACK):
+            nc.gpsimd.memset(tokens[0][d][:, T:], 0.0)
         make_identity(nc, ident[:])
-        nc.vector.memset(w1s[:].rearrange("p e s i -> p (e s i)").bitcast(I32), 0)
-        nc.gpsimd.memset(w2s[:].rearrange("p e n -> p (e n)").bitcast(I32), 0)
-        nc.scalar.activation(warm[:], ident[:, 0:8], GELU)
-
-        x_rows = xT.rearrange("(s p j) t -> s j p t", s=PASSES, j=PACK)
-        first = UNITS[0][1] * C
+        nc.vector.memset(w1_bytes[:].rearrange("p e s i -> p (e s i)").bitcast(I32), 0)
+        nc.gpsimd.memset(w2_bytes[:].rearrange("p e n -> p (e n)").bitcast(I32), 0)
 
         def load_w1_scales(e0, e1):
             rows = w1_scales[e0:e1].rearrange("e s q i -> q (e s) i")
             for r in range(4):
                 nc.sync.dma_start(
-                    w1s[r:P:32, e0:e1].rearrange("p e s i -> p (e s) i").bitcast(I32), rows[r:16:4].bitcast(I32)
+                    w1_bytes[r:P:32, e0:e1].rearrange("p e s i -> p (e s) i").bitcast(I32), rows[r:16:4].bitcast(I32)
                 )
 
         def load_w2_scales():
             rows = w2_scales.rearrange("e s q n -> q (e s) n")
             for r in range(4):
-                nc.sync.dma_start(w2s[r:P:32].bitcast(I32), rows[r:16:4].bitcast(I32))
+                nc.sync.dma_start(w2_bytes[r:P:32].bitcast(I32), rows[r:16:4].bitcast(I32))
 
         def load_w1(e0, e1):
             nc.sync.dma_start(
-                w1c[:, e0:e1].rearrange("p e s b -> p (e s) b").bitcast(I32),
+                w1_codes[:, e0:e1].rearrange("p e s b -> p (e s) b").bitcast(I32),
                 w1_words[e0:e1].rearrange("e s p b -> p (e s) b").bitcast(I32),
             )
 
-        def load_w2(e0, e1):
-            nc.sync.dma_start(
-                w2c[:, e0:e1].bitcast(I32), w2_words[e0:e1].rearrange("e s p b -> p (e s) b").bitcast(I32)
-            )
-
-        nc.sync.dma_start(planes[0][0][:, 0:T], x_rows[0, 0])
+        x_rows = xT.rearrange("(s p d) t -> s d p t", s=PASSES, d=PACK)
+        first_slots = UNITS[0][1] * C
+        nc.sync.dma_start(tokens[0][0][:, 0:T], x_rows[0, 0])
         nc.sync.dma_start(offs_sb[:], offs)
         nc.sync.dma_start(gate_sb[:, 0:C], gate[0:P, 0:C])
-        nc.sync.dma_start(gate_sb[:, C:first], gate[0:P, C:first])
+        nc.sync.dma_start(gate_sb[:, C:first_slots], gate[0:P, C:first_slots])
         for s in range(PASSES):
-            for j in range(PACK):
-                if s or j:
-                    nc.sync.dma_start(planes[s][j][:, 0:T], x_rows[s, j])
-        nc.sync.dma_start(gate_sb[:, first:SLOTS], gate[0:P, first:SLOTS])
+            for d in range(PACK):
+                if s or d:
+                    nc.sync.dma_start(tokens[s][d][:, 0:T], x_rows[s, d])
+        nc.sync.dma_start(gate_sb[:, first_slots:SLOTS], gate[0:P, first_slots:SLOTS])
         load_w1_scales(0, 3)
         load_w1(0, 1)
         load_w1(1, 3)
-        load_w1_scales(3, 8)
+        load_w1_scales(3, E)
         load_w2_scales()
         load_w1(3, 5)
         load_w1(5, 7)
-        load_w1(7, 8)
-        load_w2(0, 8)
+        load_w1(7, E)
+        nc.sync.dma_start(w2_codes[:].bitcast(I32), w2_words.rearrange("e s p b -> p (e s) b").bitcast(I32))
         nc.sync.dma_start(pos_sb[0][:], pos1)
         nc.sync.dma_start(pos_sb[1][:], pos2)
 
@@ -114,46 +113,36 @@ def tile_moe_pre_mlp_gelu_kernel(
         sums = {}
         h_rows = {}
         h_turned = {}
-        h_in = {}
+        h_woven = {}
 
-        def staging(units, tag):
-            widths = [(UNITS[u][1] - UNITS[u][0]) * C * PACK for u in units]
-            g = keep.tile([P, sum(widths)], F32, name="g%d" % units[0], tag=tag, align_bytes=64)
-            for k, u in enumerate(units):
-                at = sum(widths[:k])
-                gathered[u] = g[:, at : at + widths[k]].rearrange("p (t c) -> p t c", t=PACK)
-
-        def rounding(units):
-            widths = [(UNITS[u][1] - UNITS[u][0]) * C for u in units]
-            tag = HELD_BEHIND.get(units[0], "xb%d" % units[0])
-            xb = keep.tile([P, sum(widths), PACK], BF16, name="xb%d" % units[0], tag=tag, align_bytes=64)
-            for k, u in enumerate(units):
-                at = sum(widths[:k])
-                rounded[u] = xb[:, at : at + widths[k], :]
-
-        def gather(u):
-            e0, e1, s = UNITS[u]
+        def gather(unit, tag):
+            e0, e1, s = UNITS[unit]
             lo, hi = e0 * C, e1 * C
-            g = gathered[u]
-            for j in range(PACK):
-                cuts = [lo, C, hi] if (u, j) == (0, 0) else [lo, hi]
+            flat = keep.tile([P, PACK * (hi - lo)], F32, name="gathered%d" % unit, tag=tag, align_bytes=64)
+            g = flat[:].rearrange("p (d c) -> p d c", d=PACK)
+            for d in range(PACK):
+                cuts = [lo, C, hi] if (unit, d) == (0, 0) else [lo, hi]
                 for a, b in zip(cuts, cuts[1:]):
                     nc.vector.tensor_tensor(
-                        g[:, j, a - lo : b - lo],
-                        planes[s][j][:].indirect(offs_sb[:, a // 16 : b // 16]),
+                        g[:, d, a - lo : b - lo],
+                        tokens[s][d][:].indirect(offs_sb[:, a // LIST : b // LIST]),
                         gate_sb[:, a:b],
                         MULT,
                     )
+            gathered[unit] = g
 
-        def interleave(u, copy):
+        def interleave(unit, tag, copy):
+            e0, e1, s = UNITS[unit]
+            xb = keep.tile([P, (e1 - e0) * C, PACK], BF16, name="rounded%d" % unit, tag=tag, align_bytes=64)
             copy(
-                rounded[u].rearrange("p (c i) t -> p c t i", i=4),
-                gathered[u].rearrange("p t (c i) -> p c t i", i=4),
+                xb[:].rearrange("p (c i) d -> p c d i", i=4),
+                gathered[unit].rearrange("p d (c i) -> p c d i", i=4),
             )
+            rounded[unit] = xb
 
-        def quantise_x(u):
-            e0, e1, s = UNITS[u]
-            xc = keep.tile([P, (e1 - e0) * C], U32, name="xc%d" % u, tag="xc%d" % u, align_bytes=64)
+        def quantise_x(unit):
+            e0, e1, s = UNITS[unit]
+            xc = keep.tile([P, (e1 - e0) * C], U32, name="codes%d" % unit, align_bytes=64)
             for e in range(e0, e1):
                 x_codes[e, s] = xc[:, (e - e0) * C : (e - e0 + 1) * C]
             step = 2 if e1 - e0 == 3 else e1 - e0
@@ -161,106 +150,100 @@ def tile_moe_pre_mlp_gelu_kernel(
                 lo, hi = (b0 - e0) * C, (min(b0 + step, e1) - e0) * C
                 nc.vector.quantize_mx(
                     out=xc[:, lo:hi].bitcast(FP8X4),
-                    scales=xs[:, s, e0 * C + lo : e0 * C + hi],
-                    in_=rounded[u][:, lo:hi, :].rearrange("p c t -> p (c t)"),
+                    scales=x_bytes[:, s, e0 * C + lo : e0 * C + hi],
+                    in_=rounded[unit][:, lo:hi, :].rearrange("p c d -> p (c d)"),
                 )
 
         def first_pass(e0, e1, s):
             for e in range(e0, e1):
                 if s == 0:
-                    sums[e] = psum.tile([P, H], F32, name="a", tag="a%d" % (e % 3))
+                    sums[e] = psum.tile([P, H], F32, name="sums", tag="sums%d" % (e % SUM_BANKS))
                 nc.tensor.matmul_mx(
                     out=sums[e][:],
                     lhsT=x_codes[e, s].bitcast(FP8X4),
-                    lhsT_scale=xs[:, s, e * C : (e + 1) * C],
-                    rhs=w1c[:, e, s, :].bitcast(FP4X4),
-                    rhs_scale=w1s[:, e, s, :],
+                    lhsT_scale=x_bytes[:, s, e * C : (e + 1) * C],
+                    rhs=w1_codes[:, e, s, :].bitcast(FP4X4),
+                    rhs_scale=w1_bytes[:, e, s, :],
                     start=(s == 0),
                     stop=(s == PASSES - 1),
                 )
 
-        def activate(e, halves=1):
-            hb = keep.tile([P, 2, P, 2], BF16, name="hb%d" % e, align_bytes=64)
-            pairs = sums[e][:].rearrange("c (p u d) -> c u p d", u=2, d=2)
-            for u in range(0, 2, 2 // halves):
-                nc.scalar.activation(hb[:, u : u + 2 // halves], pairs[:, u : u + 2 // halves], GELU)
+        def activate(e, calls=1):
+            hb = keep.tile([P, 2, P, 2], BF16, name="h_rows%d" % e, align_bytes=64)
+            pairs = sums[e][:].rearrange("c (p u v) -> c u p v", u=2, v=2)
+            for u in range(0, 2, 2 // calls):
+                nc.scalar.activation(hb[:, u : u + 2 // calls], pairs[:, u : u + 2 // calls], GELU)
             h_rows[e] = hb
 
         def turn(i):
             e0, e1 = TURNS[i]
-            tag, bufs = ("acc0", 1) if e1 == E else ("turned", 2)
+            tag, bufs = ("y_last", 1) if e1 == E else ("turned", 2)
             turned = psum.tile([P, e1 - e0, 2, C], F32, name="turned", tag=tag, bufs=bufs)
             for e in range(e0, e1):
-                words = h_rows[e][:].rearrange("c u p d -> c (u p d)").bitcast(F32)
+                words = h_rows[e][:].rearrange("c u p v -> c (u p v)").bitcast(F32)
                 for u in range(2):
                     nc.tensor.transpose(turned[:, e - e0, u, :], words[:, u * P : (u + 1) * P], ident[:])
             h_turned[i] = turned
 
         def weave(i, copy):
             e0, e1 = TURNS[i]
-            turned = h_turned[i]
-            hq = keep.tile([P, (e1 - e0) * C * PACK], BF16, name="hq%d" % i, align_bytes=64)
+            hq = keep.tile([P, (e1 - e0) * C * PACK], BF16, name="h_woven%d" % i, align_bytes=64)
             copy(
                 hq[:].bitcast(F32).rearrange("p (e c u) -> p e c u", u=2, c=C),
-                turned[:].rearrange("p e u c -> p e c u"),
+                h_turned[i][:].rearrange("p e u c -> p e c u"),
             )
-            h_in[i] = hq
+            h_woven[i] = hq
 
-        def quantise_h(hk, i):
+        def quantise_h(h_codes, i):
             cols = slice(TURNS[i][0] * C, TURNS[i][1] * C)
-            nc.vector.quantize_mx(out=hk[:, cols].bitcast(FP8X4), scales=hs[:, cols], in_=h_in[i][:])
+            nc.vector.quantize_mx(out=h_codes[:, cols].bitcast(FP8X4), scales=h_bytes[:, cols], in_=h_woven[i][:])
 
-        def second_product(hk, c, e0, e1, tag, copy):
+        def second_product(h_codes, chunk, e0, e1, tag, copy):
             acc = psum.tile([P, (e1 - e0) * C], F32, name="acc", tag=tag)
             for e in range(e0, e1):
                 cols = slice(e * C, (e + 1) * C)
                 nc.tensor.matmul_mx(
                     out=acc[:, (e - e0) * C : (e - e0 + 1) * C],
-                    lhsT=w2c[:, e, 2 * P * c : 2 * P * (c + 1)].bitcast(FP4X4),
-                    lhsT_scale=w2s[:, e, P * c : P * (c + 1)],
-                    rhs=hk[:, cols].bitcast(FP8X4),
-                    rhs_scale=hs[:, cols],
+                    lhsT=w2_codes[:, e, 2 * P * chunk : 2 * P * (chunk + 1)].bitcast(FP4X4),
+                    lhsT_scale=w2_bytes[:, e, P * chunk : P * (chunk + 1)],
+                    rhs=h_codes[:, cols].bitcast(FP8X4),
+                    rhs_scale=h_bytes[:, cols],
                     start=True,
                     stop=True,
                 )
-            copy(y[c][:, e0 * C : e1 * C], acc[:])
+            copy(y[chunk][:, e0 * C : e1 * C], acc[:])
 
         on_scalar, on_vector = nc.scalar.copy, nc.vector.tensor_copy
-        for u in range(2):
-            staging([u], "g%d" % u)
-            gather(u)
-            rounding([u])
-            interleave(u, on_scalar)
-        for u in range(2):
-            quantise_x(u)
-            first_pass(0, 3, u)
-        staging([2], "g0")
-        gather(2)
-        for e in range(0, 3):
+
+        for unit in range(2):
+            gather(unit, "gathered%d" % unit)
+            interleave(unit, "rounded%d" % unit, on_scalar)
+        for unit in range(2):
+            quantise_x(unit)
+            first_pass(0, 3, unit)
+
+        gather(2, "gathered0")
+        for e in range(3):
             activate(e)
-        rounding([2])
-        interleave(2, on_scalar)
-        staging([3], "g1")
-        gather(3)
-        staging([4], "xb1")
-        gather(4)
+        interleave(2, "codes1", on_scalar)
+
+        gather(3, "gathered1")
+        gather(4, "rounded1")
         turn(0)
         turn(1)
-        rounding([3, 4])
-        interleave(3, on_scalar)
+        interleave(3, "h_rows2", on_scalar)
         weave(0, on_scalar)
         weave(1, on_scalar)
-        interleave(4, on_scalar)
+        interleave(4, "h_rows1", on_scalar)
         quantise_x(2)
         first_pass(3, 6, 0)
         quantise_x(3)
         first_pass(3, 5, 1)
-        staging([5], "g1")
-        gather(5)
+
+        gather(5, "gathered1")
         activate(3)
         first_pass(6, 7, 0)
-        rounding([5])
-        interleave(5, on_scalar)
+        interleave(5, "rounded5", on_scalar)
         activate(4)
         quantise_x(4)
         first_pass(5, 7, 1)
@@ -268,43 +251,42 @@ def tile_moe_pre_mlp_gelu_kernel(
         weave(2, on_scalar)
         activate(5)
         activate(6)
-        staging([6], "xb1")
-        gather(6)
-        rounding([6])
-        interleave(6, on_vector)
+
+        gather(6, "rounded1")
+        interleave(6, "rounded6", on_vector)
         quantise_x(5)
-        first_pass(7, 8, 0)
+        first_pass(7, E, 0)
         quantise_x(6)
-        first_pass(7, 8, 1)
-        for i in range(3, 5):
+        first_pass(7, E, 1)
+        for i in (3, 4):
             turn(i)
             weave(i, on_vector)
-        activate(7, 2)
-        hk = keep.tile([P, SLOTS], U32, name="hk", tag="x_1_3", align_bytes=64)
+        activate(7, calls=2)
+        h_codes = keep.tile([P, SLOTS], U32, name="h_codes", tag="tokens_1_3", align_bytes=64)
         turn(5)
         weave(5, on_vector)
         for i in reversed(range(len(TURNS))):
-            quantise_h(hk, i)
-        second_product(hk, 0, 0, 3, "acc1", on_scalar)
-        second_product(hk, 0, 3, 7, "acc2", on_scalar)
-        second_product(hk, 0, 7, 8, "acc0", on_vector)
-        second_product(hk, 1, 0, 4, "a1", on_scalar)
-        second_product(hk, 1, 4, 8, "a2", on_scalar)
-        second_product(hk, 2, 0, 4, "acc2", on_scalar)
-        second_product(hk, 2, 4, 8, "a0", on_scalar)
+            quantise_h(h_codes, i)
+
+        second_product(h_codes, 0, 0, 3, "y_first", on_scalar)
+        second_product(h_codes, 0, 3, 7, "y_middle", on_scalar)
+        second_product(h_codes, 0, 7, E, "y_last", on_vector)
+        second_product(h_codes, 1, 0, 4, "sums1", on_scalar)
+        second_product(h_codes, 1, 4, E, "sums2", on_scalar)
+        second_product(h_codes, 2, 0, 4, "y_middle", on_scalar)
+        second_product(h_codes, 2, 4, E, "sums0", on_scalar)
 
         half = T // 2
-        for c in range(CHUNKS):
-            picked = keep.tile([P, T], F32, name="picked%d" % c)
-            summed = keep.tile([P, T], F32, name="summed%d" % c)
-            for h in range(2):
-                cols = slice(h * half, (h + 1) * half)
+        for chunk in range(CHUNKS):
+            picked = keep.tile([P, T], F32, name="picked%d" % chunk)
+            summed = keep.tile([P, T], F32, name="summed%d" % chunk)
+            for a in (0, half):
                 nc.vector.tensor_copy(
-                    picked[:, cols], y[c][:].indirect(pos_sb[0][:, h * half // 16 : (h + 1) * half // 16])
+                    picked[:, a : a + half], y[chunk][:].indirect(pos_sb[0][:, a // LIST : (a + half) // LIST])
                 )
-            cuts = [0, half, T - P, T] if c == CHUNKS - 1 else [0, half, T]
+            cuts = [0, half, T - T // 4, T] if chunk == CHUNKS - 1 else [0, half, T]
             for a, b in zip(cuts, cuts[1:]):
                 nc.vector.tensor_tensor(
-                    summed[:, a:b], y[c][:].indirect(pos_sb[1][:, a // 16 : b // 16]), picked[:, a:b], ADD
+                    summed[:, a:b], y[chunk][:].indirect(pos_sb[1][:, a // LIST : b // LIST]), picked[:, a:b], ADD
                 )
-                nc.sync.dma_start(out[c * P : (c + 1) * P, a:b], summed[:, a:b])
+                nc.sync.dma_start(out[chunk * P : (chunk + 1) * P, a:b], summed[:, a:b])

@@ -274,19 +274,25 @@ def tile_moe_pre_mlp_gelu_kernel(
         second_product(h_codes, 1, 0, 4, "sums1", on_scalar)
         second_product(h_codes, 1, 4, E, "sums2", on_scalar)
         second_product(h_codes, 2, 0, 4, "y_middle", on_scalar)
-        second_product(h_codes, 2, 4, E, "sums0", on_scalar)
+        second_product(h_codes, 2, 4, E, "sums2", on_scalar)
 
-        half = T // 2
-        for chunk in range(CHUNKS):
-            picked = keep.tile([P, T], F32, name="picked%d" % chunk)
-            summed = keep.tile([P, T], F32, name="summed%d" % chunk)
-            for a in (0, half):
-                nc.vector.tensor_copy(
-                    picked[:, a : a + half], y[chunk][:].indirect(pos_sb[0][:, a // LIST : (a + half) // LIST])
-                )
-            cuts = [0, half, T - T // 4, T] if chunk == CHUNKS - 1 else [0, half, T]
+        picked = [keep.tile([P, T], F32, name="picked%d" % c) for c in range(CHUNKS)]
+
+        def pick(chunk, cuts):
+            for a, b in zip(cuts, cuts[1:]):
+                nc.vector.tensor_copy(picked[chunk][:, a:b], y[chunk][:].indirect(pos_sb[0][:, a // LIST : b // LIST]))
+
+        def combine(chunk, cuts, tag):
+            summed = keep.tile([P, T], F32, name="summed%d" % chunk, tag=tag, align_bytes=64)
             for a, b in zip(cuts, cuts[1:]):
                 nc.vector.tensor_tensor(
-                    summed[:, a:b], y[chunk][:].indirect(pos_sb[1][:, a // LIST : b // LIST]), picked[:, a:b], ADD
+                    summed[:, a:b], y[chunk][:].indirect(pos_sb[1][:, a // LIST : b // LIST]), picked[chunk][:, a:b], ADD
                 )
                 nc.sync.dma_start(out[chunk * P : (chunk + 1) * P, a:b], summed[:, a:b])
+
+        pick(0, [0, T])
+        pick(1, [0, T])
+        combine(0, [0, T], "w2_codes")
+        combine(1, [0, T], "summed1")
+        pick(2, [0, T - T // 4, T])
+        combine(2, [0, T - T // 4, T], "summed2")

@@ -274,7 +274,7 @@ def tile_moe_pre_mlp_gelu_kernel(
         second_product(h_codes, 1, 0, 4, "sums1", on_scalar)
         second_product(h_codes, 1, 4, E, "sums2", on_scalar)
         second_product(h_codes, 2, 0, 4, "y_middle", on_scalar)
-        second_product(h_codes, 2, 4, E, "sums2", on_scalar)
+        second_product(h_codes, 2, 4, E, "sums0", on_scalar)
 
         picked = [keep.tile([P, T], F32, name="picked%d" % c) for c in range(CHUNKS)]
 
@@ -283,16 +283,22 @@ def tile_moe_pre_mlp_gelu_kernel(
                 nc.vector.tensor_copy(picked[chunk][:, a:b], y[chunk][:].indirect(pos_sb[0][:, a // LIST : b // LIST]))
 
         def combine(chunk, cuts, tag):
-            summed = keep.tile([P, T], F32, name="summed%d" % chunk, tag=tag, align_bytes=64)
+            lo, hi = cuts[0], cuts[-1]
+            summed = keep.tile([P, hi - lo], F32, name="summed", tag=tag)
             for a, b in zip(cuts, cuts[1:]):
                 nc.vector.tensor_tensor(
-                    summed[:, a:b], y[chunk][:].indirect(pos_sb[1][:, a // LIST : b // LIST]), picked[chunk][:, a:b], ADD
+                    summed[:, a - lo : b - lo],
+                    y[chunk][:].indirect(pos_sb[1][:, a // LIST : b // LIST]),
+                    picked[chunk][:, a:b],
+                    ADD,
                 )
-                nc.sync.dma_start(out[chunk * P : (chunk + 1) * P, a:b], summed[:, a:b])
+                nc.sync.dma_start(out[chunk * P : (chunk + 1) * P, a:b], summed[:, a - lo : b - lo])
 
-        pick(0, [0, T])
+        half = T // 2
+        pick(0, [0, half, T])
+        combine(0, [0, half], "summed_first")
+        combine(0, [half, T], "summed_second")
         pick(1, [0, T])
-        combine(0, [0, T], "w2_codes")
-        combine(1, [0, T], "summed1")
-        pick(2, [0, T - T // 4, T])
-        combine(2, [0, T - T // 4, T], "summed2")
+        pick(2, [0, T])
+        combine(1, [0, T], "summed_first")
+        combine(2, [0, half, T - T // 4, T], "summed_second")

@@ -236,15 +236,17 @@ def tile_moe_pre_mlp_gelu_kernel(
         weave(1, on_scalar)
         interleave(4, "h_rows1", on_scalar)
         quantise_x(2)
-        first_pass(3, 6, 0)
         quantise_x(3)
-        first_pass(3, 5, 1)
+        for e in (3, 4):
+            first_pass(e, e + 1, 0)
+            first_pass(e, e + 1, 1)
+        first_pass(5, 6, 0)
 
         gather(5, "gathered1")
         activate(3)
         first_pass(6, 7, 0)
-        interleave(5, "rounded5", on_scalar)
         activate(4)
+        interleave(5, "codes3", on_scalar)
         quantise_x(4)
         first_pass(5, 7, 1)
         turn(2)
@@ -253,7 +255,7 @@ def tile_moe_pre_mlp_gelu_kernel(
         activate(6)
 
         gather(6, "rounded1")
-        interleave(6, "rounded6", on_vector)
+        interleave(6, "gathered1", on_vector)
         quantise_x(5)
         first_pass(7, E, 0)
         quantise_x(6)
@@ -262,18 +264,18 @@ def tile_moe_pre_mlp_gelu_kernel(
             turn(i)
             weave(i, on_vector)
         activate(7, calls=2)
-        h_codes = keep.tile([P, SLOTS], U32, name="h_codes", tag="tokens_1_3", align_bytes=64)
+        h_codes = keep.tile([P, SLOTS], U32, name="h_codes", tag="gathered1", align_bytes=64)
         turn(5)
         weave(5, on_vector)
-        for i in reversed(range(len(TURNS))):
+        for i in (3, 4, 5, 2, 1, 0):
             quantise_h(h_codes, i)
 
         second_product(h_codes, 0, 0, 3, "y_first", on_scalar)
-        second_product(h_codes, 0, 3, 7, "y_middle", on_scalar)
-        second_product(h_codes, 0, 7, E, "y_last", on_vector)
-        second_product(h_codes, 1, 0, 4, "sums1", on_scalar)
+        second_product(h_codes, 0, 3, 6, "y_middle", on_scalar)
+        second_product(h_codes, 0, 6, E, "y_last", on_scalar)
+        second_product(h_codes, 1, 0, 4, "y_last", on_scalar)
         second_product(h_codes, 1, 4, E, "sums2", on_scalar)
-        second_product(h_codes, 2, 0, 4, "y_middle", on_scalar)
+        second_product(h_codes, 2, 0, 4, "sums2", on_scalar)
         second_product(h_codes, 2, 4, E, "sums0", on_scalar)
 
         picked = [keep.tile([P, T], F32, name="picked%d" % c) for c in range(CHUNKS)]

@@ -27,7 +27,7 @@ MULT = mybir.AluOpType.mult
 ADD = mybir.AluOpType.add
 GELU = mybir.ActivationFunctionType.Gelu_apprx_tanh
 
-UNITS = [(0, 3, 0), (0, 3, 1), (3, 7, 0), (3, 5, 1), (5, 7, 1), (7, 8, 0), (7, 8, 1)]
+UNITS = [(0, 3, 0), (0, 3, 1), (3, 5, 1), (3, 7, 0), (5, 7, 1), (7, 8, 0), (7, 8, 1)]
 SPARE = 16
 TURNS = [(0, 2), (2, 3), (3, 5), (5, 6), (6, 7), (7, 8)]
 SUM_BANKS = 3
@@ -142,21 +142,21 @@ def tile_moe_pre_mlp_gelu_kernel(
 
         def quantise_x(unit):
             e0, e1, s = UNITS[unit]
-            xc = keep.tile([P, (e1 - e0) * C], U32, name="codes%d" % unit, align_bytes=64)
-            for e in range(e0, e1):
-                x_codes[e, s] = xc[:, (e - e0) * C : (e - e0 + 1) * C]
-            step = 2 if e1 - e0 == 3 else e1 - e0
-            for b0 in range(e0, e1, step):
-                lo, hi = (b0 - e0) * C, (min(b0 + step, e1) - e0) * C
+            for b0 in range(e0, e1, 2):
+                b1 = min(b0 + 2, e1)
+                xc = keep.tile([P, (b1 - b0) * C], U32, name="codes%d_%d" % (unit, b0), align_bytes=64)
+                for e in range(b0, b1):
+                    x_codes[e, s] = xc[:, (e - b0) * C : (e - b0 + 1) * C]
                 nc.vector.quantize_mx(
-                    out=xc[:, lo:hi].bitcast(FP8X4),
-                    scales=x_bytes[:, s, e0 * C + lo : e0 * C + hi],
-                    in_=rounded[unit][:, lo:hi, :].rearrange("p c d -> p (c d)"),
+                    out=xc[:].bitcast(FP8X4),
+                    scales=x_bytes[:, s, b0 * C : b1 * C],
+                    in_=rounded[unit][:, (b0 - e0) * C : (b1 - e0) * C, :].rearrange("p c d -> p (c d)"),
                 )
 
         def first_pass(e0, e1, s):
             for e in range(e0, e1):
-                if s == 0:
+                opens = e not in sums
+                if opens:
                     sums[e] = psum.tile([P, H], F32, name="sums", tag="sums%d" % (e % SUM_BANKS))
                 nc.tensor.matmul_mx(
                     out=sums[e][:],
@@ -164,8 +164,8 @@ def tile_moe_pre_mlp_gelu_kernel(
                     lhsT_scale=x_bytes[:, s, e * C : (e + 1) * C],
                     rhs=w1_codes[:, e, s, :].bitcast(FP4X4),
                     rhs_scale=w1_bytes[:, e, s, :],
-                    start=(s == 0),
-                    stop=(s == PASSES - 1),
+                    start=opens,
+                    stop=not opens,
                 )
 
         def activate(e, calls=1):
@@ -218,44 +218,39 @@ def tile_moe_pre_mlp_gelu_kernel(
         for unit in range(2):
             gather(unit, "gathered%d" % unit)
             interleave(unit, "rounded%d" % unit, on_scalar)
-        for unit in range(2):
-            quantise_x(unit)
-            first_pass(0, 3, unit)
-
-        gather(2, "gathered0")
+        quantise_x(0)
+        first_pass(0, 3, 0)
+        gather(2, "rounded0")
+        quantise_x(1)
+        first_pass(0, 3, 1)
+        gather(3, "rounded1")
         for e in range(3):
             activate(e)
-        interleave(2, "codes1", on_scalar)
-
-        gather(3, "gathered1")
-        gather(4, "rounded1")
+        interleave(2, "codes1_2", on_scalar)
         turn(0)
         turn(1)
-        interleave(3, "h_rows2", on_scalar)
         weave(0, on_scalar)
         weave(1, on_scalar)
-        interleave(4, "h_rows1", on_scalar)
+        interleave(3, "h_rows2", on_scalar)
         quantise_x(2)
+        first_pass(3, 5, 1)
+        gather(4, "codes1_2")
+        interleave(4, "rounded4", on_scalar)
         quantise_x(3)
-        for e in (3, 4):
-            first_pass(e, e + 1, 0)
-            first_pass(e, e + 1, 1)
-        first_pass(5, 6, 0)
-
-        gather(5, "gathered1")
+        first_pass(3, 6, 0)
+        gather(5, "h_rows2")
         activate(3)
         first_pass(6, 7, 0)
         activate(4)
-        interleave(5, "codes3", on_scalar)
+        interleave(5, "codes3_3", on_scalar)
         quantise_x(4)
         first_pass(5, 7, 1)
         turn(2)
         weave(2, on_scalar)
         activate(5)
         activate(6)
-
-        gather(6, "rounded1")
-        interleave(6, "gathered1", on_vector)
+        gather(6, "rounded4")
+        interleave(6, "h_rows2", on_vector)
         quantise_x(5)
         first_pass(7, E, 0)
         quantise_x(6)
@@ -264,7 +259,7 @@ def tile_moe_pre_mlp_gelu_kernel(
             turn(i)
             weave(i, on_vector)
         activate(7, calls=2)
-        h_codes = keep.tile([P, SLOTS], U32, name="h_codes", tag="gathered1", align_bytes=64)
+        h_codes = keep.tile([P, SLOTS], U32, name="h_codes", tag="h_rows2", align_bytes=64)
         turn(5)
         weave(5, on_vector)
         for i in (3, 4, 5, 2, 1, 0):

@@ -220,10 +220,10 @@ def tile_moe_pre_mlp_gelu_kernel(
             interleave(unit, "rounded%d" % unit, on_scalar)
         quantise_x(0)
         first_pass(0, 3, 0)
-        gather(2, "rounded0")
+        gather(2, "gathered0")
         quantise_x(1)
         first_pass(0, 3, 1)
-        gather(3, "rounded1")
+        gather(3, "gathered1")
         for e in range(3):
             activate(e)
         interleave(2, "codes1_2", on_scalar)
@@ -234,11 +234,11 @@ def tile_moe_pre_mlp_gelu_kernel(
         interleave(3, "h_rows2", on_scalar)
         quantise_x(2)
         first_pass(3, 5, 1)
-        gather(4, "codes1_2")
+        gather(4, "gathered0")
         interleave(4, "rounded4", on_scalar)
         quantise_x(3)
         first_pass(3, 6, 0)
-        gather(5, "h_rows2")
+        gather(5, "gathered1")
         activate(3)
         first_pass(6, 7, 0)
         activate(4)
@@ -249,8 +249,8 @@ def tile_moe_pre_mlp_gelu_kernel(
         weave(2, on_scalar)
         activate(5)
         activate(6)
-        gather(6, "rounded4")
-        interleave(6, "h_rows2", on_vector)
+        gather(6, "gathered0")
+        interleave(6, "gathered1", on_vector)
         quantise_x(5)
         first_pass(7, E, 0)
         quantise_x(6)
@@ -259,7 +259,7 @@ def tile_moe_pre_mlp_gelu_kernel(
             turn(i)
             weave(i, on_vector)
         activate(7, calls=2)
-        h_codes = keep.tile([P, SLOTS], U32, name="h_codes", tag="h_rows2", align_bytes=64)
+        h_codes = keep.tile([P, SLOTS], U32, name="h_codes", tag="gathered0", align_bytes=64)
         turn(5)
         weave(5, on_vector)
         for i in (3, 4, 5, 2, 1, 0):

@@ -30,6 +30,7 @@ GELU = mybir.ActivationFunctionType.Gelu_apprx_tanh
 UNITS = [(0, 3, 0), (0, 3, 1), (3, 5, 1), (3, 7, 0), (5, 7, 1), (7, 8, 0), (7, 8, 1)]
 SPARE = 16
 TURNS = [(0, 2), (2, 3), (3, 5), (5, 6), (6, 7), (7, 8)]
+LAST = E - 1
 SUM_BANKS = 3
 
 
@@ -51,8 +52,12 @@ def tile_moe_pre_mlp_gelu_kernel(
             for s in range(PASSES)
         ]
         gate_sb = keep.tile([P, SLOTS], F32, name="gate_sb")
-        w1_codes = keep.tile([P, E, PASSES, 2 * H], U8, name="w1_codes", align_bytes=64)
-        w1_bytes = keep.tile([P, E, PASSES, H], U8, name="w1_bytes", align_bytes=64)
+        w1_codes = keep.tile([P, LAST, PASSES, 2 * H], U8, name="w1_codes", align_bytes=64)
+        w1_bytes = keep.tile([P, LAST, PASSES, H], U8, name="w1_bytes", align_bytes=64)
+        last_codes_in = keep.tile([P, PASSES, 2 * H], U8, name="last_codes_in", align_bytes=64)
+        last_bytes_in = keep.tile([P, PASSES, H], U8, name="last_bytes_in", align_bytes=64)
+        last_codes = keep.tile([P, PASSES, PACK, 2 * P], U8, name="last_codes", align_bytes=64)
+        last_bytes = keep.tile([P, PASSES, PACK, P], U8, name="last_bytes", align_bytes=64)
         w2_codes = keep.tile([P, E, 2 * N], U8, name="w2_codes", align_bytes=64)
         w2_bytes = keep.tile([P, E, N], U8, name="w2_bytes", align_bytes=64)
         x_bytes = keep.tile([P, PASSES, SLOTS], U8, name="x_bytes", align_bytes=64)
@@ -60,6 +65,7 @@ def tile_moe_pre_mlp_gelu_kernel(
         y = [keep.tile([P, SLOTS], F32, name="y%d" % c) for c in range(CHUNKS)]
         ident = keep.tile([P, P], F32, name="ident")
 
+        nc.gpsimd.memset(last_bytes_in[:].rearrange("p s i -> p (s i)").bitcast(I32), 0)
         for d in range(PACK):
             nc.gpsimd.memset(tokens[0][d][:, T:], 0.0)
         make_identity(nc, ident[:])
@@ -94,15 +100,19 @@ def tile_moe_pre_mlp_gelu_kernel(
             for d in range(PACK):
                 if s or d:
                     nc.sync.dma_start(tokens[s][d][:, 0:T], x_rows[s, d])
+            if s == 0:
+                nc.sync.dma_start(last_codes_in[:].bitcast(I32), w1_words[LAST].rearrange("s p b -> p s b").bitcast(I32))
         nc.sync.dma_start(gate_sb[:, first_slots:SLOTS], gate[0:P, first_slots:SLOTS])
         load_w1_scales(0, 3)
         load_w1(0, 1)
         load_w1(1, 3)
-        load_w1_scales(3, E)
+        load_w1_scales(3, LAST)
+        last_rows = w1_scales[LAST].rearrange("s q i -> q s i")
+        for r in range(4):
+            nc.sync.dma_start(last_bytes_in[r:P:32].bitcast(I32), last_rows[r:16:4].bitcast(I32))
         load_w2_scales()
         load_w1(3, 5)
         load_w1(5, 7)
-        load_w1(7, E)
         nc.sync.dma_start(w2_codes[:].bitcast(I32), w2_words.rearrange("e s p b -> p (e s) b").bitcast(I32))
         nc.sync.dma_start(pos_sb[0][:], pos1)
         nc.sync.dma_start(pos_sb[1][:], pos2)
@@ -166,6 +176,20 @@ def tile_moe_pre_mlp_gelu_kernel(
                     rhs_scale=w1_bytes[:, e, s, :],
                     start=opens,
                     stop=not opens,
+                )
+
+        def last_pass(s):
+            if s == 0:
+                sums[LAST] = psum.tile([P, PACK, C], F32, name="sums", tag="sums%d" % ((LAST - 1) % SUM_BANKS))
+            for d in range(PACK):
+                nc.tensor.matmul_mx(
+                    out=sums[LAST][:, d, :],
+                    lhsT=last_codes[:, s, d, :].bitcast(FP4X4),
+                    lhsT_scale=last_bytes[:, s, d, :],
+                    rhs=x_codes[LAST, s].bitcast(FP8X4),
+                    rhs_scale=x_bytes[:, s, LAST * C : E * C],
+                    start=(s, d) == (0, 0),
+                    stop=(s, d) == (PASSES - 1, PACK - 1),
                 )
 
         def activate(e, calls=1):
@@ -232,6 +256,10 @@ def tile_moe_pre_mlp_gelu_kernel(
         weave(0, on_scalar)
         weave(1, on_scalar)
         interleave(3, "h_rows2", on_scalar)
+        nc.scalar.copy(
+            last_codes[:].bitcast(U16), last_codes_in[:].bitcast(U16).rearrange("p s (m d) -> p s d m", d=PACK)
+        )
+        nc.vector.tensor_copy(last_bytes[:], last_bytes_in[:].rearrange("p s (m d) -> p s d m", d=PACK))
         quantise_x(2)
         first_pass(3, 5, 1)
         gather(4, "gathered0")
@@ -250,23 +278,24 @@ def tile_moe_pre_mlp_gelu_kernel(
         activate(5)
         activate(6)
         gather(6, "gathered0")
-        interleave(6, "gathered1", on_vector)
-        quantise_x(5)
-        first_pass(7, E, 0)
-        quantise_x(6)
-        first_pass(7, E, 1)
         for i in (3, 4):
             turn(i)
-            weave(i, on_vector)
-        activate(7, calls=2)
+            weave(i, on_scalar)
+        quantise_x(5)
+        last_pass(0)
+        interleave(6, "gathered1", on_vector)
+        quantise_x(6)
+        last_pass(1)
+        h_woven[5] = keep.tile([P, C * PACK], BF16, name="h_woven5", align_bytes=64)
+        nc.scalar.activation(
+            h_woven[5][:].rearrange("p (c d) -> p c d", d=PACK), sums[LAST][:].rearrange("p d c -> p c d"), GELU
+        )
         h_codes = keep.tile([P, SLOTS], U32, name="h_codes", tag="gathered0", align_bytes=64)
-        turn(5)
-        weave(5, on_vector)
-        for i in (3, 4, 5, 2, 1, 0):
+        for i in range(len(TURNS)):
             quantise_h(h_codes, i)
 
         second_product(h_codes, 0, 0, 3, "y_first", on_scalar)
-        second_product(h_codes, 0, 3, 6, "y_middle", on_scalar)
+        second_product(h_codes, 0, 3, 6, "y_middle", on_vector)
         second_product(h_codes, 0, 6, E, "y_last", on_scalar)
         second_product(h_codes, 1, 0, 4, "y_last", on_scalar)
         second_product(h_codes, 1, 4, E, "sums2", on_scalar)

@@ -57,7 +57,7 @@ def tile_moe_pre_mlp_gelu_kernel(
         last_codes_in = keep.tile([P, PASSES, 2 * H], U8, name="last_codes_in", align_bytes=64)
         last_bytes_in = keep.tile([P, PASSES, H], U8, name="last_bytes_in", align_bytes=64)
         last_codes = keep.tile([P, PASSES, PACK, 2 * P], U8, name="last_codes", align_bytes=64)
-        last_bytes = keep.tile([P, PASSES, PACK, P], U8, name="last_bytes", align_bytes=64)
+        last_bytes = {}
         w2_codes = keep.tile([P, E, 2 * N], U8, name="w2_codes", align_bytes=64)
         w2_bytes = keep.tile([P, E, N], U8, name="w2_bytes", align_bytes=64)
         x_bytes = keep.tile([P, PASSES, SLOTS], U8, name="x_bytes", align_bytes=64)
@@ -178,6 +178,10 @@ def tile_moe_pre_mlp_gelu_kernel(
                     stop=not opens,
                 )
 
+        def permute_scales(s, tag):
+            last_bytes[s] = keep.tile([P, PACK, P], U8, name="last_bytes", tag=tag, align_bytes=64)
+            nc.vector.tensor_copy(last_bytes[s][:], last_bytes_in[:, s].rearrange("p (m d) -> p d m", d=PACK))
+
         def last_pass(s):
             if s == 0:
                 sums[LAST] = psum.tile([P, PACK, C], F32, name="sums", tag="sums%d" % ((LAST - 1) % SUM_BANKS))
@@ -185,7 +189,7 @@ def tile_moe_pre_mlp_gelu_kernel(
                 nc.tensor.matmul_mx(
                     out=sums[LAST][:, d, :],
                     lhsT=last_codes[:, s, d, :].bitcast(FP4X4),
-                    lhsT_scale=last_bytes[:, s, d, :],
+                    lhsT_scale=last_bytes[s][:, d, :],
                     rhs=x_codes[LAST, s].bitcast(FP8X4),
                     rhs_scale=x_bytes[:, s, LAST * C : E * C],
                     start=(s, d) == (0, 0),
@@ -201,7 +205,7 @@ def tile_moe_pre_mlp_gelu_kernel(
 
         def turn(i):
             e0, e1 = TURNS[i]
-            tag, bufs = ("y_last", 1) if e1 == E else ("turned", 2)
+            tag, bufs = ("y_last", 1) if e1 == LAST else ("turned", 2)
             turned = psum.tile([P, e1 - e0, 2, C], F32, name="turned", tag=tag, bufs=bufs)
             for e in range(e0, e1):
                 words = h_rows[e][:].rearrange("c u p v -> c (u p v)").bitcast(F32)
@@ -259,7 +263,7 @@ def tile_moe_pre_mlp_gelu_kernel(
         nc.scalar.copy(
             last_codes[:].bitcast(U16), last_codes_in[:].bitcast(U16).rearrange("p s (m d) -> p s d m", d=PACK)
         )
-        nc.vector.tensor_copy(last_bytes[:], last_bytes_in[:].rearrange("p s (m d) -> p s d m", d=PACK))
+        permute_scales(0, "last_bytes0")
         quantise_x(2)
         first_pass(3, 5, 1)
         gather(4, "gathered0")
@@ -274,9 +278,9 @@ def tile_moe_pre_mlp_gelu_kernel(
         quantise_x(4)
         first_pass(5, 7, 1)
         turn(2)
-        weave(2, on_scalar)
         activate(5)
         activate(6)
+        weave(2, on_scalar)
         gather(6, "gathered0")
         for i in (3, 4):
             turn(i)
@@ -284,20 +288,22 @@ def tile_moe_pre_mlp_gelu_kernel(
         quantise_x(5)
         last_pass(0)
         interleave(6, "gathered1", on_vector)
+        permute_scales(1, "gathered0")
         quantise_x(6)
         last_pass(1)
         h_woven[5] = keep.tile([P, C * PACK], BF16, name="h_woven5", align_bytes=64)
         nc.scalar.activation(
             h_woven[5][:].rearrange("p (c d) -> p c d", d=PACK), sums[LAST][:].rearrange("p d c -> p c d"), GELU
         )
-        h_codes = keep.tile([P, SLOTS], U32, name="h_codes", tag="gathered0", align_bytes=64)
+        h_codes = keep.tile([P, SLOTS], U32, name="h_codes", tag="last_bytes_in", align_bytes=64)
         for i in range(len(TURNS)):
             quantise_h(h_codes, i)
 
         second_product(h_codes, 0, 0, 3, "y_first", on_scalar)
         second_product(h_codes, 0, 3, 6, "y_middle", on_vector)
-        second_product(h_codes, 0, 6, E, "y_last", on_scalar)
-        second_product(h_codes, 1, 0, 4, "y_last", on_scalar)
+        second_product(h_codes, 0, 6, LAST, "y_last", on_scalar)
+        second_product(h_codes, 0, LAST, E, "sums1", on_scalar)
+        second_product(h_codes, 1, 0, 4, "sums1", on_scalar)
         second_product(h_codes, 1, 4, E, "sums2", on_scalar)
         second_product(h_codes, 2, 0, 4, "sums2", on_scalar)
         second_product(h_codes, 2, 4, E, "sums0", on_scalar)

@@ -25,13 +25,14 @@ FP8X4 = mybir.dt.float8_e4m3fn_x4
 FP4X4 = mybir.dt.float4_e2m1fn_x4
 MULT = mybir.AluOpType.mult
 ADD = mybir.AluOpType.add
+COPY = mybir.ActivationFunctionType.Copy
 GELU = mybir.ActivationFunctionType.Gelu_apprx_tanh
 
-UNITS = [(0, 3, 0), (0, 3, 1), (3, 5, 1), (3, 7, 0), (5, 7, 1), (7, 8, 0), (7, 8, 1)]
+OWN = (4, 8, 0)
+LENT = [(0, 4, 0), (0, 4, 1), (4, 6, 1), (6, 7, 1), (7, 8, 1)]
 SPARE = 16
-TURNS = [(0, 2), (2, 3), (3, 5), (5, 6), (6, 7), (7, 8)]
+TURNS = [(0, 2), (2, 4), (4, 6), (6, 7), (7, 8)]
 LAST = E - 1
-SUM_BANKS = 3
 
 
 def tile_moe_pre_mlp_gelu_kernel(
@@ -46,169 +47,126 @@ def tile_moe_pre_mlp_gelu_kernel(
         pos_sb = [keep.tile([P, T // LIST], U16, name="pos%d_sb" % r) for r in range(2)]
         tokens = [
             [
-                keep.tile([P, T + (0 if s else SPARE)], F32, name="tokens_%d_%d" % (s, d), align_bytes=64)
+                keep.tile([P, T + SPARE], F32, name="tokens_%d_%d" % (s, d), align_bytes=64)
                 for d in range(PACK)
             ]
             for s in range(PASSES)
         ]
         gate_sb = keep.tile([P, SLOTS], F32, name="gate_sb")
-        w1_codes = keep.tile([P, LAST, PASSES, 2 * H], U8, name="w1_codes", align_bytes=64)
-        w1_bytes = keep.tile([P, LAST, PASSES, H], U8, name="w1_bytes", align_bytes=64)
-        last_codes_in = keep.tile([P, PASSES, 2 * H], U8, name="last_codes_in", align_bytes=64)
-        last_bytes_in = keep.tile([P, PASSES, H], U8, name="last_bytes_in", align_bytes=64)
-        last_codes = keep.tile([P, PASSES, PACK, 2 * P], U8, name="last_codes", align_bytes=64)
-        last_bytes = {}
+        w1_codes = [keep.tile([P, E, 2 * H], U8, name="w1_codes%d" % s, align_bytes=64) for s in range(PASSES)]
+        w1_bytes = keep.tile([P, E, PASSES, H], U8, name="w1_bytes", align_bytes=64)
         w2_codes = keep.tile([P, E, 2 * N], U8, name="w2_codes", align_bytes=64)
         w2_bytes = keep.tile([P, E, N], U8, name="w2_bytes", align_bytes=64)
-        x_bytes = keep.tile([P, PASSES, SLOTS], U8, name="x_bytes", align_bytes=64)
-        h_bytes = keep.tile([P, SLOTS], U8, name="h_bytes", align_bytes=64)
         y = [keep.tile([P, SLOTS], F32, name="y%d" % c) for c in range(CHUNKS)]
         ident = keep.tile([P, P], F32, name="ident")
+        warm = keep.tile([P, 2], F32, name="warm")
 
-        nc.gpsimd.memset(last_bytes_in[:].rearrange("p s i -> p (s i)").bitcast(I32), 0)
-        for d in range(PACK):
-            nc.gpsimd.memset(tokens[0][d][:, T:], 0.0)
+        nc.vector.memset(warm[:, 0:1], 0.0)
+        nc.scalar.activation(warm[:, 1:2], warm[:, 0:1], GELU)
+        for row in tokens:
+            for tile in row:
+                nc.gpsimd.memset(tile[:, T:], 0.0)
         make_identity(nc, ident[:])
         nc.vector.memset(w1_bytes[:].rearrange("p e s i -> p (e s i)").bitcast(I32), 0)
         nc.gpsimd.memset(w2_bytes[:].rearrange("p e n -> p (e n)").bitcast(I32), 0)
 
-        def load_w1_scales(e0, e1):
-            rows = w1_scales[e0:e1].rearrange("e s q i -> q (e s) i")
-            for r in range(4):
-                nc.sync.dma_start(
-                    w1_bytes[r:P:32, e0:e1].rearrange("p e s i -> p (e s) i").bitcast(I32), rows[r:16:4].bitcast(I32)
-                )
-
-        def load_w2_scales():
-            rows = w2_scales.rearrange("e s q n -> q (e s) n")
-            for r in range(4):
-                nc.sync.dma_start(w2_bytes[r:P:32].bitcast(I32), rows[r:16:4].bitcast(I32))
-
-        def load_w1(e0, e1):
-            nc.sync.dma_start(
-                w1_codes[:, e0:e1].rearrange("p e s b -> p (e s) b").bitcast(I32),
-                w1_words[e0:e1].rearrange("e s p b -> p (e s) b").bitcast(I32),
-            )
-
         x_rows = xT.rearrange("(s p d) t -> s d p t", s=PASSES, d=PACK)
-        first_slots = UNITS[0][1] * C
+        half_slots = SLOTS // 2
         nc.sync.dma_start(tokens[0][0][:, 0:T], x_rows[0, 0])
         nc.sync.dma_start(offs_sb[:], offs)
-        nc.sync.dma_start(gate_sb[:, 0:C], gate[0:P, 0:C])
-        nc.sync.dma_start(gate_sb[:, C:first_slots], gate[0:P, C:first_slots])
+        for a, b in ((half_slots, half_slots + C), (half_slots + C, SLOTS)):
+            nc.sync.dma_start(gate_sb[:, a:b], gate[0:P, a:b])
         for s in range(PASSES):
             for d in range(PACK):
                 if s or d:
                     nc.sync.dma_start(tokens[s][d][:, 0:T], x_rows[s, d])
-            if s == 0:
-                nc.sync.dma_start(last_codes_in[:].bitcast(I32), w1_words[LAST].rearrange("s p b -> p s b").bitcast(I32))
-        nc.sync.dma_start(gate_sb[:, first_slots:SLOTS], gate[0:P, first_slots:SLOTS])
-        load_w1_scales(0, 3)
-        load_w1(0, 1)
-        load_w1(1, 3)
-        load_w1_scales(3, LAST)
-        last_rows = w1_scales[LAST].rearrange("s q i -> q s i")
+        nc.sync.dma_start(gate_sb[:, 0:half_slots], gate[0:P, 0:half_slots])
+        w1_rows = w1_scales.rearrange("e s q i -> q (e s) i")
+        w2_rows = w2_scales.rearrange("e s q n -> q (e s) n")
         for r in range(4):
-            nc.sync.dma_start(last_bytes_in[r:P:32].bitcast(I32), last_rows[r:16:4].bitcast(I32))
-        load_w2_scales()
-        load_w1(3, 5)
-        load_w1(5, 7)
-        nc.sync.dma_start(w2_codes[:].bitcast(I32), w2_words.rearrange("e s p b -> p (e s) b").bitcast(I32))
+            nc.sync.dma_start(
+                w1_bytes[r:P:32].rearrange("p e s i -> p (e s) i").bitcast(I32), w1_rows[r:16:4].bitcast(I32)
+            )
+        for r in range(4):
+            nc.sync.dma_start(w2_bytes[r:P:32].bitcast(I32), w2_rows[r:16:4].bitcast(I32))
+        w1_passes = w1_words.rearrange("e s p b -> s p e b")
+        nc.sync.dma_start(w1_codes[0][:].bitcast(I32), w1_passes[0].bitcast(I32))
         nc.sync.dma_start(pos_sb[0][:], pos1)
         nc.sync.dma_start(pos_sb[1][:], pos2)
+        nc.sync.dma_start(w2_codes[:].bitcast(I32), w2_words.rearrange("e s p b -> p (e s) b").bitcast(I32))
+        nc.sync.dma_start(w1_codes[1][:].bitcast(I32), w1_passes[1].bitcast(I32))
 
         gathered = {}
         rounded = {}
         x_codes = {}
+        h_codes = {}
         sums = {}
         h_rows = {}
         h_turned = {}
         h_woven = {}
 
-        def gather(unit, tag):
-            e0, e1, s = UNITS[unit]
+        def gather(unit, flat):
+            e0, e1, s = unit
             lo, hi = e0 * C, e1 * C
-            flat = keep.tile([P, PACK * (hi - lo)], F32, name="gathered%d" % unit, tag=tag, align_bytes=64)
-            g = flat[:].rearrange("p (d c) -> p d c", d=PACK)
+            g = flat.rearrange("p (d c) -> p d c", d=PACK)
             for d in range(PACK):
-                cuts = [lo, C, hi] if (unit, d) == (0, 0) else [lo, hi]
+                cuts = [lo, lo + C, hi] if unit == OWN and d == 0 else [lo, hi]
                 for a, b in zip(cuts, cuts[1:]):
-                    nc.vector.tensor_tensor(
-                        g[:, d, a - lo : b - lo],
-                        tokens[s][d][:].indirect(offs_sb[:, a // LIST : b // LIST]),
-                        gate_sb[:, a:b],
-                        MULT,
-                    )
-            gathered[unit] = g
+                    picked_tokens = tokens[s][d][:].indirect(offs_sb[:, a // LIST : b // LIST])
+                    if unit == OWN:
+                        nc.vector.tensor_tensor(g[:, d, a - lo : b - lo], picked_tokens, gate_sb[:, a:b], MULT)
+                    else:
+                        nc.scalar.activation(g[:, d, :], picked_tokens, COPY)
+            for e in range(e0, e1):
+                gathered[e, s] = (g, (e - e0) * C)
 
-        def interleave(unit, tag, copy):
-            e0, e1, s = UNITS[unit]
-            xb = keep.tile([P, (e1 - e0) * C, PACK], BF16, name="rounded%d" % unit, tag=tag, align_bytes=64)
-            copy(
-                xb[:].rearrange("p (c i) d -> p c d i", i=4),
-                gathered[unit].rearrange("p d (c i) -> p c d i", i=4),
+        def interleave(e0, e1, s):
+            slots = (e1 - e0) * C
+            xb = keep.tile([P, slots, PACK], BF16, name="rounded%d_%d" % (e0, s), align_bytes=64)
+            g, lo = gathered[e0, s]
+            dst = xb[:].rearrange("p (c i) d -> p c d i", i=4)
+            src = g[:, :, lo : lo + slots].rearrange("p d (c i) -> p c d i", i=4)
+            if s == OWN[2] and OWN[0] <= e0 < OWN[1]:
+                nc.vector.tensor_copy(dst, src)
+            else:
+                weights = gate_sb[:, e0 * C : e1 * C].rearrange("p (c o i) -> p c o i", o=1, i=4)
+                nc.vector.tensor_tensor(dst, src, weights.broadcast_to([P, slots // 4, PACK, 4]), MULT)
+            rounded[e0, s] = xb
+
+        def quantise_x(e0, e1, s):
+            xc = keep.tile([P, (e1 - e0) * C], U32, name="codes%d_%d" % (e0, s), align_bytes=64)
+            xs = keep.tile([P, (e1 - e0) * C], U8, name="bytes%d_%d" % (e0, s), align_bytes=64)
+            for e in range(e0, e1):
+                cols = slice((e - e0) * C, (e - e0 + 1) * C)
+                x_codes[e, s] = (xc[:, cols], xs[:, cols])
+            nc.vector.quantize_mx(
+                out=xc[:].bitcast(FP8X4), scales=xs[:], in_=rounded[e0, s][:].rearrange("p c d -> p (c d)")
             )
-            rounded[unit] = xb
-
-        def quantise_x(unit):
-            e0, e1, s = UNITS[unit]
-            for b0 in range(e0, e1, 2):
-                b1 = min(b0 + 2, e1)
-                xc = keep.tile([P, (b1 - b0) * C], U32, name="codes%d_%d" % (unit, b0), align_bytes=64)
-                for e in range(b0, b1):
-                    x_codes[e, s] = xc[:, (e - b0) * C : (e - b0 + 1) * C]
-                nc.vector.quantize_mx(
-                    out=xc[:].bitcast(FP8X4),
-                    scales=x_bytes[:, s, b0 * C : b1 * C],
-                    in_=rounded[unit][:, (b0 - e0) * C : (b1 - e0) * C, :].rearrange("p c d -> p (c d)"),
-                )
 
         def first_pass(e0, e1, s):
             for e in range(e0, e1):
-                opens = e not in sums
-                if opens:
-                    sums[e] = psum.tile([P, H], F32, name="sums", tag="sums%d" % (e % SUM_BANKS))
+                if s == 0:
+                    sums[e] = psum.tile([P, H], F32, name="sums", tag="bank%d" % e)
                 nc.tensor.matmul_mx(
                     out=sums[e][:],
-                    lhsT=x_codes[e, s].bitcast(FP8X4),
-                    lhsT_scale=x_bytes[:, s, e * C : (e + 1) * C],
-                    rhs=w1_codes[:, e, s, :].bitcast(FP4X4),
+                    lhsT=x_codes[e, s][0].bitcast(FP8X4),
+                    lhsT_scale=x_codes[e, s][1],
+                    rhs=w1_codes[s][:, e, :].bitcast(FP4X4),
                     rhs_scale=w1_bytes[:, e, s, :],
-                    start=opens,
-                    stop=not opens,
+                    start=s == 0,
+                    stop=s == PASSES - 1,
                 )
 
-        def permute_scales(s, tag):
-            last_bytes[s] = keep.tile([P, PACK, P], U8, name="last_bytes", tag=tag, align_bytes=64)
-            nc.vector.tensor_copy(last_bytes[s][:], last_bytes_in[:, s].rearrange("p (m d) -> p d m", d=PACK))
-
-        def last_pass(s):
-            if s == 0:
-                sums[LAST] = psum.tile([P, PACK, C], F32, name="sums", tag="sums%d" % ((LAST - 1) % SUM_BANKS))
-            for d in range(PACK):
-                nc.tensor.matmul_mx(
-                    out=sums[LAST][:, d, :],
-                    lhsT=last_codes[:, s, d, :].bitcast(FP4X4),
-                    lhsT_scale=last_bytes[s][:, d, :],
-                    rhs=x_codes[LAST, s].bitcast(FP8X4),
-                    rhs_scale=x_bytes[:, s, LAST * C : E * C],
-                    start=(s, d) == (0, 0),
-                    stop=(s, d) == (PASSES - 1, PACK - 1),
-                )
-
-        def activate(e, calls=1):
-            hb = keep.tile([P, 2, P, 2], BF16, name="h_rows%d" % e, align_bytes=64)
-            pairs = sums[e][:].rearrange("c (p u v) -> c u p v", u=2, v=2)
-            for u in range(0, 2, 2 // calls):
-                nc.scalar.activation(hb[:, u : u + 2 // calls], pairs[:, u : u + 2 // calls], GELU)
+        def activate(e):
+            hb = keep.tile([P, 2, P, 2], BF16, name="h_rows%d" % e, align_bytes=64)[:]
+            nc.scalar.activation(hb, sums[e][:].rearrange("c (p u v) -> c u p v", u=2, v=2), GELU)
             h_rows[e] = hb
 
         def turn(i):
             e0, e1 = TURNS[i]
-            tag, bufs = ("y_last", 1) if e1 == LAST else ("turned", 2)
-            turned = psum.tile([P, e1 - e0, 2, C], F32, name="turned", tag=tag, bufs=bufs)
+            turned = psum.tile([P, e1 - e0, 2, C], F32, name="turned", tag="bank%d" % e0)
             for e in range(e0, e1):
-                words = h_rows[e][:].rearrange("c u p v -> c (u p v)").bitcast(F32)
+                words = h_rows[e].rearrange("c u p v -> c (u p v)").bitcast(F32)
                 for u in range(2):
                     nc.tensor.transpose(turned[:, e - e0, u, :], words[:, u * P : (u + 1) * P], ident[:])
             h_turned[i] = turned
@@ -222,20 +180,24 @@ def tile_moe_pre_mlp_gelu_kernel(
             )
             h_woven[i] = hq
 
-        def quantise_h(h_codes, i):
-            cols = slice(TURNS[i][0] * C, TURNS[i][1] * C)
-            nc.vector.quantize_mx(out=h_codes[:, cols].bitcast(FP8X4), scales=h_bytes[:, cols], in_=h_woven[i][:])
-
-        def second_product(h_codes, chunk, e0, e1, tag, copy):
-            acc = psum.tile([P, (e1 - e0) * C], F32, name="acc", tag=tag)
+        def quantise_h(i):
+            e0, e1 = TURNS[i]
+            hc = keep.tile([P, (e1 - e0) * C], U32, name="h_codes%d" % i, align_bytes=64)
+            hs = keep.tile([P, (e1 - e0) * C], U8, name="h_bytes%d" % i, align_bytes=64)
             for e in range(e0, e1):
-                cols = slice(e * C, (e + 1) * C)
+                cols = slice((e - e0) * C, (e - e0 + 1) * C)
+                h_codes[e] = (hc[:, cols], hs[:, cols])
+            nc.vector.quantize_mx(out=hc[:].bitcast(FP8X4), scales=hs[:], in_=h_woven[i][:])
+
+        def second_product(chunk, e0, e1, bank, copy):
+            acc = psum.tile([P, (e1 - e0) * C], F32, name="acc", tag="bank%d" % bank)
+            for e in range(e0, e1):
                 nc.tensor.matmul_mx(
                     out=acc[:, (e - e0) * C : (e - e0 + 1) * C],
                     lhsT=w2_codes[:, e, 2 * P * chunk : 2 * P * (chunk + 1)].bitcast(FP4X4),
                     lhsT_scale=w2_bytes[:, e, P * chunk : P * (chunk + 1)],
-                    rhs=h_codes[:, cols].bitcast(FP8X4),
-                    rhs_scale=h_bytes[:, cols],
+                    rhs=h_codes[e][0].bitcast(FP8X4),
+                    rhs_scale=h_codes[e][1],
                     start=True,
                     stop=True,
                 )
@@ -243,94 +205,61 @@ def tile_moe_pre_mlp_gelu_kernel(
 
         on_scalar, on_vector = nc.scalar.copy, nc.vector.tensor_copy
 
-        for unit in range(2):
-            gather(unit, "gathered%d" % unit)
-            interleave(unit, "rounded%d" % unit, on_scalar)
-        quantise_x(0)
-        first_pass(0, 3, 0)
-        gather(2, "gathered0")
-        quantise_x(1)
-        first_pass(0, 3, 1)
-        gather(3, "gathered1")
-        for e in range(3):
-            activate(e)
-        interleave(2, "codes1_2", on_scalar)
-        turn(0)
-        turn(1)
-        weave(0, on_scalar)
-        weave(1, on_scalar)
-        interleave(3, "h_rows2", on_scalar)
-        nc.scalar.copy(
-            last_codes[:].bitcast(U16), last_codes_in[:].bitcast(U16).rearrange("p s (m d) -> p s d m", d=PACK)
-        )
-        permute_scales(0, "last_bytes0")
-        quantise_x(2)
-        first_pass(3, 5, 1)
-        gather(4, "gathered0")
-        interleave(4, "rounded4", on_scalar)
-        quantise_x(3)
-        first_pass(3, 6, 0)
-        gather(5, "gathered1")
-        activate(3)
-        first_pass(6, 7, 0)
-        activate(4)
-        interleave(5, "codes3_3", on_scalar)
-        quantise_x(4)
-        first_pass(5, 7, 1)
-        turn(2)
-        activate(5)
-        activate(6)
-        weave(2, on_scalar)
-        gather(6, "gathered0")
-        for i in (3, 4):
-            turn(i)
-            weave(i, on_scalar)
-        quantise_x(5)
-        last_pass(0)
-        interleave(6, "gathered1", on_vector)
-        permute_scales(1, "gathered0")
-        quantise_x(6)
-        last_pass(1)
-        h_woven[5] = keep.tile([P, C * PACK], BF16, name="h_woven5", align_bytes=64)
-        nc.scalar.activation(
-            h_woven[5][:].rearrange("p (c d) -> p c d", d=PACK), sums[LAST][:].rearrange("p d c -> p c d"), GELU
-        )
-        h_codes = keep.tile([P, SLOTS], U32, name="h_codes", tag="last_bytes_in", align_bytes=64)
-        for i in range(len(TURNS)):
-            quantise_h(h_codes, i)
+        def staging(name, tag):
+            return keep.tile([P, PACK * half_slots], F32, name=name, tag=tag, align_bytes=64)
 
-        second_product(h_codes, 0, 0, 3, "y_first", on_scalar)
-        second_product(h_codes, 0, 3, 6, "y_middle", on_vector)
-        second_product(h_codes, 0, 6, LAST, "y_last", on_scalar)
-        second_product(h_codes, 0, LAST, E, "sums1", on_scalar)
-        second_product(h_codes, 1, 0, 4, "sums1", on_scalar)
-        second_product(h_codes, 1, 4, E, "sums2", on_scalar)
-        second_product(h_codes, 2, 0, 4, "sums2", on_scalar)
-        second_product(h_codes, 2, 4, E, "sums0", on_scalar)
+        gather(LENT[0], staging("gathered_first", "gathered_first")[:])
+        gather(OWN, staging("gathered_own", "gathered_own")[:])
+        gather(LENT[1], staging("gathered_second", "gathered_second")[:])
+        for first in (4, 0):
+            interleave(first, first + 2, 0)
+            interleave(first + 2, first + 4, 0)
+            quantise_x(first, first + 2, 0)
+            quantise_x(first + 2, first + 4, 0)
+            first_pass(first, first + 4, 0)
+        late = staging("gathered_late", "gathered_first")
+        for e0, e1, s in LENT[2:]:
+            gather((e0, e1, s), late[:, PACK * (e0 * C - half_slots) : PACK * (e1 * C - half_slots)])
+        steps = [(0, 2), (2, 4), (4, 6), (6, 7), (7, 8)]
+        interleave(0, 2, 1)
+        for i, (e0, e1) in enumerate(steps):
+            if i + 1 < len(steps):
+                interleave(steps[i + 1][0], steps[i + 1][1], 1)
+            quantise_x(e0, e1, 1)
+            if e1 <= 6:
+                first_pass(e0, e1, 1)
+        for i, (e0, e1) in enumerate(TURNS):
+            for e in range(e0, e1):
+                activate(e)
+            turn(i)
+            if i == 0:
+                first_pass(6, E, 1)
+            weave(i, on_vector if e1 - e0 == 2 else on_scalar)
+            if i:
+                quantise_h(i - 1)
+        quantise_h(len(TURNS) - 1)
+        second_product(0, LAST, E, 2, on_scalar)
+        second_product(0, 4, LAST, 0, on_vector)
+        second_product(0, 0, 4, 1, on_scalar)
+        second_product(1, 4, E, 4, on_vector)
+        second_product(1, 0, 4, 1, on_vector)
+        second_product(2, 6, E, 6, on_vector)
 
         picked = [keep.tile([P, T], F32, name="picked%d" % c) for c in range(CHUNKS)]
+        summed = [keep.tile([P, T], F32, name="summed%d" % c) for c in range(CHUNKS)]
 
-        def pick(chunk, cuts):
+        def combine(chunk, cuts):
             for a, b in zip(cuts, cuts[1:]):
-                nc.vector.tensor_copy(picked[chunk][:, a:b], y[chunk][:].indirect(pos_sb[0][:, a // LIST : b // LIST]))
-
-        def combine(chunk, cuts, tag):
-            lo, hi = cuts[0], cuts[-1]
-            summed = keep.tile([P, hi - lo], F32, name="summed", tag=tag)
-            for a, b in zip(cuts, cuts[1:]):
+                lists = [pos[:, a // LIST : b // LIST] for pos in pos_sb]
+                nc.scalar.activation(picked[chunk][:, a:b], y[chunk][:].indirect(lists[0]), COPY)
                 nc.vector.tensor_tensor(
-                    summed[:, a - lo : b - lo],
-                    y[chunk][:].indirect(pos_sb[1][:, a // LIST : b // LIST]),
-                    picked[chunk][:, a:b],
-                    ADD,
+                    summed[chunk][:, a:b], y[chunk][:].indirect(lists[1]), picked[chunk][:, a:b], ADD
                 )
-                nc.sync.dma_start(out[chunk * P : (chunk + 1) * P, a:b], summed[:, a - lo : b - lo])
+                nc.sync.dma_start(out[chunk * P : (chunk + 1) * P, a:b], summed[chunk][:, a:b])
 
         half = T // 2
-        pick(0, [0, half, T])
-        combine(0, [0, half], "summed_first")
-        combine(0, [half, T], "summed_second")
-        pick(1, [0, T])
-        pick(2, [0, T])
-        combine(1, [0, T], "summed_first")
-        combine(2, [0, half, T - T // 4, T], "summed_second")
+        combine(0, [0, half, T])
+        combine(1, [0, half, T])
+        second_product(2, 0, 4, 4, on_scalar)
+        second_product(2, 4, 6, 1, on_scalar)
+        combine(2, [0, half, T - T // 4, T])

@@ -87,14 +87,14 @@ def tile_moe_pre_mlp_gelu_kernel(
             nc.sync.dma_start(
                 w1_bytes[r:P:32].rearrange("p e s i -> p (e s) i").bitcast(I32), w1_rows[r:16:4].bitcast(I32)
             )
-        for r in range(4):
-            nc.sync.dma_start(w2_bytes[r:P:32].bitcast(I32), w2_rows[r:16:4].bitcast(I32))
         w1_passes = w1_words.rearrange("e s p b -> s p e b")
         nc.sync.dma_start(w1_codes[0][:].bitcast(I32), w1_passes[0].bitcast(I32))
+        nc.sync.dma_start(w1_codes[1][:].bitcast(I32), w1_passes[1].bitcast(I32))
+        for r in range(4):
+            nc.sync.dma_start(w2_bytes[r:P:32].bitcast(I32), w2_rows[r:16:4].bitcast(I32))
+        nc.sync.dma_start(w2_codes[:].bitcast(I32), w2_words.rearrange("e s p b -> p (e s) b").bitcast(I32))
         nc.sync.dma_start(pos_sb[0][:], pos1)
         nc.sync.dma_start(pos_sb[1][:], pos2)
-        nc.sync.dma_start(w2_codes[:].bitcast(I32), w2_words.rearrange("e s p b -> p (e s) b").bitcast(I32))
-        nc.sync.dma_start(w1_codes[1][:].bitcast(I32), w1_passes[1].bitcast(I32))
 
         gathered = {}
         rounded = {}
@@ -238,9 +238,9 @@ def tile_moe_pre_mlp_gelu_kernel(
             if i:
                 quantise_h(i - 1)
         quantise_h(len(TURNS) - 1)
-        second_product(0, LAST, E, 2, on_scalar)
-        second_product(0, 4, LAST, 0, on_vector)
         second_product(0, 0, 4, 1, on_scalar)
+        second_product(0, 4, LAST, 0, on_vector)
+        second_product(0, LAST, E, 2, on_scalar)
         second_product(1, 4, E, 4, on_vector)
         second_product(1, 0, 4, 1, on_vector)
         second_product(2, 6, E, 6, on_vector)

@@ -32,6 +32,7 @@ OWN = (4, 8, 0)
 LENT = [(0, 4, 0), (0, 4, 1), (4, 6, 1), (6, 7, 1), (7, 8, 1)]
 SPARE = 16
 TURNS = [(0, 2), (2, 4), (4, 6), (6, 7), (7, 8)]
+TURN_BANKS = [0, 4, 5, 6, 7]
 LAST = E - 1
 
 
@@ -52,7 +53,8 @@ def tile_moe_pre_mlp_gelu_kernel(
             ]
             for s in range(PASSES)
         ]
-        gate_sb = keep.tile([P, SLOTS], F32, name="gate_sb")
+        gate_sb = keep.tile([P, SLOTS // 2], F32, name="gate_sb")
+        gate_cols = keep.tile([P, E // 2], F32, name="gate_cols")
         w1_codes = [keep.tile([P, E, 2 * H], U8, name="w1_codes%d" % s, align_bytes=64) for s in range(PASSES)]
         w1_bytes = keep.tile([P, E, PASSES, H], U8, name="w1_bytes", align_bytes=64)
         w2_codes = keep.tile([P, E, 2 * N], U8, name="w2_codes", align_bytes=64)
@@ -75,12 +77,13 @@ def tile_moe_pre_mlp_gelu_kernel(
         nc.sync.dma_start(tokens[0][0][:, 0:T], x_rows[0, 0])
         nc.sync.dma_start(offs_sb[:], offs)
         for a, b in ((half_slots, half_slots + C), (half_slots + C, SLOTS)):
-            nc.sync.dma_start(gate_sb[:, a:b], gate[0:P, a:b])
+            nc.sync.dma_start(gate_sb[:, a - half_slots : b - half_slots], gate[0:P, a:b])
         for s in range(PASSES):
             for d in range(PACK):
                 if s or d:
                     nc.sync.dma_start(tokens[s][d][:, 0:T], x_rows[s, d])
-        nc.sync.dma_start(gate_sb[:, 0:half_slots], gate[0:P, 0:half_slots])
+        with nc.allow_non_contiguous_dma(reason="one weight for each partition and expert"):
+            nc.sync.dma_start(gate_cols[:], gate[0, 0:half_slots].rearrange("(e p) -> p e", p=P))
         w1_rows = w1_scales.rearrange("e s q i -> q (e s) i")
         w2_rows = w2_scales.rearrange("e s q n -> q (e s) n")
         for r in range(4):
@@ -89,7 +92,8 @@ def tile_moe_pre_mlp_gelu_kernel(
             )
         w1_passes = w1_words.rearrange("e s p b -> s p e b")
         nc.sync.dma_start(w1_codes[0][:].bitcast(I32), w1_passes[0].bitcast(I32))
-        nc.sync.dma_start(w1_codes[1][:].bitcast(I32), w1_passes[1].bitcast(I32))
+        for e in range(0, E, E // 2):
+            nc.sync.dma_start(w1_codes[1][:, e : e + E // 2].bitcast(I32), w1_passes[1, :, e : e + E // 2].bitcast(I32))
         for r in range(4):
             nc.sync.dma_start(w2_bytes[r:P:32].bitcast(I32), w2_rows[r:16:4].bitcast(I32))
         nc.sync.dma_start(w2_codes[:].bitcast(I32), w2_words.rearrange("e s p b -> p (e s) b").bitcast(I32))
@@ -114,7 +118,7 @@ def tile_moe_pre_mlp_gelu_kernel(
                 for a, b in zip(cuts, cuts[1:]):
                     picked_tokens = tokens[s][d][:].indirect(offs_sb[:, a // LIST : b // LIST])
                     if unit == OWN:
-                        nc.vector.tensor_tensor(g[:, d, a - lo : b - lo], picked_tokens, gate_sb[:, a:b], MULT)
+                        nc.vector.tensor_tensor(g[:, d, a - lo : b - lo], picked_tokens, gate_sb[:, a - half_slots : b - half_slots], MULT)
                     else:
                         nc.scalar.activation(g[:, d, :], picked_tokens, COPY)
             for e in range(e0, e1):
@@ -129,7 +133,9 @@ def tile_moe_pre_mlp_gelu_kernel(
             if s == OWN[2] and OWN[0] <= e0 < OWN[1]:
                 nc.vector.tensor_copy(dst, src)
             else:
-                weights = gate_sb[:, e0 * C : e1 * C].rearrange("p (c o i) -> p c o i", o=1, i=4)
+                spread = gate_bank if e0 < E // 2 else gate_sb
+                first = e0 * C % half_slots
+                weights = spread[:, first : first + slots].rearrange("p (c o i) -> p c o i", o=1, i=4)
                 nc.vector.tensor_tensor(dst, src, weights.broadcast_to([P, slots // 4, PACK, 4]), MULT)
             rounded[e0, s] = xb
 
@@ -164,7 +170,7 @@ def tile_moe_pre_mlp_gelu_kernel(
 
         def turn(i):
             e0, e1 = TURNS[i]
-            turned = psum.tile([P, e1 - e0, 2, C], F32, name="turned", tag="bank%d" % e0)
+            turned = psum.tile([P, e1 - e0, 2, C], F32, name="turned", tag="bank%d" % TURN_BANKS[i])
             for e in range(e0, e1):
                 words = h_rows[e].rearrange("c u p v -> c (u p v)").bitcast(F32)
                 for u in range(2):
@@ -208,6 +214,9 @@ def tile_moe_pre_mlp_gelu_kernel(
         def staging(name, tag):
             return keep.tile([P, PACK * half_slots], F32, name=name, tag=tag, align_bytes=64)
 
+        gate_bank = psum.tile([P, half_slots], F32, name="gate_bank", tag="bank%d" % LAST)
+        for e in range(E // 2):
+            nc.tensor.transpose(gate_bank[:, e * C : (e + 1) * C], gate_cols[:, e : e + 1].to_broadcast([P, P]), ident[:])
         gather(LENT[0], staging("gathered_first", "gathered_first")[:])
         gather(OWN, staging("gathered_own", "gathered_own")[:])
         gather(LENT[1], staging("gathered_second", "gathered_second")[:])
@@ -216,7 +225,7 @@ def tile_moe_pre_mlp_gelu_kernel(
             interleave(first + 2, first + 4, 0)
             quantise_x(first, first + 2, 0)
             quantise_x(first + 2, first + 4, 0)
-            first_pass(first, first + 4, 0)
+            first_pass(first, min(first + 4, LAST), 0)
         late = staging("gathered_late", "gathered_first")
         for e0, e1, s in LENT[2:]:
             gather((e0, e1, s), late[:, PACK * (e0 * C - half_slots) : PACK * (e1 * C - half_slots)])
@@ -226,14 +235,19 @@ def tile_moe_pre_mlp_gelu_kernel(
             if i + 1 < len(steps):
                 interleave(steps[i + 1][0], steps[i + 1][1], 1)
             quantise_x(e0, e1, 1)
-            if e1 <= 6:
+            if i == 0:
+                first_pass(LAST, E, 0)
+            if e1 <= 4:
                 first_pass(e0, e1, 1)
         for i, (e0, e1) in enumerate(TURNS):
             for e in range(e0, e1):
-                activate(e)
+                if e not in h_rows:
+                    activate(e)
+            if i == 1:
+                activate(e1)
             turn(i)
             if i == 0:
-                first_pass(6, E, 1)
+                first_pass(4, E, 1)
             weave(i, on_vector if e1 - e0 == 2 else on_scalar)
             if i:
                 quantise_h(i - 1)

@@ -90,15 +90,14 @@ def tile_moe_pre_mlp_gelu_kernel(
             nc.sync.dma_start(
                 w1_bytes[r:P:32].rearrange("p e s i -> p (e s) i").bitcast(I32), w1_rows[r:16:4].bitcast(I32)
             )
-        w1_passes = w1_words.rearrange("e s p b -> s p e b")
-        nc.sync.dma_start(w1_codes[0][:].bitcast(I32), w1_passes[0].bitcast(I32))
-        for e in range(0, E, E // 2):
-            nc.sync.dma_start(w1_codes[1][:, e : e + E // 2].bitcast(I32), w1_passes[1, :, e : e + E // 2].bitcast(I32))
-        for r in range(4):
-            nc.sync.dma_start(w2_bytes[r:P:32].bitcast(I32), w2_rows[r:16:4].bitcast(I32))
-        nc.sync.dma_start(w2_codes[:].bitcast(I32), w2_words.rearrange("e s p b -> p (e s) b").bitcast(I32))
         nc.sync.dma_start(pos_sb[0][:], pos1)
         nc.sync.dma_start(pos_sb[1][:], pos2)
+        for r in range(4):
+            nc.sync.dma_start(w2_bytes[r:P:32].bitcast(I32), w2_rows[r:16:4].bitcast(I32))
+        w1_passes = w1_words.rearrange("e s p b -> s p e b")
+        for s, e0, e1 in ((0, 4, LAST), (0, 2, 4), (0, 0, 2), (0, LAST, E), (1, 0, 4), (1, 4, E)):
+            nc.sync.dma_start(w1_codes[s][:, e0:e1].bitcast(I32), w1_passes[s, :, e0:e1].bitcast(I32))
+        nc.sync.dma_start(w2_codes[:].bitcast(I32), w2_words.rearrange("e s p b -> p (e s) b").bitcast(I32))
 
         gathered = {}
         rounded = {}

@@ -29,10 +29,9 @@ COPY = mybir.ActivationFunctionType.Copy
 GELU = mybir.ActivationFunctionType.Gelu_apprx_tanh
 
 OWN = (4, 8, 0)
-LENT = [(0, 4, 0), (0, 4, 1), (4, 6, 1), (6, 7, 1), (7, 8, 1)]
+LENT = [(0, 4, 0), (0, 4, 1), (4, 6, 1), (6, 8, 1)]
 SPARE = 16
-TURNS = [(0, 2), (2, 4), (4, 6), (6, 7), (7, 8)]
-TURN_BANKS = [0, 4, 5, 6, 7]
+TURNS = [(0, 2), (2, 3), (3, 5), (5, 6), (6, 7), (7, 8)]
 LAST = E - 1
 
 
@@ -169,7 +168,7 @@ def tile_moe_pre_mlp_gelu_kernel(
 
         def turn(i):
             e0, e1 = TURNS[i]
-            turned = psum.tile([P, e1 - e0, 2, C], F32, name="turned", tag="bank%d" % TURN_BANKS[i])
+            turned = psum.tile([P, e1 - e0, 2, C], F32, name="turned", tag="bank%d" % e0)
             for e in range(e0, e1):
                 words = h_rows[e].rearrange("c u p v -> c (u p v)").bitcast(F32)
                 for u in range(2):
@@ -187,7 +186,8 @@ def tile_moe_pre_mlp_gelu_kernel(
 
         def quantise_h(i):
             e0, e1 = TURNS[i]
-            hc = keep.tile([P, (e1 - e0) * C], U32, name="h_codes%d" % i, align_bytes=64)
+            tag = "h_rows%d" % e1 if i == 0 else "h_codes%d" % i
+            hc = keep.tile([P, (e1 - e0) * C], U32, name="h_codes%d" % i, tag=tag, align_bytes=64)
             hs = keep.tile([P, (e1 - e0) * C], U8, name="h_bytes%d" % i, align_bytes=64)
             for e in range(e0, e1):
                 cols = slice((e - e0) * C, (e - e0 + 1) * C)
@@ -196,7 +196,7 @@ def tile_moe_pre_mlp_gelu_kernel(
 
         def second_product(chunk, e0, e1, bank, copy):
             acc = psum.tile([P, (e1 - e0) * C], F32, name="acc", tag="bank%d" % bank)
-            for e in range(e0, e1):
+            for e in range(e0, e1) if e0 == 0 else reversed(range(e0, e1)):
                 nc.tensor.matmul_mx(
                     out=acc[:, (e - e0) * C : (e - e0 + 1) * C],
                     lhsT=w2_codes[:, e, 2 * P * chunk : 2 * P * (chunk + 1)].bitcast(FP4X4),
@@ -228,35 +228,33 @@ def tile_moe_pre_mlp_gelu_kernel(
         late = staging("gathered_late", "gathered_first")
         for e0, e1, s in LENT[2:]:
             gather((e0, e1, s), late[:, PACK * (e0 * C - half_slots) : PACK * (e1 * C - half_slots)])
-        steps = [(0, 2), (2, 4), (4, 6), (6, 7), (7, 8)]
         interleave(0, 2, 1)
-        for i, (e0, e1) in enumerate(steps):
-            if i + 1 < len(steps):
-                interleave(steps[i + 1][0], steps[i + 1][1], 1)
-            quantise_x(e0, e1, 1)
-            if i == 0:
-                first_pass(LAST, E, 0)
-            if e1 <= 4:
-                first_pass(e0, e1, 1)
+        interleave(2, 4, 1)
+        quantise_x(0, 2, 1)
+        first_pass(LAST, E, 0)
+        first_pass(0, 2, 1)
+        interleave(4, 6, 1)
+        quantise_x(2, 4, 1)
+        first_pass(2, 4, 1)
+        quantise_x(4, 6, 1)
+        interleave(6, E, 1)
+        quantise_x(6, E, 1)
         for i, (e0, e1) in enumerate(TURNS):
             for e in range(e0, e1):
-                if e not in h_rows:
-                    activate(e)
-            if i == 1:
-                activate(e1)
+                activate(e)
             turn(i)
-            if i == 0:
+            if i == 1:
                 first_pass(4, E, 1)
-            weave(i, on_vector if e1 - e0 == 2 else on_scalar)
+            weave(i, on_vector if e1 < LAST else on_scalar)
             if i:
                 quantise_h(i - 1)
         quantise_h(len(TURNS) - 1)
-        second_product(0, 0, 4, 1, on_scalar)
+        second_product(0, 0, 4, 6, on_scalar)
         second_product(0, 4, LAST, 0, on_vector)
         second_product(0, LAST, E, 2, on_scalar)
+        second_product(1, 0, 4, LAST, on_vector)
         second_product(1, 4, E, 4, on_vector)
-        second_product(1, 0, 4, 1, on_vector)
-        second_product(2, 6, E, 6, on_vector)
+        second_product(2, 6, E, 1, on_vector)
 
         picked = [keep.tile([P, T], F32, name="picked%d" % c) for c in range(CHUNKS)]
         summed = [keep.tile([P, T], F32, name="summed%d" % c) for c in range(CHUNKS)]
@@ -271,8 +269,8 @@ def tile_moe_pre_mlp_gelu_kernel(
                 nc.sync.dma_start(out[chunk * P : (chunk + 1) * P, a:b], summed[chunk][:, a:b])
 
         half = T // 2
-        combine(0, [0, half, T])
-        combine(1, [0, half, T])
+        combine(0, [0, T])
+        combine(1, [0, T])
         second_product(2, 0, 4, 4, on_scalar)
-        second_product(2, 4, 6, 1, on_scalar)
-        combine(2, [0, half, T - T // 4, T])
+        second_product(2, 4, 6, 6, on_scalar)
+        combine(2, [0, half, T - T // 8, T])

@@ -28,8 +28,8 @@ ADD = mybir.AluOpType.add
 COPY = mybir.ActivationFunctionType.Copy
 GELU = mybir.ActivationFunctionType.Gelu_apprx_tanh
 
-OWN = (4, 8, 0)
-LENT = [(0, 4, 0), (0, 4, 1), (4, 6, 1), (6, 8, 1)]
+OWN = [(4, 8, 0), (7, 8, 1)]
+LENT = [(0, 4, 0), (0, 4, 1), (4, 6, 1), (6, 7, 1)]
 SPARE = 16
 TURNS = [(0, 2), (2, 3), (3, 5), (5, 6), (6, 7), (7, 8)]
 LAST = E - 1
@@ -112,10 +112,10 @@ def tile_moe_pre_mlp_gelu_kernel(
             lo, hi = e0 * C, e1 * C
             g = flat.rearrange("p (d c) -> p d c", d=PACK)
             for d in range(PACK):
-                cuts = [lo, lo + C, hi] if unit == OWN and d == 0 else [lo, hi]
+                cuts = [lo, lo + C, hi] if unit == OWN[0] and d == 0 else [lo, hi]
                 for a, b in zip(cuts, cuts[1:]):
                     picked_tokens = tokens[s][d][:].indirect(offs_sb[:, a // LIST : b // LIST])
-                    if unit == OWN:
+                    if unit in OWN:
                         nc.vector.tensor_tensor(g[:, d, a - lo : b - lo], picked_tokens, gate_sb[:, a - half_slots : b - half_slots], MULT)
                     else:
                         nc.scalar.activation(g[:, d, :], picked_tokens, COPY)
@@ -128,7 +128,7 @@ def tile_moe_pre_mlp_gelu_kernel(
             g, lo = gathered[e0, s]
             dst = xb[:].rearrange("p (c i) d -> p c d i", i=4)
             src = g[:, :, lo : lo + slots].rearrange("p d (c i) -> p c d i", i=4)
-            if s == OWN[2] and OWN[0] <= e0 < OWN[1]:
+            if any(s == s1 and a <= e0 < b for a, b, s1 in OWN):
                 nc.vector.tensor_copy(dst, src)
             else:
                 spread = gate_bank if e0 < E // 2 else gate_sb
@@ -217,7 +217,7 @@ def tile_moe_pre_mlp_gelu_kernel(
         for e in range(E // 2):
             nc.tensor.transpose(gate_bank[:, e * C : (e + 1) * C], gate_cols[:, e : e + 1].to_broadcast([P, P]), ident[:])
         gather(LENT[0], staging("gathered_first", "gathered_first")[:])
-        gather(OWN, staging("gathered_own", "gathered_own")[:])
+        gather(OWN[0], staging("gathered_own", "gathered_own")[:])
         gather(LENT[1], staging("gathered_second", "gathered_second")[:])
         for first in (4, 0):
             interleave(first, first + 2, 0)
@@ -236,16 +236,19 @@ def tile_moe_pre_mlp_gelu_kernel(
         interleave(4, 6, 1)
         quantise_x(2, 4, 1)
         first_pass(2, 4, 1)
+        interleave(6, LAST, 1)
         quantise_x(4, 6, 1)
-        interleave(6, E, 1)
-        quantise_x(6, E, 1)
+        gather(OWN[1], keep.tile([P, PACK * C], F32, name="gathered_last", tag="rounded2_1", align_bytes=64)[:])
+        quantise_x(6, LAST, 1)
+        interleave(LAST, E, 1)
+        quantise_x(LAST, E, 1)
         for i, (e0, e1) in enumerate(TURNS):
             for e in range(e0, e1):
                 activate(e)
             turn(i)
             if i == 1:
                 first_pass(4, E, 1)
-            weave(i, on_vector if e1 < LAST else on_scalar)
+            weave(i, on_vector if e1 < LAST - 1 else on_scalar)
             if i:
                 quantise_h(i - 1)
         quantise_h(len(TURNS) - 1)

@@ -33,6 +33,7 @@ LENT = [(0, 4, 0), (0, 4, 1), (4, 6, 1), (6, 7, 1)]
 SPARE = 16
 TURNS = [(0, 2), (2, 3), (3, 5), (5, 6), (6, 7), (7, 8)]
 LAST = E - 1
+SCALE_GROUPS = [(0, 0, E), (1, 0, 4), (1, 4, E)]
 
 
 def tile_moe_pre_mlp_gelu_kernel(
@@ -55,7 +56,10 @@ def tile_moe_pre_mlp_gelu_kernel(
         gate_sb = keep.tile([P, SLOTS // 2], F32, name="gate_sb")
         gate_cols = keep.tile([P, E // 2], F32, name="gate_cols")
         w1_codes = [keep.tile([P, E, 2 * H], U8, name="w1_codes%d" % s, align_bytes=64) for s in range(PASSES)]
-        w1_bytes = keep.tile([P, E, PASSES, H], U8, name="w1_bytes", align_bytes=64)
+        w1_bytes = {
+            group: keep.tile([P, group[2] - group[1], H], U8, name="w1_bytes%d_%d" % group[:2], align_bytes=64)
+            for group in SCALE_GROUPS
+        }
         w2_codes = keep.tile([P, E, 2 * N], U8, name="w2_codes", align_bytes=64)
         w2_bytes = keep.tile([P, E, N], U8, name="w2_bytes", align_bytes=64)
         y = [keep.tile([P, SLOTS], F32, name="y%d" % c) for c in range(CHUNKS)]
@@ -68,7 +72,8 @@ def tile_moe_pre_mlp_gelu_kernel(
             for tile in row:
                 nc.gpsimd.memset(tile[:, T:], 0.0)
         make_identity(nc, ident[:])
-        nc.vector.memset(w1_bytes[:].rearrange("p e s i -> p (e s i)").bitcast(I32), 0)
+        for tile in [w1_bytes[group] for group in SCALE_GROUPS]:
+            nc.vector.memset(tile[:].rearrange("p e i -> p (e i)").bitcast(I32), 0)
         nc.gpsimd.memset(w2_bytes[:].rearrange("p e n -> p (e n)").bitcast(I32), 0)
 
         x_rows = xT.rearrange("(s p d) t -> s d p t", s=PASSES, d=PACK)
@@ -83,19 +88,25 @@ def tile_moe_pre_mlp_gelu_kernel(
                     nc.sync.dma_start(tokens[s][d][:, 0:T], x_rows[s, d])
         with nc.allow_non_contiguous_dma(reason="one weight for each partition and expert"):
             nc.sync.dma_start(gate_cols[:], gate[0, 0:half_slots].rearrange("(e p) -> p e", p=P))
-        w1_rows = w1_scales.rearrange("e s q i -> q (e s) i")
-        w2_rows = w2_scales.rearrange("e s q n -> q (e s) n")
-        for r in range(4):
-            nc.sync.dma_start(
-                w1_bytes[r:P:32].rearrange("p e s i -> p (e s) i").bitcast(I32), w1_rows[r:16:4].bitcast(I32)
-            )
+        def load_scales(tile, rows):
+            for r in range(4):
+                nc.sync.dma_start(tile[r:P:32].bitcast(I32), rows[r:16:4].bitcast(I32))
+
+        def load_w1(s, e0, e1):
+            nc.sync.dma_start(w1_codes[s][:, e0:e1].bitcast(I32), w1_passes[s, :, e0:e1].bitcast(I32))
+
+        w1_rows = w1_scales.rearrange("e s q i -> s q e i")
+        w1_passes = w1_words.rearrange("e s p b -> s p e b")
+        for s, e0, e1 in SCALE_GROUPS[:2]:
+            load_scales(w1_bytes[s, e0, e1][:], w1_rows[s, :, e0:e1])
         nc.sync.dma_start(pos_sb[0][:], pos1)
         nc.sync.dma_start(pos_sb[1][:], pos2)
-        for r in range(4):
-            nc.sync.dma_start(w2_bytes[r:P:32].bitcast(I32), w2_rows[r:16:4].bitcast(I32))
-        w1_passes = w1_words.rearrange("e s p b -> s p e b")
-        for s, e0, e1 in ((0, 4, LAST), (0, 2, 4), (0, 0, 2), (0, LAST, E), (1, 0, 4), (1, 4, E)):
-            nc.sync.dma_start(w1_codes[s][:, e0:e1].bitcast(I32), w1_passes[s, :, e0:e1].bitcast(I32))
+        for e0, e1 in ((4, LAST), (2, 4), (0, 2), (LAST, E)):
+            load_w1(0, e0, e1)
+        load_w1(1, 0, 4)
+        load_scales(w1_bytes[SCALE_GROUPS[2]][:], w1_rows[1, :, 4:E])
+        load_w1(1, 4, E)
+        load_scales(w2_bytes[:], w2_scales.rearrange("e s q n -> q (e s) n"))
         nc.sync.dma_start(w2_codes[:].bitcast(I32), w2_words.rearrange("e s p b -> p (e s) b").bitcast(I32))
 
         gathered = {}
@@ -149,6 +160,7 @@ def tile_moe_pre_mlp_gelu_kernel(
 
         def first_pass(e0, e1, s):
             for e in range(e0, e1):
+                group = [g for g in SCALE_GROUPS if g[0] == s and g[1] <= e < g[2]][0]
                 if s == 0:
                     sums[e] = psum.tile([P, H], F32, name="sums", tag="bank%d" % e)
                 nc.tensor.matmul_mx(
@@ -156,7 +168,7 @@ def tile_moe_pre_mlp_gelu_kernel(
                     lhsT=x_codes[e, s][0].bitcast(FP8X4),
                     lhsT_scale=x_codes[e, s][1],
                     rhs=w1_codes[s][:, e, :].bitcast(FP4X4),
-                    rhs_scale=w1_bytes[:, e, s, :],
+                    rhs_scale=w1_bytes[group][:, e - group[1], :],
                     start=s == 0,
                     stop=s == PASSES - 1,
                 )
@@ -168,7 +180,7 @@ def tile_moe_pre_mlp_gelu_kernel(
 
         def turn(i):
             e0, e1 = TURNS[i]
-            turned = psum.tile([P, e1 - e0, 2, C], F32, name="turned", tag="bank%d" % e0)
+            turned = psum.tile([P, e1 - e0, 2, C], F32, name="turned", tag="bank%d" % (e1 - 1))
             for e in range(e0, e1):
                 words = h_rows[e].rearrange("c u p v -> c (u p v)").bitcast(F32)
                 for u in range(2):

@@ -28,12 +28,11 @@ ADD = mybir.AluOpType.add
 COPY = mybir.ActivationFunctionType.Copy
 GELU = mybir.ActivationFunctionType.Gelu_apprx_tanh
 
-OWN = [(4, 8, 0), (7, 8, 1)]
-LENT = [(0, 4, 0), (0, 4, 1), (4, 6, 1), (6, 7, 1)]
-SPARE = 16
+
 TURNS = [(0, 2), (2, 3), (3, 5), (5, 6), (6, 7), (7, 8)]
 LAST = E - 1
 SCALE_GROUPS = [(0, 0, E), (1, 0, 4), (1, 4, E)]
+PAIR = 2 * C * PACK
 
 
 def tile_moe_pre_mlp_gelu_kernel(
@@ -46,15 +45,10 @@ def tile_moe_pre_mlp_gelu_kernel(
 
         offs_sb = keep.tile([P, SLOTS // LIST], U16, name="offs_sb")
         pos_sb = [keep.tile([P, T // LIST], U16, name="pos%d_sb" % r) for r in range(2)]
-        tokens = [
-            [
-                keep.tile([P, T + SPARE], F32, name="tokens_%d_%d" % (s, d), align_bytes=64)
-                for d in range(PACK)
-            ]
-            for s in range(PASSES)
-        ]
-        gate_sb = keep.tile([P, SLOTS // 2], F32, name="gate_sb")
-        gate_cols = keep.tile([P, E // 2], F32, name="gate_cols")
+        tokens = [keep.tile([P, T], F32, name="tokens%d" % j, align_bytes=64) for j in range(PASSES * PACK)]
+        gate_first = keep.tile([P, 2 * C], F32, name="gate_first")
+        gate_last = keep.tile([P, 2 * C], F32, name="gate_last")
+        gate_cols = [keep.tile([P, 2], F32, name=name, align_bytes=64) for name in ("last0", "late1")]
         w1_codes = [keep.tile([P, E, 2 * H], U8, name="w1_codes%d" % s, align_bytes=64) for s in range(PASSES)]
         w1_bytes = {
             group: keep.tile([P, group[2] - group[1], H], U8, name="w1_bytes%d_%d" % group[:2], align_bytes=64)
@@ -65,29 +59,37 @@ def tile_moe_pre_mlp_gelu_kernel(
         y = [keep.tile([P, SLOTS], F32, name="y%d" % c) for c in range(CHUNKS)]
         ident = keep.tile([P, P], F32, name="ident")
         warm = keep.tile([P, 2], F32, name="warm")
+        rounded = keep.tile([P, 3 * PAIR], BF16, name="rounded", align_bytes=64)
 
         nc.vector.memset(warm[:, 0:1], 0.0)
         nc.scalar.activation(warm[:, 1:2], warm[:, 0:1], GELU)
-        for row in tokens:
-            for tile in row:
-                nc.gpsimd.memset(tile[:, T:], 0.0)
         make_identity(nc, ident[:])
         for tile in [w1_bytes[group] for group in SCALE_GROUPS]:
             nc.vector.memset(tile[:].rearrange("p e i -> p (e i)").bitcast(I32), 0)
         nc.gpsimd.memset(w2_bytes[:].rearrange("p e n -> p (e n)").bitcast(I32), 0)
 
         x_rows = xT.rearrange("(s p d) t -> s d p t", s=PASSES, d=PACK)
-        half_slots = SLOTS // 2
-        nc.sync.dma_start(tokens[0][0][:, 0:T], x_rows[0, 0])
+
+        def load_plane(s, d):
+            j = PACK * s + d
+            nc.sync.dma_start(tokens[j][:], x_rows[s, d])
+
+        def load_cols(n):
+            with nc.allow_non_contiguous_dma(reason="one weight for each partition and expert"):
+                rows = gate[0, (2 + 2 * n) * C : (4 + 2 * n) * C]
+                nc.sync.dma_start(gate_cols[n][:], rows.rearrange("(e p) -> p e", p=P))
+
+        load_plane(0, 0)
         nc.sync.dma_start(offs_sb[:], offs)
-        for a, b in ((half_slots, half_slots + C), (half_slots + C, SLOTS)):
-            nc.sync.dma_start(gate_sb[:, a - half_slots : b - half_slots], gate[0:P, a:b])
-        for s in range(PASSES):
-            for d in range(PACK):
-                if s or d:
-                    nc.sync.dma_start(tokens[s][d][:, 0:T], x_rows[s, d])
-        with nc.allow_non_contiguous_dma(reason="one weight for each partition and expert"):
-            nc.sync.dma_start(gate_cols[:], gate[0, 0:half_slots].rearrange("(e p) -> p e", p=P))
+        for d in range(1, PACK):
+            load_plane(0, d)
+        load_cols(0)
+        nc.sync.dma_start(gate_first[:], gate[0:P, 0 : 2 * C])
+        for d in range(PACK):
+            load_plane(1, d)
+        nc.sync.dma_start(gate_last[:], gate[0:P, 6 * C : SLOTS])
+        load_cols(1)
+
         def load_scales(tile, rows):
             for r in range(4):
                 nc.sync.dma_start(tile[r:P:32].bitcast(I32), rows[r:16:4].bitcast(I32))
@@ -101,16 +103,15 @@ def tile_moe_pre_mlp_gelu_kernel(
             load_scales(w1_bytes[s, e0, e1][:], w1_rows[s, :, e0:e1])
         nc.sync.dma_start(pos_sb[0][:], pos1)
         nc.sync.dma_start(pos_sb[1][:], pos2)
-        for e0, e1 in ((4, LAST), (2, 4), (0, 2), (LAST, E)):
+        for e0, e1 in ((0, 2), (2, 4), (4, LAST)):
             load_w1(0, e0, e1)
         load_w1(1, 0, 4)
+        load_w1(0, LAST, E)
         load_scales(w1_bytes[SCALE_GROUPS[2]][:], w1_rows[1, :, 4:E])
         load_w1(1, 4, E)
         load_scales(w2_bytes[:], w2_scales.rearrange("e s q n -> q (e s) n"))
         nc.sync.dma_start(w2_codes[:].bitcast(I32), w2_words.rearrange("e s p b -> p (e s) b").bitcast(I32))
 
-        gathered = {}
-        rounded = {}
         x_codes = {}
         h_codes = {}
         sums = {}
@@ -118,44 +119,37 @@ def tile_moe_pre_mlp_gelu_kernel(
         h_turned = {}
         h_woven = {}
 
-        def gather(unit, flat):
-            e0, e1, s = unit
-            lo, hi = e0 * C, e1 * C
-            g = flat.rearrange("p (d c) -> p d c", d=PACK)
-            for d in range(PACK):
-                cuts = [lo, lo + C, hi] if unit == OWN[0] and d == 0 else [lo, hi]
-                for a, b in zip(cuts, cuts[1:]):
-                    picked_tokens = tokens[s][d][:].indirect(offs_sb[:, a // LIST : b // LIST])
-                    if unit in OWN:
-                        nc.vector.tensor_tensor(g[:, d, a - lo : b - lo], picked_tokens, gate_sb[:, a - half_slots : b - half_slots], MULT)
-                    else:
-                        nc.scalar.activation(g[:, d, :], picked_tokens, COPY)
-            for e in range(e0, e1):
-                gathered[e, s] = (g, (e - e0) * C)
+        def staging(name, experts, tag=None):
+            flat = keep.tile([P, PACK * experts * C], F32, name=name, tag=tag or name, align_bytes=64)
+            return flat[:].rearrange("p (d c) -> p d c", d=PACK)
 
-        def interleave(e0, e1, s):
-            slots = (e1 - e0) * C
-            xb = keep.tile([P, slots, PACK], BF16, name="rounded%d_%d" % (e0, s), align_bytes=64)
-            g, lo = gathered[e0, s]
-            dst = xb[:].rearrange("p (c i) d -> p c d i", i=4)
-            src = g[:, :, lo : lo + slots].rearrange("p d (c i) -> p c d i", i=4)
-            if any(s == s1 and a <= e0 < b for a, b, s1 in OWN):
-                nc.vector.tensor_copy(dst, src)
+        def gather(engine, g, e0, e1, s, d):
+            picked_tokens = tokens[PACK * s + d][:].indirect(offs_sb[:, e0 * C // LIST : e1 * C // LIST])
+            if engine == "vector":
+                nc.vector.tensor_copy(g, picked_tokens)
             else:
-                spread = gate_bank if e0 < E // 2 else gate_sb
-                first = e0 * C % half_slots
-                weights = spread[:, first : first + slots].rearrange("p (c o i) -> p c o i", o=1, i=4)
-                nc.vector.tensor_tensor(dst, src, weights.broadcast_to([P, slots // 4, PACK, 4]), MULT)
-            rounded[e0, s] = xb
+                nc.scalar.activation(g, picked_tokens, COPY)
 
-        def quantise_x(e0, e1, s):
-            xc = keep.tile([P, (e1 - e0) * C], U32, name="codes%d_%d" % (e0, s), align_bytes=64)
-            xs = keep.tile([P, (e1 - e0) * C], U8, name="bytes%d_%d" % (e0, s), align_bytes=64)
-            for e in range(e0, e1):
-                cols = slice((e - e0) * C, (e - e0 + 1) * C)
-                x_codes[e, s] = (xc[:, cols], xs[:, cols])
+        def weigh_on_gpsimd(at, g, weights):
+            slots = g.shape[2]
+            dst = rounded[:, at : at + PACK * slots].rearrange("p (c d) -> p c d", d=PACK)
+            spread = weights.rearrange("p (c o) -> p c o", o=1).broadcast_to([P, slots, PACK])
+            nc.gpsimd.tensor_tensor(dst, g.rearrange("p d c -> p c d"), spread, MULT)
+
+        def weigh_on_vector(at, g, weights):
+            slots = g.shape[2]
+            dst = rounded[:, at : at + PACK * slots].rearrange("p (c i d) -> p c d i", i=4, d=PACK)
+            spread = weights.rearrange("p (c o i) -> p c o i", o=1, i=4).broadcast_to([P, slots // 4, PACK, 4])
+            nc.vector.tensor_tensor(dst, g.rearrange("p d (c i) -> p c d i", i=4), spread, MULT)
+
+        def quantise_x(at, experts, s):
+            name = "%d_%d" % (experts[0], s)
+            xc = keep.tile([P, len(experts) * C], U32, name="codes" + name, align_bytes=64)
+            xs = keep.tile([P, len(experts) * C], U8, name="bytes" + name, align_bytes=64)
+            for n, e in enumerate(experts):
+                x_codes[e, s] = (xc[:, n * C : (n + 1) * C], xs[:, n * C : (n + 1) * C])
             nc.vector.quantize_mx(
-                out=xc[:].bitcast(FP8X4), scales=xs[:], in_=rounded[e0, s][:].rearrange("p c d -> p (c d)")
+                out=xc[:].bitcast(FP8X4), scales=xs[:], in_=rounded[:, at : at + PACK * len(experts) * C]
             )
 
         def first_pass(e0, e1, s):
@@ -222,38 +216,42 @@ def tile_moe_pre_mlp_gelu_kernel(
 
         on_scalar, on_vector = nc.scalar.copy, nc.vector.tensor_copy
 
-        def staging(name, tag):
-            return keep.tile([P, PACK * half_slots], F32, name=name, tag=tag, align_bytes=64)
+        gate_bank = psum.tile([P, 4 * C], F32, name="gate_bank", tag="bank%d" % LAST)
+        for e in range(4):
+            nc.tensor.transpose(gate_bank[:, e * C : (e + 1) * C], gate_cols[e // 2][:, e % 2 : e % 2 + 1].to_broadcast([P, P]), ident[:])
 
-        gate_bank = psum.tile([P, half_slots], F32, name="gate_bank", tag="bank%d" % LAST)
-        for e in range(E // 2):
-            nc.tensor.transpose(gate_bank[:, e * C : (e + 1) * C], gate_cols[:, e : e + 1].to_broadcast([P, P]), ident[:])
-        gather(LENT[0], staging("gathered_first", "gathered_first")[:])
-        gather(OWN[0], staging("gathered_own", "gathered_own")[:])
-        gather(LENT[1], staging("gathered_second", "gathered_second")[:])
-        for first in (4, 0):
-            interleave(first, first + 2, 0)
-            interleave(first + 2, first + 4, 0)
-            quantise_x(first, first + 2, 0)
-            quantise_x(first + 2, first + 4, 0)
-            first_pass(first, min(first + 4, LAST), 0)
-        late = staging("gathered_late", "gathered_first")
-        for e0, e1, s in LENT[2:]:
-            gather((e0, e1, s), late[:, PACK * (e0 * C - half_slots) : PACK * (e1 * C - half_slots)])
-        interleave(0, 2, 1)
-        interleave(2, 4, 1)
-        quantise_x(0, 2, 1)
+        first0, last0, middle0 = staging("first0", 2), staging("last0", 2), staging("middle0", 4)
+        for d in range(PACK):
+            gather("vector", first0[:, d, :], 0, 2, 0, d)
+            gather("scalar", middle0[:, d, 0 : 2 * C], 2, 4, 0, d)
+            gather("scalar", middle0[:, d, 2 * C : 4 * C], 4, 6, 0, d)
+        for d in range(PACK):
+            gather("vector", last0[:, d, :], 6, E, 0, d)
+        half_pair = PAIR // 2
+        weigh_on_gpsimd(half_pair, first0, gate_first[:])
+        quantise_x(half_pair, [0, 1], 0)
+        weigh_on_gpsimd(0, last0, gate_last[:])
+        weigh_on_vector(PAIR, middle0, gate_bank[:])
+        quantise_x(0, [6, 7, 2, 3], 0)
+        quantise_x(2 * PAIR, [4, 5], 0)
+        first_pass(0, LAST, 0)
+        first1, second1, late1 = staging("first1", 2), staging("second1", 2), staging("late1", 3)
+        third1, seventh1, sixth1 = late1[:, :, 0 : 2 * C], late1[:, :, 2 * C :], staging("sixth1", 1, tag="middle0")
+        for g, e0, e1 in ((first1, 0, 2), (second1, 2, 4), (third1, 4, 6), (seventh1, LAST, E)):
+            for d in range(PACK):
+                gather("scalar", g[:, d, :], e0, e1, 1, d)
+        for d in range(PACK):
+            gather("vector", sixth1[:, d, :], 6, LAST, 1, d)
+        weigh_on_gpsimd(3 * half_pair, first1, gate_first[:])
+        weigh_on_vector(half_pair, second1, gate_bank[:, 0 : 2 * C])
+        quantise_x(half_pair, [2, 3, 0, 1], 1)
+        first_pass(0, 4, 1)
+        weigh_on_gpsimd(3 * half_pair, sixth1, gate_last[:, 0:C])
+        weigh_on_vector(half_pair, third1, gate_bank[:, 2 * C : 4 * C])
+        weigh_on_vector(2 * PAIR, seventh1, gate_last[:, C : 2 * C])
+        quantise_x(half_pair, [4, 5], 1)
+        quantise_x(3 * half_pair, [6, 7], 1)
         first_pass(LAST, E, 0)
-        first_pass(0, 2, 1)
-        interleave(4, 6, 1)
-        quantise_x(2, 4, 1)
-        first_pass(2, 4, 1)
-        interleave(6, LAST, 1)
-        quantise_x(4, 6, 1)
-        gather(OWN[1], keep.tile([P, PACK * C], F32, name="gathered_last", tag="rounded2_1", align_bytes=64)[:])
-        quantise_x(6, LAST, 1)
-        interleave(LAST, E, 1)
-        quantise_x(LAST, E, 1)
         for i, (e0, e1) in enumerate(TURNS):
             for e in range(e0, e1):
                 activate(e)

@@ -31,7 +31,8 @@ GELU = mybir.ActivationFunctionType.Gelu_apprx_tanh
 
 TURNS = [(0, 2), (2, 3), (3, 5), (5, 6), (6, 7), (7, 8)]
 LAST = E - 1
-SCALE_GROUPS = [(0, 0, E), (1, 0, 4), (1, 4, E)]
+SCALE_GROUPS = [(0, 0, E), (1, 0, E)]
+EARLY = 3
 PAIR = 2 * C * PACK
 
 
@@ -56,7 +57,6 @@ def tile_moe_pre_mlp_gelu_kernel(
         }
         w2_codes = keep.tile([P, E, 2 * N], U8, name="w2_codes", align_bytes=64)
         w2_bytes = keep.tile([P, E, N], U8, name="w2_bytes", align_bytes=64)
-        y = [keep.tile([P, SLOTS], F32, name="y%d" % c) for c in range(CHUNKS)]
         ident = keep.tile([P, P], F32, name="ident")
         warm = keep.tile([P, 2], F32, name="warm")
         rounded = keep.tile([P, 3 * PAIR], BF16, name="rounded", align_bytes=64)
@@ -99,18 +99,19 @@ def tile_moe_pre_mlp_gelu_kernel(
 
         w1_rows = w1_scales.rearrange("e s q i -> s q e i")
         w1_passes = w1_words.rearrange("e s p b -> s p e b")
-        for s, e0, e1 in SCALE_GROUPS[:2]:
+        for s, e0, e1 in SCALE_GROUPS:
             load_scales(w1_bytes[s, e0, e1][:], w1_rows[s, :, e0:e1])
+        load_scales(w2_bytes[:], w2_scales.rearrange("e s q n -> q (e s) n"))
         nc.sync.dma_start(pos_sb[0][:], pos1)
         nc.sync.dma_start(pos_sb[1][:], pos2)
         for e0, e1 in ((0, 2), (2, 4), (4, LAST)):
             load_w1(0, e0, e1)
         load_w1(1, 0, 4)
         load_w1(0, LAST, E)
-        load_scales(w1_bytes[SCALE_GROUPS[2]][:], w1_rows[1, :, 4:E])
         load_w1(1, 4, E)
-        load_scales(w2_bytes[:], w2_scales.rearrange("e s q n -> q (e s) n"))
-        nc.sync.dma_start(w2_codes[:].bitcast(I32), w2_words.rearrange("e s p b -> p (e s) b").bitcast(I32))
+        w2_rows = w2_words.rearrange("e s p b -> p (e s) b")
+        for e0, e1 in ((0, EARLY), (EARLY, E)):
+            nc.sync.dma_start(w2_codes[:, e0:e1].bitcast(I32), w2_rows[:, e0:e1].bitcast(I32))
 
         x_codes = {}
         h_codes = {}
@@ -202,7 +203,7 @@ def tile_moe_pre_mlp_gelu_kernel(
 
         def second_product(chunk, e0, e1, bank, copy):
             acc = psum.tile([P, (e1 - e0) * C], F32, name="acc", tag="bank%d" % bank)
-            for e in range(e0, e1) if e0 == 0 else reversed(range(e0, e1)):
+            for e in range(e0, e1):
                 nc.tensor.matmul_mx(
                     out=acc[:, (e - e0) * C : (e - e0 + 1) * C],
                     lhsT=w2_codes[:, e, 2 * P * chunk : 2 * P * (chunk + 1)].bitcast(FP4X4),
@@ -258,16 +259,19 @@ def tile_moe_pre_mlp_gelu_kernel(
             turn(i)
             if i == 1:
                 first_pass(4, E, 1)
-            weave(i, on_vector if e1 < LAST - 1 else on_scalar)
+            weave(i, on_vector if e1 < LAST else on_scalar)
             if i:
                 quantise_h(i - 1)
         quantise_h(len(TURNS) - 1)
-        second_product(0, 0, 4, 6, on_scalar)
-        second_product(0, 4, LAST, 0, on_vector)
-        second_product(0, LAST, E, 2, on_scalar)
-        second_product(1, 0, 4, LAST, on_vector)
-        second_product(1, 4, E, 4, on_vector)
-        second_product(2, 6, E, 1, on_vector)
+        y = [keep.tile([P, SLOTS], F32, name="y%d" % c) for c in range(CHUNKS)]
+        for chunk in range(CHUNKS):
+            second_product(chunk, 0, EARLY, chunk, on_vector)
+        second_product(0, EARLY, 6, 3, on_scalar)
+        second_product(2, EARLY, 6, 5, on_scalar)
+        second_product(0, 6, E, 6, on_scalar)
+        second_product(1, EARLY, 6, 4, on_vector)
+        second_product(1, 6, E, LAST, on_vector)
+        second_product(2, 6, E, 0, on_vector)
 
         picked = [keep.tile([P, T], F32, name="picked%d" % c) for c in range(CHUNKS)]
         summed = [keep.tile([P, T], F32, name="summed%d" % c) for c in range(CHUNKS)]
@@ -282,8 +286,6 @@ def tile_moe_pre_mlp_gelu_kernel(
                 nc.sync.dma_start(out[chunk * P : (chunk + 1) * P, a:b], summed[chunk][:, a:b])
 
         half = T // 2
-        combine(0, [0, T])
-        combine(1, [0, T])
-        second_product(2, 0, 4, 4, on_scalar)
-        second_product(2, 4, 6, 6, on_scalar)
+        combine(0, [0, half, T])
+        combine(1, [0, half, T])
         combine(2, [0, half, T - T // 8, T])

@@ -33,6 +33,8 @@ TURNS = [(0, 2), (2, 3), (3, 5), (5, 6), (6, 7), (7, 8)]
 LAST = E - 1
 SCALE_GROUPS = [(0, 0, E), (1, 0, E)]
 EARLY = 3
+W1_LOADS = [slice(0, 8, 2), slice(12, 13), slice(1, 8, 2), slice(8, 15, 6), slice(9, 12), slice(13, 16, 2)]
+UNIT = C * PACK
 PAIR = 2 * C * PACK
 
 
@@ -50,7 +52,7 @@ def tile_moe_pre_mlp_gelu_kernel(
         gate_first = keep.tile([P, 2 * C], F32, name="gate_first")
         gate_last = keep.tile([P, 2 * C], F32, name="gate_last")
         gate_cols = [keep.tile([P, 2], F32, name=name, align_bytes=64) for name in ("last0", "late1")]
-        w1_codes = [keep.tile([P, E, 2 * H], U8, name="w1_codes%d" % s, align_bytes=64) for s in range(PASSES)]
+        w1_codes = keep.tile([P, E * PASSES, 2 * H], U8, name="w1_codes", align_bytes=64)
         w1_bytes = {
             group: keep.tile([P, group[2] - group[1], H], U8, name="w1_bytes%d_%d" % group[:2], align_bytes=64)
             for group in SCALE_GROUPS
@@ -59,7 +61,7 @@ def tile_moe_pre_mlp_gelu_kernel(
         w2_bytes = keep.tile([P, E, N], U8, name="w2_bytes", align_bytes=64)
         ident = keep.tile([P, P], F32, name="ident")
         warm = keep.tile([P, 2], F32, name="warm")
-        rounded = keep.tile([P, 3 * PAIR], BF16, name="rounded", align_bytes=64)
+        rounded = keep.tile([P, 4 * PAIR], BF16, name="rounded", align_bytes=64)
 
         nc.vector.memset(warm[:, 0:1], 0.0)
         nc.scalar.activation(warm[:, 1:2], warm[:, 0:1], GELU)
@@ -76,7 +78,7 @@ def tile_moe_pre_mlp_gelu_kernel(
 
         def load_cols(n):
             with nc.allow_non_contiguous_dma(reason="one weight for each partition and expert"):
-                rows = gate[0, (2 + 2 * n) * C : (4 + 2 * n) * C]
+                rows = gate[0, 4 * n * C : (4 * n + 2) * C]
                 nc.sync.dma_start(gate_cols[n][:], rows.rearrange("(e p) -> p e", p=P))
 
         load_plane(0, 0)
@@ -84,31 +86,28 @@ def tile_moe_pre_mlp_gelu_kernel(
         for d in range(1, PACK):
             load_plane(0, d)
         load_cols(0)
-        nc.sync.dma_start(gate_first[:], gate[0:P, 0 : 2 * C])
+        nc.sync.dma_start(gate_first[:], gate[0:P, 2 * C : 4 * C])
         for d in range(PACK):
             load_plane(1, d)
-        nc.sync.dma_start(gate_last[:], gate[0:P, 6 * C : SLOTS])
         load_cols(1)
+        nc.sync.dma_start(gate_last[:], gate[0:P, 6 * C : SLOTS])
 
         def load_scales(tile, rows):
             for r in range(4):
                 nc.sync.dma_start(tile[r:P:32].bitcast(I32), rows[r:16:4].bitcast(I32))
 
-        def load_w1(s, e0, e1):
-            nc.sync.dma_start(w1_codes[s][:, e0:e1].bitcast(I32), w1_passes[s, :, e0:e1].bitcast(I32))
+        def load_w1(passes):
+            nc.sync.dma_start(w1_codes[:, passes].bitcast(I32), w1_passes[:, passes].bitcast(I32))
 
         w1_rows = w1_scales.rearrange("e s q i -> s q e i")
-        w1_passes = w1_words.rearrange("e s p b -> s p e b")
+        w1_passes = w1_words.rearrange("e s p b -> p (e s) b")
         for s, e0, e1 in SCALE_GROUPS:
             load_scales(w1_bytes[s, e0, e1][:], w1_rows[s, :, e0:e1])
         load_scales(w2_bytes[:], w2_scales.rearrange("e s q n -> q (e s) n"))
         nc.sync.dma_start(pos_sb[0][:], pos1)
         nc.sync.dma_start(pos_sb[1][:], pos2)
-        for e0, e1 in ((0, 2), (2, 4), (4, LAST)):
-            load_w1(0, e0, e1)
-        load_w1(1, 0, 4)
-        load_w1(0, LAST, E)
-        load_w1(1, 4, E)
+        for passes in W1_LOADS:
+            load_w1(passes)
         w2_rows = w2_words.rearrange("e s p b -> p (e s) b")
         for e0, e1 in ((0, EARLY), (EARLY, E)):
             nc.sync.dma_start(w2_codes[:, e0:e1].bitcast(I32), w2_rows[:, e0:e1].bitcast(I32))
@@ -131,27 +130,24 @@ def tile_moe_pre_mlp_gelu_kernel(
             else:
                 nc.scalar.activation(g, picked_tokens, COPY)
 
-        def weigh_on_gpsimd(at, g, weights):
+        def weigh_on_gpsimd(xb, g, weights):
             slots = g.shape[2]
-            dst = rounded[:, at : at + PACK * slots].rearrange("p (c d) -> p c d", d=PACK)
             spread = weights.rearrange("p (c o) -> p c o", o=1).broadcast_to([P, slots, PACK])
-            nc.gpsimd.tensor_tensor(dst, g.rearrange("p d c -> p c d"), spread, MULT)
+            nc.gpsimd.tensor_tensor(xb.rearrange("p (c d) -> p c d", d=PACK), g.rearrange("p d c -> p c d"), spread, MULT)
 
-        def weigh_on_vector(at, g, weights):
+        def weigh_on_vector(xb, g, weights):
             slots = g.shape[2]
-            dst = rounded[:, at : at + PACK * slots].rearrange("p (c i d) -> p c d i", i=4, d=PACK)
+            dst = xb.rearrange("p (c i d) -> p c d i", i=4, d=PACK)
             spread = weights.rearrange("p (c o i) -> p c o i", o=1, i=4).broadcast_to([P, slots // 4, PACK, 4])
             nc.vector.tensor_tensor(dst, g.rearrange("p d (c i) -> p c d i", i=4), spread, MULT)
 
-        def quantise_x(at, experts, s):
-            name = "%d_%d" % (experts[0], s)
-            xc = keep.tile([P, len(experts) * C], U32, name="codes" + name, align_bytes=64)
-            xs = keep.tile([P, len(experts) * C], U8, name="bytes" + name, align_bytes=64)
-            for n, e in enumerate(experts):
-                x_codes[e, s] = (xc[:, n * C : (n + 1) * C], xs[:, n * C : (n + 1) * C])
-            nc.vector.quantize_mx(
-                out=xc[:].bitcast(FP8X4), scales=xs[:], in_=rounded[:, at : at + PACK * len(experts) * C]
-            )
+        def quantise_x(xb, units, tag=None):
+            name = "%d_%d" % units[0]
+            xc = keep.tile([P, len(units) * C], U32, name="codes" + name, tag=tag or "codes" + name, align_bytes=64)
+            xs = keep.tile([P, len(units) * C], U8, name="bytes" + name, align_bytes=64)
+            for n, unit in enumerate(units):
+                x_codes[unit] = (xc[:, n * C : (n + 1) * C], xs[:, n * C : (n + 1) * C])
+            nc.vector.quantize_mx(out=xc[:].bitcast(FP8X4), scales=xs[:], in_=xb)
 
         def first_pass(e0, e1, s):
             for e in range(e0, e1):
@@ -162,7 +158,7 @@ def tile_moe_pre_mlp_gelu_kernel(
                     out=sums[e][:],
                     lhsT=x_codes[e, s][0].bitcast(FP8X4),
                     lhsT_scale=x_codes[e, s][1],
-                    rhs=w1_codes[s][:, e, :].bitcast(FP4X4),
+                    rhs=w1_codes[:, PASSES * e + s, :].bitcast(FP4X4),
                     rhs_scale=w1_bytes[group][:, e - group[1], :],
                     start=s == 0,
                     stop=s == PASSES - 1,
@@ -221,44 +217,55 @@ def tile_moe_pre_mlp_gelu_kernel(
         for e in range(4):
             nc.tensor.transpose(gate_bank[:, e * C : (e + 1) * C], gate_cols[e // 2][:, e % 2 : e % 2 + 1].to_broadcast([P, P]), ident[:])
 
-        first0, last0, middle0 = staging("first0", 2), staging("last0", 2), staging("middle0", 4)
+        def units(tile, a, b):
+            return tile[:, a * UNIT : b * UNIT]
+
+        a0, b0, d0 = staging("a0", 2), staging("last0", 2), staging("d0", 2)
         for d in range(PACK):
-            gather("vector", first0[:, d, :], 0, 2, 0, d)
-            gather("scalar", middle0[:, d, 0 : 2 * C], 2, 4, 0, d)
-            gather("scalar", middle0[:, d, 2 * C : 4 * C], 4, 6, 0, d)
+            gather("vector", d0[:, d, :], 2, 4, 0, d)
+            gather("scalar", a0[:, d, :], 0, 2, 0, d)
         for d in range(PACK):
-            gather("vector", last0[:, d, :], 6, E, 0, d)
-        half_pair = PAIR // 2
-        weigh_on_gpsimd(half_pair, first0, gate_first[:])
-        quantise_x(half_pair, [0, 1], 0)
-        weigh_on_gpsimd(0, last0, gate_last[:])
-        weigh_on_vector(PAIR, middle0, gate_bank[:])
-        quantise_x(0, [6, 7, 2, 3], 0)
-        quantise_x(2 * PAIR, [4, 5], 0)
-        first_pass(0, LAST, 0)
-        first1, second1, late1 = staging("first1", 2), staging("second1", 2), staging("late1", 3)
-        third1, seventh1, sixth1 = late1[:, :, 0 : 2 * C], late1[:, :, 2 * C :], staging("sixth1", 1, tag="middle0")
-        for g, e0, e1 in ((first1, 0, 2), (second1, 2, 4), (third1, 4, 6), (seventh1, LAST, E)):
+            gather("vector", b0[:, d, :], 6, E, 0, d)
+        a1 = staging("a1", 2)
+        late = keep.tile([P, 5 * PAIR], F32, name="late", tag="late1", align_bytes=64)
+        d1, c1, c0 = [late[:, n * PAIR : (n + 1) * PAIR].rearrange("p (d c) -> p d c", d=PACK) for n in range(3)]
+        late_rounded = late[:, 3 * PAIR - UNIT // 2 :].bitcast(BF16)
+        for g, e0, s in ((a1, 0, 1), (d1, 2, 1), (c0, 4, 0), (c1, 4, 1)):
             for d in range(PACK):
-                gather("scalar", g[:, d, :], e0, e1, 1, d)
+                gather("scalar", g[:, d, :], e0, e0 + 2, s, d)
+        weigh_on_gpsimd(units(rounded, 3, 5), d0, gate_first[:])
+        weigh_on_gpsimd(units(rounded, 5, 7), b0, gate_last[:])
+        weigh_on_vector(units(rounded, 1, 3), a0, gate_bank[:, 0 : 2 * C])
+        weigh_on_vector(units(rounded, 0, 1), a1[:, :, 0:C], gate_bank[:, 0:C])
+        weigh_on_vector(units(rounded, 7, 8), a1[:, :, C:], gate_bank[:, C : 2 * C])
+        quantise_x(units(rounded, 0, 4), [(0, 1), (0, 0), (1, 0), (2, 0)])
+        weigh_on_gpsimd(units(late_rounded, 1, 3), d1, gate_first[:])
+        b1 = staging("b1", 2, tag="a1")
         for d in range(PACK):
-            gather("vector", sixth1[:, d, :], 6, LAST, 1, d)
-        weigh_on_gpsimd(3 * half_pair, first1, gate_first[:])
-        weigh_on_vector(half_pair, second1, gate_bank[:, 0 : 2 * C])
-        quantise_x(half_pair, [2, 3, 0, 1], 1)
+            gather("vector", b1[:, d, :], 6, E, 1, d)
+        quantise_x(units(rounded, 4, 8), [(3, 0), (6, 0), (7, 0), (1, 1)], tag="tokens3")
+        weigh_on_gpsimd(units(late_rounded, 5, 6), b1[:, :, 0:C], gate_last[:, 0:C])
+        weigh_on_vector(units(late_rounded, 3, 4), c0[:, :, 0:C], gate_bank[:, 2 * C : 3 * C])
+        weigh_on_vector(units(late_rounded, 4, 5), c0[:, :, C:], gate_bank[:, 3 * C :])
+        quantise_x(units(late_rounded, 1, 4), [(2, 1), (3, 1), (4, 0)])
+        weigh_on_gpsimd(units(late_rounded, 0, 1), b1[:, :, C:], gate_last[:, C:])
+        weigh_on_vector(units(late_rounded, 3, 4), c1[:, :, 0:C], gate_bank[:, 2 * C : 3 * C])
+        weigh_on_vector(units(late_rounded, 1, 2), c1[:, :, C:], gate_bank[:, 3 * C :])
+        quantise_x(units(late_rounded, 3, 6), [(4, 1), (5, 0), (6, 1)])
+        quantise_x(units(late_rounded, 0, 2), [(7, 1), (5, 1)])
+        first_pass(0, 4, 0)
+        first_pass(6, LAST, 0)
         first_pass(0, 4, 1)
-        weigh_on_gpsimd(3 * half_pair, sixth1, gate_last[:, 0:C])
-        weigh_on_vector(half_pair, third1, gate_bank[:, 2 * C : 4 * C])
-        weigh_on_vector(2 * PAIR, seventh1, gate_last[:, C : 2 * C])
-        quantise_x(half_pair, [4, 5], 1)
-        quantise_x(3 * half_pair, [6, 7], 1)
+        first_pass(4, 5, 0)
         first_pass(LAST, E, 0)
         for i, (e0, e1) in enumerate(TURNS):
             for e in range(e0, e1):
                 activate(e)
             turn(i)
             if i == 1:
-                first_pass(4, E, 1)
+                first_pass(4, 5, 1)
+                first_pass(5, 6, 0)
+                first_pass(5, E, 1)
             weave(i, on_vector if e1 < LAST else on_scalar)
             if i:
                 quantise_h(i - 1)

@@ -33,7 +33,7 @@ TURNS = [(0, 2), (2, 3), (3, 5), (5, 6), (6, 7), (7, 8)]
 LAST = E - 1
 SCALE_GROUPS = [(0, 0, E), (1, 0, E)]
 EARLY = 3
-W1_LOADS = [slice(0, 8, 2), slice(12, 13), slice(1, 8, 2), slice(8, 15, 6), slice(9, 12), slice(13, 16, 2)]
+W1_LOADS = [slice(0, 8, 2), slice(12, 13), slice(1, 8, 2), slice(8, 11, 2), slice(9, 16, 2), slice(14, 15)]
 UNIT = C * PACK
 PAIR = 2 * C * PACK
 
@@ -87,10 +87,11 @@ def tile_moe_pre_mlp_gelu_kernel(
             load_plane(0, d)
         load_cols(0)
         nc.sync.dma_start(gate_first[:], gate[0:P, 2 * C : 4 * C])
-        for d in range(PACK):
+        load_plane(1, 0)
+        nc.sync.dma_start(gate_last[:], gate[0:P, 6 * C : SLOTS])
+        for d in range(1, PACK):
             load_plane(1, d)
         load_cols(1)
-        nc.sync.dma_start(gate_last[:], gate[0:P, 6 * C : SLOTS])
 
         def load_scales(tile, rows):
             for r in range(4):
@@ -152,7 +153,8 @@ def tile_moe_pre_mlp_gelu_kernel(
         def first_pass(e0, e1, s):
             for e in range(e0, e1):
                 group = [g for g in SCALE_GROUPS if g[0] == s and g[1] <= e < g[2]][0]
-                if s == 0:
+                opens = e not in sums
+                if opens:
                     sums[e] = psum.tile([P, H], F32, name="sums", tag="bank%d" % e)
                 nc.tensor.matmul_mx(
                     out=sums[e][:],
@@ -160,8 +162,8 @@ def tile_moe_pre_mlp_gelu_kernel(
                     lhsT_scale=x_codes[e, s][1],
                     rhs=w1_codes[:, PASSES * e + s, :].bitcast(FP4X4),
                     rhs_scale=w1_bytes[group][:, e - group[1], :],
-                    start=s == 0,
-                    stop=s == PASSES - 1,
+                    start=opens,
+                    stop=not opens,
                 )
 
         def activate(e):
@@ -213,59 +215,62 @@ def tile_moe_pre_mlp_gelu_kernel(
 
         on_scalar, on_vector = nc.scalar.copy, nc.vector.tensor_copy
 
-        gate_bank = psum.tile([P, 4 * C], F32, name="gate_bank", tag="bank%d" % LAST)
+        gate_banks = [psum.tile([P, 2 * C], F32, name="gate_bank", tag="bank%d" % bank) for bank in (4, LAST)]
         for e in range(4):
-            nc.tensor.transpose(gate_bank[:, e * C : (e + 1) * C], gate_cols[e // 2][:, e % 2 : e % 2 + 1].to_broadcast([P, P]), ident[:])
+            column = gate_cols[e // 2][:, e % 2 : e % 2 + 1]
+            nc.tensor.transpose(gate_banks[e // 2][:, e % 2 * C : (e % 2 + 1) * C], column.to_broadcast([P, P]), ident[:])
 
-        def units(tile, a, b):
-            return tile[:, a * UNIT : b * UNIT]
+        def units(a, b):
+            return rounded[:, int(a * UNIT) : int(b * UNIT)]
 
-        a0, b0, d0 = staging("a0", 2), staging("last0", 2), staging("d0", 2)
+        a0, held, d0 = staging("a0", 2), staging("last0", 3), staging("d0", 2)
+        b0, sixth1 = held[:, :, 0 : 2 * C], held[:, :, 2 * C :]
         for d in range(PACK):
             gather("vector", d0[:, d, :], 2, 4, 0, d)
             gather("scalar", a0[:, d, :], 0, 2, 0, d)
         for d in range(PACK):
             gather("vector", b0[:, d, :], 6, E, 0, d)
-        a1 = staging("a1", 2)
-        late = keep.tile([P, 5 * PAIR], F32, name="late", tag="late1", align_bytes=64)
-        d1, c1, c0 = [late[:, n * PAIR : (n + 1) * PAIR].rearrange("p (d c) -> p d c", d=PACK) for n in range(3)]
-        late_rounded = late[:, 3 * PAIR - UNIT // 2 :].bitcast(BF16)
+        a1, d1 = staging("a1", 2), staging("d1", 2)
+        late = staging("late1", 4)
+        c0, c1 = late[:, :, 0 : 2 * C], late[:, :, 2 * C :]
         for g, e0, s in ((a1, 0, 1), (d1, 2, 1), (c0, 4, 0), (c1, 4, 1)):
             for d in range(PACK):
                 gather("scalar", g[:, d, :], e0, e0 + 2, s, d)
-        weigh_on_gpsimd(units(rounded, 3, 5), d0, gate_first[:])
-        weigh_on_gpsimd(units(rounded, 5, 7), b0, gate_last[:])
-        weigh_on_vector(units(rounded, 1, 3), a0, gate_bank[:, 0 : 2 * C])
-        weigh_on_vector(units(rounded, 0, 1), a1[:, :, 0:C], gate_bank[:, 0:C])
-        weigh_on_vector(units(rounded, 7, 8), a1[:, :, C:], gate_bank[:, C : 2 * C])
-        quantise_x(units(rounded, 0, 4), [(0, 1), (0, 0), (1, 0), (2, 0)])
-        weigh_on_gpsimd(units(late_rounded, 1, 3), d1, gate_first[:])
-        b1 = staging("b1", 2, tag="a1")
+        weigh_on_gpsimd(units(3, 5), d0, gate_first[:])
+        weigh_on_gpsimd(units(5, 7), b0, gate_last[:])
+        weigh_on_vector(units(1, 3), a0, gate_banks[0][:])
         for d in range(PACK):
-            gather("vector", b1[:, d, :], 6, E, 1, d)
-        quantise_x(units(rounded, 4, 8), [(3, 0), (6, 0), (7, 0), (1, 1)], tag="tokens3")
-        weigh_on_gpsimd(units(late_rounded, 5, 6), b1[:, :, 0:C], gate_last[:, 0:C])
-        weigh_on_vector(units(late_rounded, 3, 4), c0[:, :, 0:C], gate_bank[:, 2 * C : 3 * C])
-        weigh_on_vector(units(late_rounded, 4, 5), c0[:, :, C:], gate_bank[:, 3 * C :])
-        quantise_x(units(late_rounded, 1, 4), [(2, 1), (3, 1), (4, 0)])
-        weigh_on_gpsimd(units(late_rounded, 0, 1), b1[:, :, C:], gate_last[:, C:])
-        weigh_on_vector(units(late_rounded, 3, 4), c1[:, :, 0:C], gate_bank[:, 2 * C : 3 * C])
-        weigh_on_vector(units(late_rounded, 1, 2), c1[:, :, C:], gate_bank[:, 3 * C :])
-        quantise_x(units(late_rounded, 3, 6), [(4, 1), (5, 0), (6, 1)])
-        quantise_x(units(late_rounded, 0, 2), [(7, 1), (5, 1)])
+            gather("vector", sixth1[:, d, :], 6, LAST, 1, d)
+        weigh_on_vector(units(0, 1), a1[:, :, 0:C], gate_banks[0][:, 0:C])
+        weigh_on_vector(units(7, 8), a1[:, :, C:], gate_banks[0][:, C:])
+        quantise_x(units(0, 4), [(0, 1), (0, 0), (1, 0), (2, 0)])
+        quantise_x(units(4, 8), [(3, 0), (6, 0), (7, 0), (1, 1)])
+        weigh_on_gpsimd(units(1, 3), d1, gate_first[:])
+        seventh1 = staging("seventh1", 1, tag="a1")
+        for d in range(PACK):
+            gather("vector", seventh1[:, d, :], LAST, E, 1, d)
+        weigh_on_vector(units(4, 6), c0, gate_banks[1][:])
+        quantise_x(units(1, 3), [(2, 1), (3, 1)])
+        quantise_x(units(4, 6), [(4, 0), (5, 0)], tag="d1")
+        weigh_on_gpsimd(units(2.5, 3.5), sixth1, gate_last[:, 0:C])
+        weigh_on_vector(units(0.5, 2.5), c1, gate_banks[1][:])
+        quantise_x(units(0.5, 2.5), [(4, 1), (5, 1)])
+        rounded7 = keep.tile([P, UNIT], BF16, name="rounded7", tag="last0", align_bytes=64)
+        weigh_on_vector(rounded7[:], seventh1, gate_last[:, C:])
+        quantise_x(units(2.5, 3.5), [(6, 1)])
+        quantise_x(rounded7[:], [(7, 1)])
         first_pass(0, 4, 0)
         first_pass(6, LAST, 0)
         first_pass(0, 4, 1)
-        first_pass(4, 5, 0)
-        first_pass(LAST, E, 0)
+        first_pass(4, 6, 0)
         for i, (e0, e1) in enumerate(TURNS):
             for e in range(e0, e1):
                 activate(e)
             turn(i)
             if i == 1:
-                first_pass(4, 5, 1)
-                first_pass(5, 6, 0)
-                first_pass(5, E, 1)
+                first_pass(4, E, 1)
+            if i == 2:
+                first_pass(LAST, E, 0)
             weave(i, on_vector if e1 < LAST else on_scalar)
             if i:
                 quantise_h(i - 1)

@@ -31,7 +31,7 @@ GELU = mybir.ActivationFunctionType.Gelu_apprx_tanh
 
 TURNS = [(0, 2), (2, 3), (3, 5), (5, 6), (6, 7), (7, 8)]
 LAST = E - 1
-SCALE_GROUPS = [(0, 0, E), (1, 0, E)]
+SCALE_GROUPS = [(0, 0, E), (1, 0, 4), (1, 4, E)]
 EARLY = 3
 W1_LOADS = [slice(0, 8, 2), slice(12, 13), slice(1, 8, 2), slice(8, 11, 2), slice(9, 16, 2), slice(14, 15)]
 UNIT = C * PACK
@@ -102,13 +102,16 @@ def tile_moe_pre_mlp_gelu_kernel(
 
         w1_rows = w1_scales.rearrange("e s q i -> s q e i")
         w1_passes = w1_words.rearrange("e s p b -> p (e s) b")
-        for s, e0, e1 in SCALE_GROUPS:
+        for s, e0, e1 in SCALE_GROUPS[:2]:
             load_scales(w1_bytes[s, e0, e1][:], w1_rows[s, :, e0:e1])
-        load_scales(w2_bytes[:], w2_scales.rearrange("e s q n -> q (e s) n"))
+        for passes in W1_LOADS[:4]:
+            load_w1(passes)
+        load_scales(w1_bytes[SCALE_GROUPS[2]][:], w1_rows[1, :, 4:E])
+        for passes in W1_LOADS[4:]:
+            load_w1(passes)
         nc.sync.dma_start(pos_sb[0][:], pos1)
         nc.sync.dma_start(pos_sb[1][:], pos2)
-        for passes in W1_LOADS:
-            load_w1(passes)
+        load_scales(w2_bytes[:], w2_scales.rearrange("e s q n -> q (e s) n"))
         w2_rows = w2_words.rearrange("e s p b -> p (e s) b")
         for e0, e1 in ((0, EARLY), (EARLY, E)):
             nc.sync.dma_start(w2_codes[:, e0:e1].bitcast(I32), w2_rows[:, e0:e1].bitcast(I32))

@@ -29,10 +29,9 @@ COPY = mybir.ActivationFunctionType.Copy
 GELU = mybir.ActivationFunctionType.Gelu_apprx_tanh
 
 
-TURNS = [(0, 2), (2, 3), (3, 5), (5, 6), (6, 7), (7, 8)]
+TURNS = [(0, 2, 1), (2, 4, 4), (4, 6, 5), (6, 7, 6), (7, 8, 7)]
 LAST = E - 1
 SCALE_GROUPS = [(0, 0, E), (1, 0, 4), (1, 4, E)]
-EARLY = 3
 W1_LOADS = [slice(0, 8, 2), slice(12, 13), slice(1, 8, 2), slice(8, 11, 2), slice(9, 16, 2), slice(14, 15)]
 UNIT = C * PACK
 PAIR = 2 * C * PACK
@@ -86,10 +85,11 @@ def tile_moe_pre_mlp_gelu_kernel(
         for d in range(1, PACK):
             load_plane(0, d)
         load_cols(0)
-        nc.sync.dma_start(gate_first[:], gate[0:P, 2 * C : 4 * C])
         load_plane(1, 0)
+        nc.sync.dma_start(gate_first[:], gate[0:P, 2 * C : 4 * C])
+        load_plane(1, 1)
         nc.sync.dma_start(gate_last[:], gate[0:P, 6 * C : SLOTS])
-        for d in range(1, PACK):
+        for d in range(2, PACK):
             load_plane(1, d)
         load_cols(1)
 
@@ -113,7 +113,7 @@ def tile_moe_pre_mlp_gelu_kernel(
         nc.sync.dma_start(pos_sb[1][:], pos2)
         load_scales(w2_bytes[:], w2_scales.rearrange("e s q n -> q (e s) n"))
         w2_rows = w2_words.rearrange("e s p b -> p (e s) b")
-        for e0, e1 in ((0, EARLY), (EARLY, E)):
+        for e0, e1 in ((0, 4), (4, E)):
             nc.sync.dma_start(w2_codes[:, e0:e1].bitcast(I32), w2_rows[:, e0:e1].bitcast(I32))
 
         x_codes = {}
@@ -175,8 +175,8 @@ def tile_moe_pre_mlp_gelu_kernel(
             h_rows[e] = hb
 
         def turn(i):
-            e0, e1 = TURNS[i]
-            turned = psum.tile([P, e1 - e0, 2, C], F32, name="turned", tag="bank%d" % (e1 - 1))
+            e0, e1, bank = TURNS[i]
+            turned = psum.tile([P, e1 - e0, 2, C], F32, name="turned", tag="bank%d" % bank)
             for e in range(e0, e1):
                 words = h_rows[e].rearrange("c u p v -> c (u p v)").bitcast(F32)
                 for u in range(2):
@@ -184,7 +184,7 @@ def tile_moe_pre_mlp_gelu_kernel(
             h_turned[i] = turned
 
         def weave(i, copy):
-            e0, e1 = TURNS[i]
+            e0, e1 = TURNS[i][:2]
             hq = keep.tile([P, (e1 - e0) * C * PACK], BF16, name="h_woven%d" % i, align_bytes=64)
             copy(
                 hq[:].bitcast(F32).rearrange("p (e c u) -> p e c u", u=2, c=C),
@@ -193,8 +193,8 @@ def tile_moe_pre_mlp_gelu_kernel(
             h_woven[i] = hq
 
         def quantise_h(i):
-            e0, e1 = TURNS[i]
-            tag = "h_rows%d" % e1 if i == 0 else "h_codes%d" % i
+            e0, e1 = TURNS[i][:2]
+            tag = "h_codes%d" % i
             hc = keep.tile([P, (e1 - e0) * C], U32, name="h_codes%d" % i, tag=tag, align_bytes=64)
             hs = keep.tile([P, (e1 - e0) * C], U8, name="h_bytes%d" % i, align_bytes=64)
             for e in range(e0, e1):
@@ -234,10 +234,11 @@ def tile_moe_pre_mlp_gelu_kernel(
         for d in range(PACK):
             gather("vector", b0[:, d, :], 6, E, 0, d)
         a1, d1 = staging("a1", 2), staging("d1", 2)
-        late = staging("late1", 4)
-        c0, c1 = late[:, :, 0 : 2 * C], late[:, :, 2 * C :]
-        for g, e0, s in ((a1, 0, 1), (d1, 2, 1), (c0, 4, 0), (c1, 4, 1)):
-            for d in range(PACK):
+        late = keep.tile([P, 5 * UNIT], F32, name="late", tag="late1", align_bytes=64)
+        c0, c1 = [late[:, at : at + PAIR].rearrange("p (d c) -> p d c", d=PACK) for at in (0, 3 * UNIT)]
+        seventh1 = late[:, PAIR : 2 * PAIR].rearrange("p (d c) -> p d c", d=PACK)[:, :, 0:C]
+        for g, e0, s, rows in ((a1, 0, 1, PACK), (d1, 2, 1, PACK), (c0, 4, 0, PACK), (c1, 4, 1, PACK - 1)):
+            for d in range(rows):
                 gather("scalar", g[:, d, :], e0, e0 + 2, s, d)
         weigh_on_gpsimd(units(3, 5), d0, gate_first[:])
         weigh_on_gpsimd(units(5, 7), b0, gate_last[:])
@@ -249,44 +250,55 @@ def tile_moe_pre_mlp_gelu_kernel(
         quantise_x(units(0, 4), [(0, 1), (0, 0), (1, 0), (2, 0)])
         quantise_x(units(4, 8), [(3, 0), (6, 0), (7, 0), (1, 1)])
         weigh_on_gpsimd(units(1, 3), d1, gate_first[:])
-        seventh1 = staging("seventh1", 1, tag="a1")
-        for d in range(PACK):
+        for d in range(2):
             gather("vector", seventh1[:, d, :], LAST, E, 1, d)
+        gather("vector", c1[:, PACK - 1, :], 4, 6, 1, PACK - 1)
         weigh_on_vector(units(4, 6), c0, gate_banks[1][:])
         quantise_x(units(1, 3), [(2, 1), (3, 1)])
         quantise_x(units(4, 6), [(4, 0), (5, 0)], tag="d1")
         weigh_on_gpsimd(units(2.5, 3.5), sixth1, gate_last[:, 0:C])
-        weigh_on_vector(units(0.5, 2.5), c1, gate_banks[1][:])
-        quantise_x(units(0.5, 2.5), [(4, 1), (5, 1)])
-        rounded7 = keep.tile([P, UNIT], BF16, name="rounded7", tag="last0", align_bytes=64)
-        weigh_on_vector(rounded7[:], seventh1, gate_last[:, C:])
+        weigh_on_vector(units(0.5, 1.5), c1[:, :, 0:C], gate_banks[1][:, 0:C])
+        weigh_on_vector(units(1.5, 2.5), c1[:, :, C:], gate_banks[1][:, C:])
+        quantise_x(units(0.5, 1.5), [(4, 1)])
+        quantise_x(units(1.5, 2.5), [(5, 1)])
+        for d in range(2, PACK):
+            gather("vector", seventh1[:, d, :], LAST, E, 1, d)
         quantise_x(units(2.5, 3.5), [(6, 1)])
+        rounded7 = keep.tile([P, UNIT], BF16, name="rounded7", align_bytes=64)
+        weigh_on_vector(rounded7[:], seventh1, gate_last[:, C:])
         quantise_x(rounded7[:], [(7, 1)])
         first_pass(0, 4, 0)
         first_pass(6, LAST, 0)
         first_pass(0, 4, 1)
         first_pass(4, 6, 0)
-        for i, (e0, e1) in enumerate(TURNS):
-            for e in range(e0, e1):
-                activate(e)
+        for e in range(4):
+            activate(e)
+        turn(0)
+        weave(0, on_vector)
+        first_pass(4, E, 1)
+        activate(4)
+        turn(1)
+        weave(1, on_vector)
+        quantise_h(0)
+        first_pass(LAST, E, 0)
+        activate(5)
+        turn(2)
+        quantise_h(1)
+        for i in (3, 4):
+            activate(TURNS[i][0])
+        weave(2, on_scalar)
+        for i in (3, 4):
             turn(i)
-            if i == 1:
-                first_pass(4, E, 1)
-            if i == 2:
-                first_pass(LAST, E, 0)
-            weave(i, on_vector if e1 < LAST else on_scalar)
-            if i:
-                quantise_h(i - 1)
-        quantise_h(len(TURNS) - 1)
+            weave(i, on_scalar)
+        for i in (2, 3, 4):
+            quantise_h(i)
         y = [keep.tile([P, SLOTS], F32, name="y%d" % c) for c in range(CHUNKS)]
-        for chunk in range(CHUNKS):
-            second_product(chunk, 0, EARLY, chunk, on_vector)
-        second_product(0, EARLY, 6, 3, on_scalar)
-        second_product(2, EARLY, 6, 5, on_scalar)
-        second_product(0, 6, E, 6, on_scalar)
-        second_product(1, EARLY, 6, 4, on_vector)
-        second_product(1, 6, E, LAST, on_vector)
-        second_product(2, 6, E, 0, on_vector)
+        second_product(0, 0, 4, 0, on_scalar)
+        second_product(1, 0, 4, 2, on_vector)
+        second_product(0, 4, 6, 3, on_scalar)
+        second_product(0, 6, E, 1, on_scalar)
+        second_product(1, 4, E, 4, on_vector)
+        second_product(2, 4, E, 5, on_vector)
 
         picked = [keep.tile([P, T], F32, name="picked%d" % c) for c in range(CHUNKS)]
         summed = [keep.tile([P, T], F32, name="summed%d" % c) for c in range(CHUNKS)]
@@ -302,5 +314,6 @@ def tile_moe_pre_mlp_gelu_kernel(
 
         half = T // 2
         combine(0, [0, half, T])
+        second_product(2, 0, 4, 2, on_scalar)
         combine(1, [0, half, T])
         combine(2, [0, half, T - T // 8, T])

@@ -33,6 +33,7 @@ TURNS = [(0, 2, 1), (2, 4, 4), (4, 6, 5), (6, 7, 6), (7, 8, 7)]
 LAST = E - 1
 SCALE_GROUPS = [(0, 0, E), (1, 0, 4), (1, 4, E)]
 W1_LOADS = [slice(0, 8, 2), slice(12, 13), slice(1, 8, 2), slice(8, 11, 2), slice(9, 16, 2), slice(14, 15)]
+Y_BANKS = [(0, 0, 4, 0), (1, 0, 4, 2), (0, 4, 6, 3), (0, 6, E, 1), (1, 4, E, 4), (2, 4, E, 5), (2, 2, 4, 6), (2, 0, 2, 2)]
 UNIT = C * PACK
 PAIR = 2 * C * PACK
 
@@ -82,9 +83,10 @@ def tile_moe_pre_mlp_gelu_kernel(
 
         load_plane(0, 0)
         nc.sync.dma_start(offs_sb[:], offs)
-        for d in range(1, PACK):
-            load_plane(0, d)
+        load_plane(0, 1)
+        load_plane(0, 2)
         load_cols(0)
+        load_plane(0, 3)
         load_plane(1, 0)
         nc.sync.dma_start(gate_first[:], gate[0:P, 2 * C : 4 * C])
         load_plane(1, 1)
@@ -109,12 +111,13 @@ def tile_moe_pre_mlp_gelu_kernel(
         load_scales(w1_bytes[SCALE_GROUPS[2]][:], w1_rows[1, :, 4:E])
         for passes in W1_LOADS[4:]:
             load_w1(passes)
-        nc.sync.dma_start(pos_sb[0][:], pos1)
-        nc.sync.dma_start(pos_sb[1][:], pos2)
         load_scales(w2_bytes[:], w2_scales.rearrange("e s q n -> q (e s) n"))
         w2_rows = w2_words.rearrange("e s p b -> p (e s) b")
         for e0, e1 in ((0, 4), (4, E)):
             nc.sync.dma_start(w2_codes[:, e0:e1].bitcast(I32), w2_rows[:, e0:e1].bitcast(I32))
+
+        nc.sync.dma_start(pos_sb[0][:], pos1)
+        nc.sync.dma_start(pos_sb[1][:], pos2)
 
         x_codes = {}
         h_codes = {}
@@ -202,11 +205,11 @@ def tile_moe_pre_mlp_gelu_kernel(
                 h_codes[e] = (hc[:, cols], hs[:, cols])
             nc.vector.quantize_mx(out=hc[:].bitcast(FP8X4), scales=hs[:], in_=h_woven[i][:])
 
-        def second_product(chunk, e0, e1, bank, copy):
-            acc = psum.tile([P, (e1 - e0) * C], F32, name="acc", tag="bank%d" % bank)
+        def second_product(chunk, e0, e1):
             for e in range(e0, e1):
+                first, acc = [(a, tile) for (c, a, b), tile in y_sums.items() if c == chunk and a <= e < b][0]
                 nc.tensor.matmul_mx(
-                    out=acc[:, (e - e0) * C : (e - e0 + 1) * C],
+                    out=acc[:, (e - first) * C : (e - first + 1) * C],
                     lhsT=w2_codes[:, e, 2 * P * chunk : 2 * P * (chunk + 1)].bitcast(FP4X4),
                     lhsT_scale=w2_bytes[:, e, P * chunk : P * (chunk + 1)],
                     rhs=h_codes[e][0].bitcast(FP8X4),
@@ -214,7 +217,9 @@ def tile_moe_pre_mlp_gelu_kernel(
                     start=True,
                     stop=True,
                 )
-            copy(y[chunk][:, e0 * C : e1 * C], acc[:])
+
+        def fill_y(chunk, e0, e1, copy):
+            copy(y[chunk][:, e0 * C : e1 * C], y_sums[chunk, e0, e1][:])
 
         on_scalar, on_vector = nc.scalar.copy, nc.vector.tensor_copy
 
@@ -234,8 +239,8 @@ def tile_moe_pre_mlp_gelu_kernel(
         for d in range(PACK):
             gather("vector", b0[:, d, :], 6, E, 0, d)
         a1, d1 = staging("a1", 2), staging("d1", 2)
-        late = keep.tile([P, 5 * UNIT], F32, name="late", tag="late1", align_bytes=64)
-        c0, c1 = [late[:, at : at + PAIR].rearrange("p (d c) -> p d c", d=PACK) for at in (0, 3 * UNIT)]
+        late = keep.tile([P, 2 * PAIR + 3 * UNIT // 2], F32, name="late", tag="late1", align_bytes=64)
+        c0, c1 = [late[:, at : at + PAIR].rearrange("p (d c) -> p d c", d=PACK) for at in (0, PAIR + 3 * UNIT // 2)]
         seventh1 = late[:, PAIR : 2 * PAIR].rearrange("p (d c) -> p d c", d=PACK)[:, :, 0:C]
         for g, e0, s, rows in ((a1, 0, 1, PACK), (d1, 2, 1, PACK), (c0, 4, 0, PACK), (c1, 4, 1, PACK - 1)):
             for d in range(rows):
@@ -250,7 +255,7 @@ def tile_moe_pre_mlp_gelu_kernel(
         quantise_x(units(0, 4), [(0, 1), (0, 0), (1, 0), (2, 0)])
         quantise_x(units(4, 8), [(3, 0), (6, 0), (7, 0), (1, 1)])
         weigh_on_gpsimd(units(1, 3), d1, gate_first[:])
-        for d in range(2):
+        for d in range(PACK - 1):
             gather("vector", seventh1[:, d, :], LAST, E, 1, d)
         gather("vector", c1[:, PACK - 1, :], 4, 6, 1, PACK - 1)
         weigh_on_vector(units(4, 6), c0, gate_banks[1][:])
@@ -259,13 +264,12 @@ def tile_moe_pre_mlp_gelu_kernel(
         weigh_on_gpsimd(units(2.5, 3.5), sixth1, gate_last[:, 0:C])
         weigh_on_vector(units(0.5, 1.5), c1[:, :, 0:C], gate_banks[1][:, 0:C])
         weigh_on_vector(units(1.5, 2.5), c1[:, :, C:], gate_banks[1][:, C:])
+        gather("vector", seventh1[:, PACK - 1, :], LAST, E, 1, PACK - 1)
         quantise_x(units(0.5, 1.5), [(4, 1)])
         quantise_x(units(1.5, 2.5), [(5, 1)])
-        for d in range(2, PACK):
-            gather("vector", seventh1[:, d, :], LAST, E, 1, d)
-        quantise_x(units(2.5, 3.5), [(6, 1)])
         rounded7 = keep.tile([P, UNIT], BF16, name="rounded7", align_bytes=64)
         weigh_on_vector(rounded7[:], seventh1, gate_last[:, C:])
+        quantise_x(units(2.5, 3.5), [(6, 1)])
         quantise_x(rounded7[:], [(7, 1)])
         first_pass(0, 4, 0)
         first_pass(6, LAST, 0)
@@ -293,12 +297,26 @@ def tile_moe_pre_mlp_gelu_kernel(
         for i in (2, 3, 4):
             quantise_h(i)
         y = [keep.tile([P, SLOTS], F32, name="y%d" % c) for c in range(CHUNKS)]
-        second_product(0, 0, 4, 0, on_scalar)
-        second_product(1, 0, 4, 2, on_vector)
-        second_product(0, 4, 6, 3, on_scalar)
-        second_product(0, 6, E, 1, on_scalar)
-        second_product(1, 4, E, 4, on_vector)
-        second_product(2, 4, E, 5, on_vector)
+        y_sums = {
+            (chunk, e0, e1): psum.tile([P, (e1 - e0) * C], F32, name="y_sums", tag="bank%d" % bank)
+            for chunk, e0, e1, bank in Y_BANKS[:-1]
+        }
+        second_product(0, 0, 4)
+        fill_y(0, 0, 4, on_scalar)
+        second_product(1, 0, 4)
+        fill_y(1, 0, 4, on_vector)
+        second_product(0, 4, 6)
+        fill_y(0, 4, 6, on_scalar)
+        second_product(1, 4, 6)
+        for e in (6, LAST):
+            second_product(0, e, e + 1)
+            second_product(1, e, e + 1)
+        fill_y(0, 6, E, on_scalar)
+        fill_y(1, 4, E, on_vector)
+        second_product(2, 4, E)
+        fill_y(2, 4, E, on_vector)
+        second_product(2, 2, 4)
+        fill_y(2, 2, 4, on_vector)
 
         picked = [keep.tile([P, T], F32, name="picked%d" % c) for c in range(CHUNKS)]
         summed = [keep.tile([P, T], F32, name="summed%d" % c) for c in range(CHUNKS)]
@@ -314,6 +332,8 @@ def tile_moe_pre_mlp_gelu_kernel(
 
         half = T // 2
         combine(0, [0, half, T])
-        second_product(2, 0, 4, 2, on_scalar)
+        y_sums[2, 0, 2] = psum.tile([P, 2 * C], F32, name="y_sums", tag="bank%d" % Y_BANKS[-1][3])
+        second_product(2, 0, 2)
+        fill_y(2, 0, 2, on_scalar)
         combine(1, [0, half, T])
         combine(2, [0, half, T - T // 8, T])

@@ -29,11 +29,13 @@ COPY = mybir.ActivationFunctionType.Copy
 GELU = mybir.ActivationFunctionType.Gelu_apprx_tanh
 
 
-TURNS = [(0, 2, 1), (2, 4, 4), (4, 6, 5), (6, 7, 6), (7, 8, 7)]
+TURNS = [(0, 2, 4), (2, 4, 0), (4, 6, 6), (6, 7, 1), (7, 8, 5)]
+SUM_BANKS = [0, 1, 2, 3, 0, 1, 6, 7]
 LAST = E - 1
 SCALE_GROUPS = [(0, 0, E), (1, 0, 4), (1, 4, E)]
-W1_LOADS = [slice(0, 8, 2), slice(12, 13), slice(1, 8, 2), slice(8, 11, 2), slice(9, 16, 2), slice(14, 15)]
-Y_BANKS = [(0, 0, 4, 0), (1, 0, 4, 2), (0, 4, 6, 3), (0, 6, E, 1), (1, 4, E, 4), (2, 4, E, 5), (2, 2, 4, 6), (2, 0, 2, 2)]
+W1_LOADS = [slice(0, 10, 2), slice(12, 15, 2), slice(1, 8, 2), slice(9, 12), slice(13, 16, 2)]
+Y_BANKS = [(0, 0, 4, 2), (1, 0, 4, 3), (0, 4, E, 4), (1, 4, E, 7), (2, 0, 2, 2), (2, 4, E, 0), (2, 2, 4, 3)]
+BANK = 2048
 UNIT = C * PACK
 PAIR = 2 * C * PACK
 
@@ -51,7 +53,7 @@ def tile_moe_pre_mlp_gelu_kernel(
         tokens = [keep.tile([P, T], F32, name="tokens%d" % j, align_bytes=64) for j in range(PASSES * PACK)]
         gate_first = keep.tile([P, 2 * C], F32, name="gate_first")
         gate_last = keep.tile([P, 2 * C], F32, name="gate_last")
-        gate_cols = [keep.tile([P, 2], F32, name=name, align_bytes=64) for name in ("last0", "late1")]
+        gate_cols = [keep.tile([P, n], F32, name=name, align_bytes=64) for name, n in (("last0", 2), ("late1", 3))]
         w1_codes = keep.tile([P, E * PASSES, 2 * H], U8, name="w1_codes", align_bytes=64)
         w1_bytes = {
             group: keep.tile([P, group[2] - group[1], H], U8, name="w1_bytes%d_%d" % group[:2], align_bytes=64)
@@ -61,7 +63,6 @@ def tile_moe_pre_mlp_gelu_kernel(
         w2_bytes = keep.tile([P, E, N], U8, name="w2_bytes", align_bytes=64)
         ident = keep.tile([P, P], F32, name="ident")
         warm = keep.tile([P, 2], F32, name="warm")
-        rounded = keep.tile([P, 4 * PAIR], BF16, name="rounded", align_bytes=64)
 
         nc.vector.memset(warm[:, 0:1], 0.0)
         nc.scalar.activation(warm[:, 1:2], warm[:, 0:1], GELU)
@@ -78,7 +79,7 @@ def tile_moe_pre_mlp_gelu_kernel(
 
         def load_cols(n):
             with nc.allow_non_contiguous_dma(reason="one weight for each partition and expert"):
-                rows = gate[0, 4 * n * C : (4 * n + 2) * C]
+                rows = gate[0, 4 * n * C : (5 * n + 2) * C]
                 nc.sync.dma_start(gate_cols[n][:], rows.rearrange("(e p) -> p e", p=P))
 
         load_plane(0, 0)
@@ -106,10 +107,10 @@ def tile_moe_pre_mlp_gelu_kernel(
         w1_passes = w1_words.rearrange("e s p b -> p (e s) b")
         for s, e0, e1 in SCALE_GROUPS[:2]:
             load_scales(w1_bytes[s, e0, e1][:], w1_rows[s, :, e0:e1])
-        for passes in W1_LOADS[:4]:
+        for passes in W1_LOADS[:3]:
             load_w1(passes)
         load_scales(w1_bytes[SCALE_GROUPS[2]][:], w1_rows[1, :, 4:E])
-        for passes in W1_LOADS[4:]:
+        for passes in W1_LOADS[3:]:
             load_w1(passes)
         load_scales(w2_bytes[:], w2_scales.rearrange("e s q n -> q (e s) n"))
         w2_rows = w2_words.rearrange("e s p b -> p (e s) b")
@@ -161,7 +162,7 @@ def tile_moe_pre_mlp_gelu_kernel(
                 group = [g for g in SCALE_GROUPS if g[0] == s and g[1] <= e < g[2]][0]
                 opens = e not in sums
                 if opens:
-                    sums[e] = psum.tile([P, H], F32, name="sums", tag="bank%d" % e)
+                    sums[e] = psum.tile([P, H], F32, name="sums%d" % e, offset=BANK * SUM_BANKS[e])
                 nc.tensor.matmul_mx(
                     out=sums[e][:],
                     lhsT=x_codes[e, s][0].bitcast(FP8X4),
@@ -179,7 +180,7 @@ def tile_moe_pre_mlp_gelu_kernel(
 
         def turn(i):
             e0, e1, bank = TURNS[i]
-            turned = psum.tile([P, e1 - e0, 2, C], F32, name="turned", tag="bank%d" % bank)
+            turned = psum.tile([P, e1 - e0, 2, C], F32, name="turned%d" % i, offset=BANK * bank)
             for e in range(e0, e1):
                 words = h_rows[e].rearrange("c u p v -> c (u p v)").bitcast(F32)
                 for u in range(2):
@@ -195,9 +196,9 @@ def tile_moe_pre_mlp_gelu_kernel(
             )
             h_woven[i] = hq
 
-        def quantise_h(i):
+        def quantise_h(i, tag=None):
             e0, e1 = TURNS[i][:2]
-            tag = "h_codes%d" % i
+            tag = tag or "h_codes%d" % i
             hc = keep.tile([P, (e1 - e0) * C], U32, name="h_codes%d" % i, tag=tag, align_bytes=64)
             hs = keep.tile([P, (e1 - e0) * C], U8, name="h_bytes%d" % i, align_bytes=64)
             for e in range(e0, e1):
@@ -223,103 +224,97 @@ def tile_moe_pre_mlp_gelu_kernel(
 
         on_scalar, on_vector = nc.scalar.copy, nc.vector.tensor_copy
 
-        gate_banks = [psum.tile([P, 2 * C], F32, name="gate_bank", tag="bank%d" % bank) for bank in (4, LAST)]
-        for e in range(4):
-            column = gate_cols[e // 2][:, e % 2 : e % 2 + 1]
-            nc.tensor.transpose(gate_banks[e // 2][:, e % 2 * C : (e % 2 + 1) * C], column.to_broadcast([P, P]), ident[:])
+        gate_banks = []
+        for n, bank in enumerate((4, 5)):
+            experts = gate_cols[n].shape[1]
+            spread = psum.tile([P, experts * C], F32, name="gate_bank%d" % n, offset=BANK * bank)
+            for e in range(experts):
+                column = gate_cols[n][:, e : e + 1]
+                nc.tensor.transpose(spread[:, e * C : (e + 1) * C], column.to_broadcast([P, P]), ident[:])
+            gate_banks.append(spread)
 
         def units(a, b):
             return rounded[:, int(a * UNIT) : int(b * UNIT)]
 
-        a0, held, d0 = staging("a0", 2), staging("last0", 3), staging("d0", 2)
-        b0, sixth1 = held[:, :, 0 : 2 * C], held[:, :, 2 * C :]
+        def rows_at(flat, at):
+            return flat[:, at : at + PAIR].rearrange("p (d c) -> p d c", d=PACK)
+
+        a0, d0, a1, d1 = [staging(name, 2) for name in ("a0", "d0", "a1", "d1")]
+        held = keep.tile([P, 3 * UNIT + 9 * UNIT // 2], F32, name="held", tag="last0", align_bytes=64)
+        b0, c0 = [rows_at(held, at) for at in (0, PAIR)]
+        rounded = held[:, 3 * UNIT :].bitcast(BF16)
+        c1 = staging("c1", 2, tag="late1")
         for d in range(PACK):
             gather("vector", d0[:, d, :], 2, 4, 0, d)
             gather("scalar", a0[:, d, :], 0, 2, 0, d)
         for d in range(PACK):
             gather("vector", b0[:, d, :], 6, E, 0, d)
-        a1, d1 = staging("a1", 2), staging("d1", 2)
-        late = keep.tile([P, 2 * PAIR + 3 * UNIT // 2], F32, name="late", tag="late1", align_bytes=64)
-        c0, c1 = [late[:, at : at + PAIR].rearrange("p (d c) -> p d c", d=PACK) for at in (0, PAIR + 3 * UNIT // 2)]
-        seventh1 = late[:, PAIR : 2 * PAIR].rearrange("p (d c) -> p d c", d=PACK)[:, :, 0:C]
-        for g, e0, s, rows in ((a1, 0, 1, PACK), (d1, 2, 1, PACK), (c0, 4, 0, PACK), (c1, 4, 1, PACK - 1)):
-            for d in range(rows):
-                gather("scalar", g[:, d, :], e0, e0 + 2, s, d)
-        weigh_on_gpsimd(units(3, 5), d0, gate_first[:])
+        for g, e0 in ((a1, 0), (d1, 2), (c1, 4)):
+            for d in range(PACK):
+                gather("scalar", g[:, d, :], e0, e0 + 2, 1, d)
+        weigh_on_gpsimd(units(2, 4), d0, gate_first[:])
         weigh_on_gpsimd(units(5, 7), b0, gate_last[:])
-        weigh_on_vector(units(1, 3), a0, gate_banks[0][:])
+        weigh_on_vector(units(0, 2), a0, gate_banks[0][:])
+        for d in range(2):
+            gather("vector", c0[:, d, :], 4, 6, 0, d)
+        weigh_on_vector(units(7, 9), a1, gate_banks[0][:])
+        b1 = staging("b1", 2, tag="a1")
         for d in range(PACK):
-            gather("vector", sixth1[:, d, :], 6, LAST, 1, d)
-        weigh_on_vector(units(0, 1), a1[:, :, 0:C], gate_banks[0][:, 0:C])
-        weigh_on_vector(units(7, 8), a1[:, :, C:], gate_banks[0][:, C:])
-        quantise_x(units(0, 4), [(0, 1), (0, 0), (1, 0), (2, 0)])
-        quantise_x(units(4, 8), [(3, 0), (6, 0), (7, 0), (1, 1)])
-        weigh_on_gpsimd(units(1, 3), d1, gate_first[:])
-        for d in range(PACK - 1):
-            gather("vector", seventh1[:, d, :], LAST, E, 1, d)
-        gather("vector", c1[:, PACK - 1, :], 4, 6, 1, PACK - 1)
-        weigh_on_vector(units(4, 6), c0, gate_banks[1][:])
-        quantise_x(units(1, 3), [(2, 1), (3, 1)])
-        quantise_x(units(4, 6), [(4, 0), (5, 0)], tag="d1")
-        weigh_on_gpsimd(units(2.5, 3.5), sixth1, gate_last[:, 0:C])
-        weigh_on_vector(units(0.5, 1.5), c1[:, :, 0:C], gate_banks[1][:, 0:C])
-        weigh_on_vector(units(1.5, 2.5), c1[:, :, C:], gate_banks[1][:, C:])
-        gather("vector", seventh1[:, PACK - 1, :], LAST, E, 1, PACK - 1)
-        quantise_x(units(0.5, 1.5), [(4, 1)])
+            gather("scalar", b1[:, d, :], 6, E, 1, d)
+        quantise_x(units(0, 4), [(0, 0), (1, 0), (2, 0), (3, 0)])
+        quantise_x(units(5, 9), [(6, 0), (7, 0), (0, 1), (1, 1)])
+        weigh_on_gpsimd(units(2, 4), d1, gate_first[:])
+        for d in range(2, PACK):
+            gather("vector", c0[:, d, :], 4, 6, 0, d)
+        weigh_on_vector(units(5, 7), c0, gate_banks[1][:, 0 : 2 * C])
+        weigh_on_vector(units(7, 8), c1[:, :, 0:C], gate_banks[1][:, 0:C])
+        quantise_x(units(2, 4), [(2, 1), (3, 1)])
+        quantise_x(units(5, 8), [(4, 0), (5, 0), (4, 1)], tag="d1")
+        weigh_on_gpsimd(units(3.5, 4.5), b1[:, :, C:], gate_last[:, C:])
+        weigh_on_vector(units(1.5, 2.5), c1[:, :, C:], gate_banks[1][:, C : 2 * C])
+        weigh_on_vector(units(2.5, 3.5), b1[:, :, 0:C], gate_banks[1][:, 2 * C :])
         quantise_x(units(1.5, 2.5), [(5, 1)])
-        rounded7 = keep.tile([P, UNIT], BF16, name="rounded7", align_bytes=64)
-        weigh_on_vector(rounded7[:], seventh1, gate_last[:, C:])
-        quantise_x(units(2.5, 3.5), [(6, 1)])
-        quantise_x(rounded7[:], [(7, 1)])
+        quantise_x(units(2.5, 4.5), [(6, 1), (7, 1)])
         first_pass(0, 4, 0)
-        first_pass(6, LAST, 0)
+        first_pass(6, E, 0)
         first_pass(0, 4, 1)
-        first_pass(4, 6, 0)
         for e in range(4):
             activate(e)
+        first_pass(4, 5, 0)
         turn(0)
         weave(0, on_vector)
-        first_pass(4, E, 1)
+        first_pass(4, 5, 1)
+        first_pass(5, 6, 0)
+        first_pass(5, 6, 1)
         activate(4)
         turn(1)
         weave(1, on_vector)
-        quantise_h(0)
-        first_pass(LAST, E, 0)
-        activate(5)
-        turn(2)
+        quantise_h(0, tag="h_rows3")
         quantise_h(1)
-        for i in (3, 4):
-            activate(TURNS[i][0])
-        weave(2, on_scalar)
+        activate(5)
+        first_pass(6, E, 1)
+        for e in (6, LAST):
+            activate(e)
+        turn(2)
+        weave(2, on_vector)
         for i in (3, 4):
             turn(i)
             weave(i, on_scalar)
-        for i in (2, 3, 4):
+        for i in (3, 2, 4):
             quantise_h(i)
         y = [keep.tile([P, SLOTS], F32, name="y%d" % c) for c in range(CHUNKS)]
         y_sums = {
-            (chunk, e0, e1): psum.tile([P, (e1 - e0) * C], F32, name="y_sums", tag="bank%d" % bank)
-            for chunk, e0, e1, bank in Y_BANKS[:-1]
+            (chunk, e0, e1): psum.tile([P, (e1 - e0) * C], F32, name="y_sums%d_%d" % (chunk, e0), offset=BANK * bank)
+            for chunk, e0, e1, bank in Y_BANKS
         }
-        second_product(0, 0, 4)
-        fill_y(0, 0, 4, on_scalar)
-        second_product(1, 0, 4)
-        fill_y(1, 0, 4, on_vector)
-        second_product(0, 4, 6)
-        fill_y(0, 4, 6, on_scalar)
-        second_product(1, 4, 6)
-        for e in (6, LAST):
-            second_product(0, e, e + 1)
-            second_product(1, e, e + 1)
-        fill_y(0, 6, E, on_scalar)
-        fill_y(1, 4, E, on_vector)
-        second_product(2, 4, E)
-        fill_y(2, 4, E, on_vector)
-        second_product(2, 2, 4)
-        fill_y(2, 2, 4, on_vector)
+        for (chunk, e0, e1, bank), copy in zip(Y_BANKS, (on_scalar, on_vector) * 3 + (on_vector,)):
+            second_product(chunk, e0, e1)
+            fill_y(chunk, e0, e1, copy)
 
         picked = [keep.tile([P, T], F32, name="picked%d" % c) for c in range(CHUNKS)]
-        summed = [keep.tile([P, T], F32, name="summed%d" % c) for c in range(CHUNKS)]
+        summed = [
+            keep.tile([P, T], F32, name="summed", tag=tag, align_bytes=64) for tag in ("h_codes4", "summed1", "summed2")
+        ]
 
         def combine(chunk, cuts):
             for a, b in zip(cuts, cuts[1:]):
@@ -332,8 +327,5 @@ def tile_moe_pre_mlp_gelu_kernel(
 
         half = T // 2
         combine(0, [0, half, T])
-        y_sums[2, 0, 2] = psum.tile([P, 2 * C], F32, name="y_sums", tag="bank%d" % Y_BANKS[-1][3])
-        second_product(2, 0, 2)
-        fill_y(2, 0, 2, on_scalar)
         combine(1, [0, half, T])
         combine(2, [0, half, T - T // 8, T])

@@ -36,6 +36,7 @@ SCALE_GROUPS = [(0, 0, E), (1, 0, 4), (1, 4, E)]
 W1_LOADS = [slice(0, 10, 2), slice(12, 15, 2), slice(1, 8, 2), slice(9, 12), slice(13, 16, 2)]
 Y_BANKS = [(0, 0, 4, 2), (1, 0, 4, 3), (0, 4, E, 4), (1, 4, E, 7), (2, 0, 2, 2), (2, 4, E, 0), (2, 2, 4, 3)]
 BANK = 2048
+SPARE = 16
 UNIT = C * PACK
 PAIR = 2 * C * PACK
 
@@ -50,7 +51,9 @@ def tile_moe_pre_mlp_gelu_kernel(
 
         offs_sb = keep.tile([P, SLOTS // LIST], U16, name="offs_sb")
         pos_sb = [keep.tile([P, T // LIST], U16, name="pos%d_sb" % r) for r in range(2)]
-        tokens = [keep.tile([P, T], F32, name="tokens%d" % j, align_bytes=64) for j in range(PASSES * PACK)]
+        tokens = [
+            keep.tile([P, T + SPARE * (PACK <= j < 2 * PACK - 1)], F32, name="tokens%d" % j, align_bytes=64) for j in range(PASSES * PACK)
+        ]
         gate_first = keep.tile([P, 2 * C], F32, name="gate_first")
         gate_last = keep.tile([P, 2 * C], F32, name="gate_last")
         gate_cols = [keep.tile([P, n], F32, name=name, align_bytes=64) for name, n in (("last0", 2), ("late1", 3))]
@@ -67,6 +70,8 @@ def tile_moe_pre_mlp_gelu_kernel(
         nc.vector.memset(warm[:, 0:1], 0.0)
         nc.scalar.activation(warm[:, 1:2], warm[:, 0:1], GELU)
         make_identity(nc, ident[:])
+        for plane in tokens[PACK:-1]:
+            nc.vector.memset(plane[:, T:], 0.0)
         for tile in [w1_bytes[group] for group in SCALE_GROUPS]:
             nc.vector.memset(tile[:].rearrange("p e i -> p (e i)").bitcast(I32), 0)
         nc.gpsimd.memset(w2_bytes[:].rearrange("p e n -> p (e n)").bitcast(I32), 0)
@@ -75,7 +80,7 @@ def tile_moe_pre_mlp_gelu_kernel(
 
         def load_plane(s, d):
             j = PACK * s + d
-            nc.sync.dma_start(tokens[j][:], x_rows[s, d])
+            nc.sync.dma_start(tokens[j][:, 0:T], x_rows[s, d])
 
         def load_cols(n):
             with nc.allow_non_contiguous_dma(reason="one weight for each partition and expert"):
@@ -239,28 +244,29 @@ def tile_moe_pre_mlp_gelu_kernel(
         def rows_at(flat, at):
             return flat[:, at : at + PAIR].rearrange("p (d c) -> p d c", d=PACK)
 
-        a0, d0, a1, d1 = [staging(name, 2) for name in ("a0", "d0", "a1", "d1")]
+        a0, d0, low1 = staging("a0", 2), staging("d0", 2), staging("d1", 4)
+        a1, d1 = low1[:, :, 0 : 2 * C], low1[:, :, 2 * C :]
         held = keep.tile([P, 3 * UNIT + 9 * UNIT // 2], F32, name="held", tag="last0", align_bytes=64)
         b0, c0 = [rows_at(held, at) for at in (0, PAIR)]
         rounded = held[:, 3 * UNIT :].bitcast(BF16)
-        c1 = staging("c1", 2, tag="late1")
+        high1 = staging("high1", 4, tag="late1")
+        c1, b1 = high1[:, :, 0 : 2 * C], high1[:, :, 2 * C :]
         for d in range(PACK):
             gather("vector", d0[:, d, :], 2, 4, 0, d)
             gather("scalar", a0[:, d, :], 0, 2, 0, d)
         for d in range(PACK):
             gather("vector", b0[:, d, :], 6, E, 0, d)
-        for g, e0 in ((a1, 0), (d1, 2), (c1, 4)):
-            for d in range(PACK):
-                gather("scalar", g[:, d, :], e0, e0 + 2, 1, d)
+        for g, e0 in ((low1, 0), (high1, 4)):
+            for d in range(PACK - 1):
+                gather("scalar", g[:, d, :], e0, e0 + 4, 1, d)
+            for n in (0, 2):
+                gather("scalar", g[:, PACK - 1, n * C : (n + 2) * C], e0 + n, e0 + n + 2, 1, PACK - 1)
         weigh_on_gpsimd(units(2, 4), d0, gate_first[:])
         weigh_on_gpsimd(units(5, 7), b0, gate_last[:])
         weigh_on_vector(units(0, 2), a0, gate_banks[0][:])
         for d in range(2):
             gather("vector", c0[:, d, :], 4, 6, 0, d)
         weigh_on_vector(units(7, 9), a1, gate_banks[0][:])
-        b1 = staging("b1", 2, tag="a1")
-        for d in range(PACK):
-            gather("scalar", b1[:, d, :], 6, E, 1, d)
         quantise_x(units(0, 4), [(0, 0), (1, 0), (2, 0), (3, 0)])
         quantise_x(units(5, 9), [(6, 0), (7, 0), (0, 1), (1, 1)])
         weigh_on_gpsimd(units(2, 4), d1, gate_first[:])

from contextlib import ExitStack

import concourse.mybir as mybir
from concourse.masks import make_identity

K, T, E, C, H, N = 1024, 512, 8, 128, 512, 384
SLOTS = E * C
P = 128
PACK = 4
PASSES = K // (P * PACK)
CHUNKS = N // P
LIST = 16
FLOPS = 2 * SLOTS * (K * H + H * N)
BYTES = (
    4 * K * T + E * (K * H + H * N) // 2 + E * (K * H + H * N) // 32 + 4 * P * SLOTS + 2 * P * (SLOTS + 2 * T) // LIST + 4 * N * T
)

F32 = mybir.dt.float32
BF16 = mybir.dt.bfloat16
I32 = mybir.dt.int32
U32 = mybir.dt.uint32
U16 = mybir.dt.uint16
U8 = mybir.dt.uint8
FP8X4 = mybir.dt.float8_e4m3fn_x4
FP4X4 = mybir.dt.float4_e2m1fn_x4
MULT = mybir.AluOpType.mult
ADD = mybir.AluOpType.add
COPY = mybir.ActivationFunctionType.Copy
GELU = mybir.ActivationFunctionType.Gelu_apprx_tanh


TURNS = [(0, 2, 4), (2, 4, 0), (4, 6, 6), (6, 7, 1), (7, 8, 5)]
SUM_BANKS = [0, 1, 2, 3, 0, 1, 6, 7]
LAST = E - 1
SCALE_GROUPS = [(0, 0, E), (1, 0, 4), (1, 4, E)]
W1_LOADS = [slice(0, 10, 2), slice(12, 15, 2), slice(1, 8, 2), slice(9, 12), slice(13, 16, 2)]
Y_BANKS = [(0, 0, 4, 2), (1, 0, 4, 3), (0, 4, E, 4), (1, 4, E, 7), (2, 0, 2, 2), (2, 4, E, 0), (2, 2, 4, 3)]
BANK = 2048
SPARE = 16
UNIT = C * PACK
PAIR = 2 * C * PACK


def tile_moe_pre_mlp_gelu_kernel(
    tc, xT, w1_words, w1_scales, w2_words, w2_scales, gate, offs, pos1, pos2, out
):
    nc = tc.nc
    with ExitStack() as ctx:
        keep = ctx.enter_context(tc.tile_pool(name="keep", bufs=1))
        psum = ctx.enter_context(tc.psum_pool(name="psum", bufs=1))

        offs_sb = keep.tile([P, SLOTS // LIST], U16, name="offs_sb")
        pos_sb = [keep.tile([P, T // LIST], U16, name="pos%d_sb" % r) for r in range(2)]
        tokens = [
            keep.tile([P, T + SPARE * (PACK <= j < 2 * PACK - 1)], F32, name="tokens%d" % j, align_bytes=64) for j in range(PASSES * PACK)
        ]
        gate_first = keep.tile([P, 2 * C], F32, name="gate_first")
        gate_last = keep.tile([P, 2 * C], F32, name="gate_last")
        gate_cols = [keep.tile([P, n], F32, name=name, align_bytes=64) for name, n in (("last0", 2), ("late1", 3))]
        w1_codes = keep.tile([P, E * PASSES, 2 * H], U8, name="w1_codes", align_bytes=64)
        w1_bytes = {
            group: keep.tile([P, group[2] - group[1], H], U8, name="w1_bytes%d_%d" % group[:2], align_bytes=64)
            for group in SCALE_GROUPS
        }
        w2_codes = keep.tile([P, E, 2 * N], U8, name="w2_codes", align_bytes=64)
        w2_bytes = keep.tile([P, E, N], U8, name="w2_bytes", align_bytes=64)
        ident = keep.tile([P, P], F32, name="ident")
        warm = keep.tile([P, 2], F32, name="warm")

        nc.vector.memset(warm[:, 0:1], 0.0)
        nc.scalar.activation(warm[:, 1:2], warm[:, 0:1], GELU)
        make_identity(nc, ident[:])
        for plane in tokens[PACK:-1]:
            nc.vector.memset(plane[:, T:], 0.0)
        for tile in [w1_bytes[group] for group in SCALE_GROUPS]:
            nc.vector.memset(tile[:].rearrange("p e i -> p (e i)").bitcast(I32), 0)
        nc.gpsimd.memset(w2_bytes[:].rearrange("p e n -> p (e n)").bitcast(I32), 0)

        x_rows = xT.rearrange("(s p d) t -> s d p t", s=PASSES, d=PACK)

        def load_plane(s, d):
            j = PACK * s + d
            nc.sync.dma_start(tokens[j][:, 0:T], x_rows[s, d])

        def load_cols(n):
            with nc.allow_non_contiguous_dma(reason="one weight for each partition and expert"):
                rows = gate[0, 4 * n * C : (5 * n + 2) * C]
                nc.sync.dma_start(gate_cols[n][:], rows.rearrange("(e p) -> p e", p=P))

        load_plane(0, 0)
        nc.sync.dma_start(offs_sb[:], offs)
        load_plane(0, 1)
        load_plane(0, 2)
        load_cols(0)
        load_plane(0, 3)
        load_plane(1, 0)
        nc.sync.dma_start(gate_first[:], gate[0:P, 2 * C : 4 * C])
        load_plane(1, 1)
        nc.sync.dma_start(gate_last[:], gate[0:P, 6 * C : SLOTS])
        for d in range(2, PACK):
            load_plane(1, d)
        load_cols(1)

        def load_scales(tile, rows):
            for r in range(4):
                nc.sync.dma_start(tile[r:P:32].bitcast(I32), rows[r:16:4].bitcast(I32))

        def load_w1(passes):
            nc.sync.dma_start(w1_codes[:, passes].bitcast(I32), w1_passes[:, passes].bitcast(I32))

        w1_rows = w1_scales.rearrange("e s q i -> s q e i")
        w1_passes = w1_words.rearrange("e s p b -> p (e s) b")
        for s, e0, e1 in SCALE_GROUPS[:2]:
            load_scales(w1_bytes[s, e0, e1][:], w1_rows[s, :, e0:e1])
        for passes in W1_LOADS[:3]:
            load_w1(passes)
        load_scales(w1_bytes[SCALE_GROUPS[2]][:], w1_rows[1, :, 4:E])
        for passes in W1_LOADS[3:]:
            load_w1(passes)
        load_scales(w2_bytes[:], w2_scales.rearrange("e s q n -> q (e s) n"))
        w2_rows = w2_words.rearrange("e s p b -> p (e s) b")
        for e0, e1 in ((0, 4), (4, E)):
            nc.sync.dma_start(w2_codes[:, e0:e1].bitcast(I32), w2_rows[:, e0:e1].bitcast(I32))

        nc.sync.dma_start(pos_sb[0][:], pos1)
        nc.sync.dma_start(pos_sb[1][:], pos2)

        x_codes = {}
        h_codes = {}
        sums = {}
        h_rows = {}
        h_turned = {}
        h_woven = {}

        def staging(name, experts, tag=None):
            flat = keep.tile([P, PACK * experts * C], F32, name=name, tag=tag or name, align_bytes=64)
            return flat[:].rearrange("p (d c) -> p d c", d=PACK)

        def gather(engine, g, e0, e1, s, d):
            picked_tokens = tokens[PACK * s + d][:].indirect(offs_sb[:, e0 * C // LIST : e1 * C // LIST])
            if engine == "vector":
                nc.vector.tensor_copy(g, picked_tokens)
            else:
                nc.scalar.activation(g, picked_tokens, COPY)

        def weigh_on_gpsimd(xb, g, weights):
            slots = g.shape[2]
            spread = weights.rearrange("p (c o) -> p c o", o=1).broadcast_to([P, slots, PACK])
            nc.gpsimd.tensor_tensor(xb.rearrange("p (c d) -> p c d", d=PACK), g.rearrange("p d c -> p c d"), spread, MULT)

        def weigh_on_vector(xb, g, weights):
            slots = g.shape[2]
            dst = xb.rearrange("p (c i d) -> p c d i", i=4, d=PACK)
            spread = weights.rearrange("p (c o i) -> p c o i", o=1, i=4).broadcast_to([P, slots // 4, PACK, 4])
            nc.vector.tensor_tensor(dst, g.rearrange("p d (c i) -> p c d i", i=4), spread, MULT)

        def quantise_x(xb, units, tag=None):
            name = "%d_%d" % units[0]
            xc = keep.tile([P, len(units) * C], U32, name="codes" + name, tag=tag or "codes" + name, align_bytes=64)
            xs = keep.tile([P, len(units) * C], U8, name="bytes" + name, align_bytes=64)
            for n, unit in enumerate(units):
                x_codes[unit] = (xc[:, n * C : (n + 1) * C], xs[:, n * C : (n + 1) * C])
            nc.vector.quantize_mx(out=xc[:].bitcast(FP8X4), scales=xs[:], in_=xb)

        def first_pass(e0, e1, s):
            for e in range(e0, e1):
                group = [g for g in SCALE_GROUPS if g[0] == s and g[1] <= e < g[2]][0]
                opens = e not in sums
                if opens:
                    sums[e] = psum.tile([P, H], F32, name="sums%d" % e, offset=BANK * SUM_BANKS[e])
                nc.tensor.matmul_mx(
                    out=sums[e][:],
                    lhsT=x_codes[e, s][0].bitcast(FP8X4),
                    lhsT_scale=x_codes[e, s][1],
                    rhs=w1_codes[:, PASSES * e + s, :].bitcast(FP4X4),
                    rhs_scale=w1_bytes[group][:, e - group[1], :],
                    start=opens,
                    stop=not opens,
                )

        def activate(e):
            hb = keep.tile([P, 2, P, 2], BF16, name="h_rows%d" % e, align_bytes=64)[:]
            nc.scalar.activation(hb, sums[e][:].rearrange("c (p u v) -> c u p v", u=2, v=2), GELU)
            h_rows[e] = hb

        def turn(i):
            e0, e1, bank = TURNS[i]
            turned = psum.tile([P, e1 - e0, 2, C], F32, name="turned%d" % i, offset=BANK * bank)
            for e in range(e0, e1):
                words = h_rows[e].rearrange("c u p v -> c (u p v)").bitcast(F32)
                for u in range(2):
                    nc.tensor.transpose(turned[:, e - e0, u, :], words[:, u * P : (u + 1) * P], ident[:])
            h_turned[i] = turned

        def weave(i, copy):
            e0, e1 = TURNS[i][:2]
            hq = keep.tile([P, (e1 - e0) * C * PACK], BF16, name="h_woven%d" % i, align_bytes=64)
            copy(
                hq[:].bitcast(F32).rearrange("p (e c u) -> p e c u", u=2, c=C),
                h_turned[i][:].rearrange("p e u c -> p e c u"),
            )
            h_woven[i] = hq

        def quantise_h(i, tag=None):
            e0, e1 = TURNS[i][:2]
            tag = tag or "h_codes%d" % i
            hc = keep.tile([P, (e1 - e0) * C], U32, name="h_codes%d" % i, tag=tag, align_bytes=64)
            hs = keep.tile([P, (e1 - e0) * C], U8, name="h_bytes%d" % i, align_bytes=64)
            for e in range(e0, e1):
                cols = slice((e - e0) * C, (e - e0 + 1) * C)
                h_codes[e] = (hc[:, cols], hs[:, cols])
            nc.vector.quantize_mx(out=hc[:].bitcast(FP8X4), scales=hs[:], in_=h_woven[i][:])

        def second_product(chunk, e0, e1):
            for e in range(e0, e1):
                first, acc = [(a, tile) for (c, a, b), tile in y_sums.items() if c == chunk and a <= e < b][0]
                nc.tensor.matmul_mx(
                    out=acc[:, (e - first) * C : (e - first + 1) * C],
                    lhsT=w2_codes[:, e, 2 * P * chunk : 2 * P * (chunk + 1)].bitcast(FP4X4),
                    lhsT_scale=w2_bytes[:, e, P * chunk : P * (chunk + 1)],
                    rhs=h_codes[e][0].bitcast(FP8X4),
                    rhs_scale=h_codes[e][1],
                    start=True,
                    stop=True,
                )

        def fill_y(chunk, e0, e1, copy):
            copy(y[chunk][:, e0 * C : e1 * C], y_sums[chunk, e0, e1][:])

        on_scalar, on_vector = nc.scalar.copy, nc.vector.tensor_copy

        gate_banks = []
        for n, bank in enumerate((4, 5)):
            experts = gate_cols[n].shape[1]
            spread = psum.tile([P, experts * C], F32, name="gate_bank%d" % n, offset=BANK * bank)
            for e in range(experts):
                column = gate_cols[n][:, e : e + 1]
                nc.tensor.transpose(spread[:, e * C : (e + 1) * C], column.to_broadcast([P, P]), ident[:])
            gate_banks.append(spread)

        def units(a, b):
            return rounded[:, int(a * UNIT) : int(b * UNIT)]

        def rows_at(flat, at):
            return flat[:, at : at + PAIR].rearrange("p (d c) -> p d c", d=PACK)

        a0, d0, low1 = staging("a0", 2), staging("d0", 2), staging("d1", 4)
        a1, d1 = low1[:, :, 0 : 2 * C], low1[:, :, 2 * C :]
        held = keep.tile([P, 3 * UNIT + 9 * UNIT // 2], F32, name="held", tag="last0", align_bytes=64)
        b0, c0 = [rows_at(held, at) for at in (0, PAIR)]
        rounded = held[:, 3 * UNIT :].bitcast(BF16)
        high1 = staging("high1", 4, tag="late1")
        c1, b1 = high1[:, :, 0 : 2 * C], high1[:, :, 2 * C :]
        for d in range(PACK):
            gather("vector", d0[:, d, :], 2, 4, 0, d)
            gather("scalar", a0[:, d, :], 0, 2, 0, d)
        for d in range(PACK):
            gather("vector", b0[:, d, :], 6, E, 0, d)
        for g, e0 in ((low1, 0), (high1, 4)):
            for d in range(PACK - 1):
                gather("scalar", g[:, d, :], e0, e0 + 4, 1, d)
            for n in (0, 2):
                gather("scalar", g[:, PACK - 1, n * C : (n + 2) * C], e0 + n, e0 + n + 2, 1, PACK - 1)
        weigh_on_gpsimd(units(2, 4), d0, gate_first[:])
        weigh_on_gpsimd(units(5, 7), b0, gate_last[:])
        weigh_on_vector(units(0, 2), a0, gate_banks[0][:])
        for d in range(2):
            gather("vector", c0[:, d, :], 4, 6, 0, d)
        weigh_on_vector(units(7, 9), a1, gate_banks[0][:])
        quantise_x(units(0, 4), [(0, 0), (1, 0), (2, 0), (3, 0)])
        quantise_x(units(5, 9), [(6, 0), (7, 0), (0, 1), (1, 1)])
        weigh_on_gpsimd(units(2, 4), d1, gate_first[:])
        for d in range(2, PACK):
            gather("vector", c0[:, d, :], 4, 6, 0, d)
        weigh_on_vector(units(5, 7), c0, gate_banks[1][:, 0 : 2 * C])
        weigh_on_vector(units(7, 8), c1[:, :, 0:C], gate_banks[1][:, 0:C])
        quantise_x(units(2, 4), [(2, 1), (3, 1)])
        quantise_x(units(5, 8), [(4, 0), (5, 0), (4, 1)], tag="d1")
        weigh_on_gpsimd(units(3.5, 4.5), b1[:, :, C:], gate_last[:, C:])
        weigh_on_vector(units(1.5, 2.5), c1[:, :, C:], gate_banks[1][:, C : 2 * C])
        weigh_on_vector(units(2.5, 3.5), b1[:, :, 0:C], gate_banks[1][:, 2 * C :])
        quantise_x(units(1.5, 2.5), [(5, 1)])
        quantise_x(units(2.5, 4.5), [(6, 1), (7, 1)])
        first_pass(0, 4, 0)
        first_pass(6, E, 0)
        first_pass(0, 4, 1)
        for e in range(4):
            activate(e)
        first_pass(4, 5, 0)
        turn(0)
        weave(0, on_vector)
        first_pass(4, 5, 1)
        first_pass(5, 6, 0)
        first_pass(5, 6, 1)
        activate(4)
        turn(1)
        weave(1, on_vector)
        quantise_h(0, tag="h_rows3")
        quantise_h(1)
        activate(5)
        first_pass(6, E, 1)
        for e in (6, LAST):
            activate(e)
        turn(2)
        weave(2, on_vector)
        for i in (3, 4):
            turn(i)
            weave(i, on_scalar)
        for i in (3, 2, 4):
            quantise_h(i)
        y = [keep.tile([P, SLOTS], F32, name="y%d" % c) for c in range(CHUNKS)]
        y_sums = {
            (chunk, e0, e1): psum.tile([P, (e1 - e0) * C], F32, name="y_sums%d_%d" % (chunk, e0), offset=BANK * bank)
            for chunk, e0, e1, bank in Y_BANKS
        }
        for (chunk, e0, e1, bank), copy in zip(Y_BANKS, (on_scalar, on_vector) * 3 + (on_vector,)):
            second_product(chunk, e0, e1)
            fill_y(chunk, e0, e1, copy)

        picked = [keep.tile([P, T], F32, name="picked%d" % c) for c in range(CHUNKS)]
        summed = [
            keep.tile([P, T], F32, name="summed", tag=tag, align_bytes=64) for tag in ("h_codes4", "summed1", "summed2")
        ]

        def combine(chunk, cuts):
            for a, b in zip(cuts, cuts[1:]):
                lists = [pos[:, a // LIST : b // LIST] for pos in pos_sb]
                nc.scalar.activation(picked[chunk][:, a:b], y[chunk][:].indirect(lists[0]), COPY)
                nc.vector.tensor_tensor(
                    summed[chunk][:, a:b], y[chunk][:].indirect(lists[1]), picked[chunk][:, a:b], ADD
                )
                nc.sync.dma_start(out[chunk * P : (chunk + 1) * P, a:b], summed[chunk][:, a:b])

        half = T // 2
        combine(0, [0, half, T])
        combine(1, [0, half, T])
        combine(2, [0, half, T - T // 8, T])
